import numpy as np
import ml_dtypes


def mxq(x, axis, fmt="e4m3"):
    dtype, down = {"e4m3": (ml_dtypes.float8_e4m3fn, 7), "e5m2": (ml_dtypes.float8_e5m2, 14)}[fmt]
    v = np.moveaxis(np.asarray(x, np.float32).astype(ml_dtypes.bfloat16).astype(np.float64), axis, -1)
    blocks = v.reshape(v.shape[:-1] + (-1, 32))
    amax = np.abs(blocks).max(-1, keepdims=True)
    byte = np.maximum(np.where(amax > 0, np.frexp(amax)[1] - 1 + 127, 0) - down, 1)
    scale = np.exp2(byte - 127.0)
    codes = (blocks / scale).astype(np.float32).astype(dtype).astype(np.float64)
    return np.moveaxis((codes * scale).reshape(v.shape), -1, axis)


WIDE = False


def mx_kscale(k):
    if not WIDE:
        return np.ones(k)
    levels = np.array([10, -10, 5, -5, 0])
    if k % 512:
        return np.exp2(np.random.permutation(np.resize(levels, k // 32))).repeat(32)
    a = np.empty((k // 512, 16))
    for p in range(k // 512):
        a[p, :8] = np.random.permutation(np.resize(levels, 8))
        for g in range(8):
            far = levels[np.abs(levels - a[p, g]) >= 10]
            a[p, g + 8] = far[np.random.randint(len(far))]
    return np.exp2(a.ravel()).repeat(32)


BF16 = ml_dtypes.bfloat16


def bf(x):
    return np.asarray(x, np.float32).astype(BF16)


def f64(x):
    return np.asarray(x).astype(np.float64)


E2M1 = np.array([0.0, 0.5, 1.0, 1.5, 2.0, 3.0, 4.0, 6.0, -0.0, -0.5, -1.0, -1.5, -2.0, -3.0, -4.0, -6.0])


def pack_weight(w, fmt):
    k, n = w.shape
    w = f64(bf(w)).reshape(k // 32, 32, n)
    amax = np.abs(w).max(1)
    if fmt == "e4m3":
        byte = np.frexp(amax)[1] - 1 + 127 - 7
    else:
        mant, ex = np.frexp(amax / 6.0)
        byte = np.where(mant > 0.5, ex, ex - 1) + 127
    byte = np.clip(np.where(amax > 0, byte, 1), 1, 254)
    scaled = (w * np.exp2(127.0 - byte)[:, None, :]).reshape(k, n).astype(np.float32)
    by_word = np.ascontiguousarray(scaled.reshape(k // 512, 128, 4, n).transpose(0, 1, 3, 2))
    if fmt == "e4m3":
        words = by_word.astype(ml_dtypes.float8_e4m3fn).view(np.uint8)
    else:
        c = by_word.astype(ml_dtypes.float4_e2m1fn).view(np.uint8) & 0xF
        words = c[..., 0::2] | (c[..., 1::2] << 4)
    return np.ascontiguousarray(words), np.ascontiguousarray(byte.astype(np.uint8).reshape(k // 512, 16, n))


def unpack_weight(words, scales, fmt):
    g, p, n, _ = words.shape
    if fmt == "e4m3":
        vals = np.ascontiguousarray(words).view(ml_dtypes.float8_e4m3fn).astype(np.float64)
    else:
        nib = np.empty((g, p, n, 4), np.uint8)
        nib[..., 0::2] = words & 0xF
        nib[..., 1::2] = words >> 4
        vals = E2M1[nib]
    vals = vals * np.repeat(np.exp2(scales.astype(np.float64) - 127.0), 8, axis=1)[..., None]
    return vals.transpose(0, 1, 3, 2).reshape(g * 512, n)
def pack4(w):
    words, scales = pack_weight(w, "e2m1")
    return words.reshape(words.shape[0], 128, -1), scales


def unpack4(words, scales):
    return unpack_weight(words.reshape(words.shape[0], 128, -1, 2), scales, "e2m1")


N, D, H, O = 1024, 1024, 1024, 512

BETA = 0.5


def nudged_states(a, f, beta):
    hp = np.tanh(a + beta * f)
    hm = np.tanh(a - beta * f)
    return hp, hm


def draw0():
    s, u, t = mx_kscale(D), mx_kscale(O), mx_kscale(N)
    x = bf(np.random.standard_normal((N, D)))
    p = bf((1.0 + 0.1 * np.random.standard_normal(D)) * s)
    w1_words, w1_scales = pack4(np.random.standard_normal((D, H)) / np.sqrt(D) / s[:, None])
    e = bf(np.random.standard_normal((N, O)) * u[None, :])
    w2_words, w2_scales = pack4((np.random.standard_normal((H, O)) / np.sqrt(O) / u[None, :]).T)
    return {"x": x,
            "p": p,
            "w1_words": w1_words,
            "w1_scales": w1_scales,
            "e": e,
            "w2_words": w2_words,
            "w2_scales": w2_scales,
            "r": bf((1.0 + 0.1 * np.random.standard_normal(N)) * t),
            "g": bf((1.0 + 0.1 * np.random.standard_normal(N)) / t)}


def core(x, p, w1_words, w1_scales, e, w2_words, w2_scales, r, g):
    x, p, e, r, g = f64(x), f64(p), f64(e), f64(r), f64(g)
    n = x.shape[0]
    a = mxq(x * p[None, :], 1, "e4m3") @ unpack4(w1_words, w1_scales)
    f = mxq(e, 1, "e4m3") @ unpack4(w2_words, w2_scales)
    hp, hm = nudged_states(a, f, BETA)
    d = (hp - hm) * g[:, None] / (2.0 * BETA * np.sqrt(n))
    xr = x * r[:, None]
    return mxq(xr, 0, "e4m3").T @ mxq(d, 0, "e4m3")


def e4m3fn_bytes(y):
    return np.clip(np.asarray(y, np.float64), -448.0, 448.0).astype(np.float32).astype(ml_dtypes.float8_e4m3fn).view(np.uint8)


def e4m3fn_values(b):
    return np.asarray(b, np.uint8).view(ml_dtypes.float8_e4m3fn).astype(np.float64)


def setup_inputs():
    d = draw0()
    x0 = np.asarray(d['e']).astype(np.float64)
    s = (np.max(np.abs(x0), axis=(0,), keepdims=True) / 448.0).astype(np.float32)
    out = {}
    for k, v in d.items():
        if k == 'e':
            out['e_bytes'] = e4m3fn_bytes(x0 / s.astype(np.float64))
            out['e_scale'] = s
        else:
            out[k] = v
    return out


def reference(x, p, w1_words, w1_scales, e_bytes, e_scale, w2_words, w2_scales, r, g):
    return core(x, p, w1_words, w1_scales, e4m3fn_values(e_bytes) * e_scale.astype(np.float64), w2_words, w2_scales, r, g)

@@ -1,0 +1,690 @@
+from contextlib import ExitStack
+
+import concourse.mybir as mybir
+from concourse.masks import make_identity
+
+F32 = mybir.dt.float32
+BF16 = mybir.dt.bfloat16
+U32 = mybir.dt.uint32
+I32 = mybir.dt.int32
+U8 = mybir.dt.uint8
+E4M3 = mybir.dt.float8_e4m3fn
+FP8X4 = mybir.dt.float8_e4m3fn_x4
+FP4X4 = mybir.dt.float4_e2m1fn_x4
+MULT = mybir.AluOpType.mult
+SUB = mybir.AluOpType.subtract
+TANH = mybir.ActivationFunctionType.Tanh
+COPY = mybir.ActivationFunctionType.Copy
+
+P = 128
+N, D, H, O = 1024, 1024, 1024, 512
+FLOPS = 2 * N * D * H + 2 * N * O * H + 2 * N * D * H
+G = 2
+T = 4
+W = 512
+N_WARM = 5
+CHUNKS = ((0, 512), (512, 256), (768, 256))
+
+
+def tile_centredequilibriumpropupdate_w4_kernel(
+    tc, x, p, w1_words, w1_scales, e_bytes, e_scale, w2_words, w2_scales, r, g, out
+):
+    nc = tc.nc
+    with ExitStack() as ctx:
+        keep = ctx.enter_context(tc.tile_pool(name="keep", bufs=1))
+        work = ctx.enter_context(tc.tile_pool(name="work", bufs=3))
+        psum = ctx.enter_context(tc.psum_pool(name="psum", bufs=4))
+        ctx.enter_context(tc.manual_schedule())
+
+        xt = [keep.tile([P, T, D], BF16, name="xt%d" % i, align_bytes=64) for i in range(G)]
+        eb = keep.tile([P, G, T, O], U8, name="eb", align_bytes=64)
+        prow = keep.tile([P, D], BF16, name="prow", align_bytes=64)
+        est = keep.tile([P, 4], F32, name="est", align_bytes=64)
+        zero = keep.tile([P, 512], BF16, name="zero", align_bytes=64)
+        ones_bf = keep.tile([P, P], BF16, name="ones_bf", align_bytes=64)
+        pbp = keep.tile([P, D], BF16, name="pbp", align_bytes=64)
+        w1t = keep.tile([P, 2, 2 * H], U8, name="w1t", align_bytes=64)
+        w2t = keep.tile([P, 2 * H], U8, name="w2t", align_bytes=64)
+        wsc = keep.tile([P, 3, H], U8, name="wsc", align_bytes=64)
+        rb = keep.tile([P, G, T], BF16, name="rb", align_bytes=64)
+        gb = keep.tile([P, G, T], BF16, name="gb", align_bytes=64)
+        rf = keep.tile([P, G, T], F32, name="rf", align_bytes=64)
+        gs = keep.tile([P, G, T], F32, name="gs", align_bytes=64)
+        ident = keep.tile([P, P], F32, name="ident", align_bytes=64)
+        warm = keep.tile([P, 2], F32, name="warm", align_bytes=64)
+        xc = keep.tile([P, 8, 2, P], U32, name="xc", align_bytes=64)
+        xs = keep.tile([P, 8, 2, P], U8, name="xs", align_bytes=64)
+        ec = keep.tile([P, 8, 2, P], U32, name="ec", align_bytes=64)
+        es = keep.tile([P, 8, 2, P], U8, name="es", align_bytes=64)
+        rc = keep.tile([P, G, D], U32, name="rc", align_bytes=64)
+        rs = keep.tile([P, G, D], U8, name="rs", align_bytes=64)
+        dc = [keep.tile([P, G, w], U32, name="dc%d" % c, align_bytes=64) for c, (lo, w) in enumerate(CHUNKS)]
+        dsc = [keep.tile([P, G, w], U8, name="dsc%d" % c, align_bytes=64) for c, (lo, w) in enumerate(CHUNKS)]
+        hpm = {
+            (i, c, s): keep.tile([P, T, W], F32, name="h%d%d%d" % (i, c, s), align_bytes=64)
+            for i in range(G)
+            for c in range(2)
+            for s in range(2)
+        }
+
+        xv = x.rearrange("(g p t) d -> g p t d", g=G, p=P, t=T)
+        ev = e_bytes.rearrange("(g p t) o -> g p t o", g=G, p=P, t=T)
+        w1v = w1_words.rearrange("g p w -> p g w")
+
+        def load_w(lo, hi):
+            nc.sync.dma_start(out=w1t[:, :, 2 * lo : 2 * hi], in_=w1v[:, :, 2 * lo : 2 * hi])
+            nc.sync.dma_start(out=w2t[:, 2 * lo : 2 * hi], in_=w2_words[0, :, 2 * lo : 2 * hi])
+
+
+        nc.vector.memset(prow[:].bitcast(I32), 0)
+        nc.vector.memset(zero[:].bitcast(I32), 0)
+        nc.vector.memset(ones_bf[:], 1.0)
+        nc.vector.memset(warm[:], 0.0)
+        nc.vector.memset(wsc[:].rearrange("p k n -> p (k n)").bitcast(I32), 0)
+        nc.scalar.activation(out=warm[:, 1:2], in_=warm[:, 0:1], func=TANH)
+
+        def load_x(i, t0, t1):
+            nc.gpsimd.dma_start(out=xt[i][:, t0:t1, :], in_=xv[i, :, t0:t1, :])
+
+        def load_e(i):
+            nc.sync.dma_start(out=eb[:, i, :, :], in_=ev[i])
+
+        def load_r():
+            nc.gpsimd.dma_start(out=rb[:], in_=r.rearrange("(g p t) -> p g t", g=G, p=P, t=T))
+
+        def load_g():
+            nc.gpsimd.dma_start(out=gb[:], in_=g.rearrange("(g p t) -> p g t", g=G, p=P, t=T))
+
+        def load_scales1():
+            for q in range(4):
+                nc.sync.dma_start(
+                    out=wsc[32 * q : 32 * q + 4, 0:2, :].bitcast(I32),
+                    in_=w1_scales[:, 4 * q : 4 * q + 4, :].rearrange("g q n -> q g n").bitcast(I32),
+                )
+        def load_scales2():
+            for q in range(4):
+                nc.sync.dma_start(
+                    out=wsc[32 * q : 32 * q + 4, 2, :].bitcast(I32), in_=w2_scales[0, 4 * q : 4 * q + 4, :].bitcast(I32)
+                )
+
+        def load_prow():
+            nc.sync.dma_start(out=prow[0:1, :], in_=p.rearrange("(o d) -> o d", o=1))
+
+        def load_est():
+            nc.sync.dma_start(out=est[:], in_=e_scale.rearrange("o (q t) -> q (o t)", t=4))
+
+        def make_ident():
+            make_identity(nc, ident[:])
+
+        load_x(0, 0, 1)
+        make_ident()
+        load_x(0, 1, 2)
+        load_x(0, 2, 4)
+        load_r()
+        load_g()
+        load_x(1, 0, 2)
+        load_x(1, 2, 4)
+        load_prow()
+        load_est()
+        load_e(0)
+        load_scales1()
+        load_w(0, W)
+        load_scales2()
+        load_e(1)
+        load_w(W, H)
+        wbank = psum.tile([P, 512], F32, name="u")
+        for j in range(N_WARM):
+            nc.tensor.matmul(wbank[:], lhsT=ones_bf[:], rhs=zero[:], start=True, stop=True)
+        xpw = {}
+        pbk = {}
+        eww = {}
+        xg = {}
+        eg = {}
+        xb = {}
+        ebk = {}
+
+        def ones_p():
+            pbk[0] = psum.tile([P, D], BF16, name="m")
+            for j in range(2):
+                nc.tensor.matmul(
+                    pbk[0][:, 512 * j : 512 * (j + 1)],
+                    lhsT=ones_bf[:],
+                    rhs=prow[:, 512 * j : 512 * (j + 1)],
+                    start=True,
+                    stop=True,
+                )
+
+        def pb_copy():
+            nc.scalar.copy(
+                out=pbp[:].rearrange("p (u q e) -> p u q e", u=2, e=2),
+                in_=pbk[0][:].rearrange("p (q u e) -> p u q e", u=2, e=2),
+            )
+
+        def est_half():
+            nc.vector.tensor_scalar(out=est[:], in0=est[:], scalar1=0.5, scalar2=None, op0=MULT)
+
+        def gs_prep():
+            nc.scalar.activation(
+                out=gs[:].rearrange("p g t -> p (g t)"),
+                in_=gb[:].rearrange("p g t -> p (g t)"),
+                func=COPY,
+                scale=1.0 / 32.0,
+            )
+
+        def x_mul(b):
+            xp = work.tile([P, D], BF16, name="xp", align_bytes=64)
+            nc.vector.tensor_tensor(
+                out=xp[:].rearrange("p (u q e) -> p u q e", u=2, e=2),
+                in0=xt[b // T][:, b % T, :].rearrange("p (q u e) -> p u q e", u=2, e=2),
+                in1=pbp[:].rearrange("p (u q e) -> p u q e", u=2, e=2),
+                op=MULT,
+            )
+            xpw[b] = xp
+
+        def x_mul_psum(b):
+            xp = work.tile([P, D], BF16, name="xp", align_bytes=64)
+            nc.vector.tensor_tensor(
+                out=xp[:].rearrange("p (u q e) -> p u q e", u=2, e=2),
+                in0=xt[b // T][:, b % T, :].rearrange("p (q u e) -> p u q e", u=2, e=2),
+                in1=pbk[0][:].rearrange("p (q u e) -> p u q e", u=2, e=2),
+                op=MULT,
+            )
+            xpw[b] = xp
+
+        def e_widen(b, n, eng):
+            ew = work.tile([P, n, O], BF16, name="ew%d" % n, bufs=2, align_bytes=64)
+            src = eb[:, b // T, b % T : b % T + n, :].bitcast(E4M3)
+            if eng == "V":
+                nc.vector.tensor_copy(out=ew[:], in_=src)
+            else:
+                nc.scalar.copy(out=ew[:], in_=src)
+            for j in range(n):
+                eww[b + j] = ew[:, j, :]
+
+        def e_mul(b, j):
+            if b % 2 == 0:
+                eg[b // 2] = work.tile([P, 2, 2, P, 4], BF16, name="eg", bufs=2, align_bytes=64)
+            src = ebk[b - j][:, j].bitcast(BF16)
+            nc.vector.tensor_tensor(
+                out=eg[b // 2][:, b % 2, 0].rearrange("p n (u e) -> p n u e", u=2),
+                in0=src.rearrange("p u (n e) -> p n u e", e=2),
+                in1=est[:].unsqueeze(1).to_broadcast([P, P, 4]).rearrange("p n (u e) -> p n u e", u=2),
+                op=MULT,
+            )
+
+        def x_turn(b):
+            xb[b] = psum.tile([P, 2, 2, P], F32, name="m")
+            words = xpw[b][:].bitcast(F32)
+            for k in range(2):
+                for u in range(2):
+                    nc.tensor.transpose(xb[b][:, k, u, :], words[:, 256 * u + 128 * k : 256 * u + 128 * (k + 1)], ident[:])
+
+        def x_copy(b):
+            if b % 2 == 0:
+                xg[b // 2] = work.tile([P, 2, 2, P, 4], BF16, name="xg", bufs=2, align_bytes=64)
+            grouped = xg[b // 2][:, b % 2].rearrange("p k n j -> p k (n j)").bitcast(F32)
+            nc.scalar.copy(
+                out=grouped.rearrange("p k (n u) -> p k n u", u=2), in_=xb[b][:].rearrange("p k u n -> p k n u")
+            )
+
+        def e_turn(b, n):
+            ebk[b] = psum.tile([P, n, 2, P], F32, name="m")
+            for j in range(n):
+                words = eww[b + j].bitcast(F32)
+                for u in range(2):
+                    nc.tensor.transpose(ebk[b][:, j, u, :], words[:, u:256:2], ident[:])
+
+        def x_quant(q):
+            nc.vector.quantize_mx(
+                out=xc[:, 2 * q : 2 * q + 2].rearrange("p b k n -> p (b k n)").bitcast(FP8X4),
+                scales=xs[:, 2 * q : 2 * q + 2].rearrange("p b k n -> p (b k n)"),
+                in_=xg[q][:].rearrange("p b k n j -> p (b k n j)"),
+            )
+
+        def x_quant1(b):
+            nc.vector.quantize_mx(
+                out=xc[:, b].rearrange("p k n -> p (k n)").bitcast(FP8X4),
+                scales=xs[:, b].rearrange("p k n -> p (k n)"),
+                in_=xg[b // 2][:, b % 2].rearrange("p k n j -> p (k n j)"),
+            )
+
+        def e_neg(b, n):
+            h = b % 2
+            flat = eg[b // 2][:, h : h + n].rearrange("p b s n j -> p b s (n j)")
+            nc.vector.tensor_scalar(out=flat[:, :, 1], in0=flat[:, :, 0], scalar1=-1.0, scalar2=None, op0=MULT)
+
+        def e_quant(b, n):
+            h = b % 2
+            nc.vector.quantize_mx(
+                out=ec[:, b : b + n].rearrange("p b s n -> p (b s n)").bitcast(FP8X4),
+                scales=es[:, b : b + n].rearrange("p b s n -> p (b s n)"),
+                in_=eg[b // 2][:, h : h + n].rearrange("p b s n j -> p (b s n j)"),
+            )
+
+        ub = {}
+
+        def s1(b, c, s):
+            lo, hi = c * W, (c + 1) * W
+            ub[b, c, s] = psum.tile([P, W], F32, name="u")
+            for k in range(2):
+                nc.tensor.matmul_mx(
+                    out=ub[b, c, s][:],
+                    lhsT=xc[:, b, k, :].bitcast(FP8X4),
+                    lhsT_scale=xs[:, b, k, :],
+                    rhs=w1t[:, k, 2 * lo : 2 * hi].bitcast(FP4X4),
+                    rhs_scale=wsc[:, k, lo:hi],
+                    start=(k == 0),
+                    stop=False,
+                )
+            nc.tensor.matmul_mx(
+                out=ub[b, c, s][:],
+                lhsT=ec[:, b, s, :].bitcast(FP8X4),
+                lhsT_scale=es[:, b, s, :],
+                rhs=w2t[:, 2 * lo : 2 * hi].bitcast(FP4X4),
+                rhs_scale=wsc[:, 2, lo:hi],
+                start=False,
+                stop=True,
+            )
+
+        def tanh(b, c, s):
+            nc.scalar.activation(out=hpm[b // T, c, s][:, b % T, :], in_=ub[b, c, s][:], func=TANH)
+
+        db = {}
+        dg = {}
+
+        def diff(i, c, t0, t1):
+            nc.vector.tensor_tensor(
+                out=hpm[i, c, 0][:, t0:t1, :], in0=hpm[i, c, 0][:, t0:t1, :], in1=hpm[i, c, 1][:, t0:t1, :], op=SUB
+            )
+
+        def new_db(i, c):
+            if (i, c) not in db:
+                db[i, c] = work.tile([P, T, W], BF16, name="db", bufs=3, align_bytes=64)
+
+        def scale_s(i, c, t):
+            new_db(i, c)
+            nc.scalar.activation(out=db[i, c][:, t, :], in_=hpm[i, c, 0][:, t, :], func=COPY, scale=gs[:, i, t : t + 1])
+
+        def scale_v(i, c, t):
+            new_db(i, c)
+            nc.vector.tensor_scalar(
+                out=db[i, c][:, t, :], in0=hpm[i, c, 0][:, t, :], scalar1=gs[:, i, t : t + 1], scalar2=None, op0=MULT
+            )
+
+        def weave_d(i, c, lo, hi):
+            if lo == 0:
+                dg[i, c] = work.tile([P, W, T], BF16, name="dg", bufs=3, align_bytes=64)
+            nc.vector.tensor_copy(
+                out=dg[i, c][:, lo:hi, :].rearrange("p (n j) t -> p n t j", j=4),
+                in_=db[i, c][:, :, lo:hi].rearrange("p t (n j) -> p n t j", j=4),
+            )
+
+        def quant_d(i, c):
+            lo, w = CHUNKS[c]
+            nc.vector.quantize_mx(
+                out=dc[c][:, i, :].bitcast(FP8X4),
+                scales=dsc[c][:, i, :],
+                in_=dg[i, lo // W][:, lo % W : lo % W + w, :].rearrange("p n t -> p (n t)"),
+            )
+
+        xm = {}
+        xw = {}
+
+        def new_xw(i):
+            if i not in xw:
+                xw[i] = work.tile([P, D, T], BF16, name="xw", bufs=2, align_bytes=64)
+
+        def r_mul(i, t):
+            if i not in xm:
+                xm[i] = work.tile([P, T, D], BF16, name="xm", bufs=1, align_bytes=64)
+            nc.vector.tensor_scalar(
+                out=xm[i][:, t, :], in0=xt[i][:, t, :], scalar1=rb[:, i, t : t + 1], scalar2=None, op0=MULT
+            )
+
+        def r_prep():
+            nc.scalar.activation(
+                out=rf[:].rearrange("p g t -> p (g t)"), in_=rb[:].rearrange("p g t -> p (g t)"), func=COPY
+            )
+
+        def r_mul_s(i, t):
+            if i not in xm:
+                xm[i] = work.tile([P, T, D], BF16, name="xm", bufs=1, align_bytes=64)
+            nc.scalar.activation(out=xm[i][:, t, :], in_=xt[i][:, t, :], func=COPY, scale=rf[:, i, t : t + 1])
+
+        def r_weave(i, q):
+            new_xw(i)
+            w = D // 4
+            nc.vector.tensor_copy(
+                out=xw[i][:, q * w : (q + 1) * w, :].rearrange("p (n j) t -> p n t j", j=4),
+                in_=xm[i][:, :, q * w : (q + 1) * w].rearrange("p t (n j) -> p n t j", j=4),
+            )
+
+        def r_quant(i, lo, hi):
+            nc.vector.quantize_mx(
+                out=rc[:, i, lo:hi].bitcast(FP8X4), scales=rs[:, i, lo:hi], in_=xw[i][:, lo:hi, :].rearrange("p n t -> p (n t)")
+            )
+
+        ob = {}
+        rest = {}
+
+        def s2_last(c, f, i, tag):
+            lo, w = CHUNKS[c]
+            if i == 0:
+                ob[c, f] = psum.tile([P, w], F32, name=tag)
+            nc.tensor.matmul_mx(
+                out=ob[c, f][:],
+                lhsT=rc[:, i, f * P : (f + 1) * P].bitcast(FP8X4),
+                lhsT_scale=rs[:, i, f * P : (f + 1) * P],
+                rhs=dc[c][:, i, :].bitcast(FP8X4),
+                rhs_scale=dsc[c][:, i, :],
+                start=(i == 0),
+                stop=(i == G - 1),
+            )
+
+        def copy_last(c, f, eng):
+            lo, w = CHUNKS[c]
+            if f % 2 == 0:
+                rest[c, f] = work.tile([P, 2, w], F32, name="resl", bufs=4, align_bytes=64)
+            dst = rest[c, f - f % 2][:, f % 2, :]
+            if eng == "V":
+                nc.vector.tensor_copy(out=dst, in_=ob[c, f][:])
+            else:
+                nc.scalar.copy(out=dst, in_=ob[c, f][:])
+
+        def s2(c, f, i, tag):
+            lo, w = CHUNKS[c]
+            nt = 512 // w
+            if i == 0 and f % nt == 0:
+                ob[c, f] = psum.tile([P, nt, w], F32, name=tag)
+            nc.tensor.matmul_mx(
+                out=ob[c, f - f % nt][:, f % nt, :],
+                lhsT=rc[:, i, f * P : (f + 1) * P].bitcast(FP8X4),
+                lhsT_scale=rs[:, i, f * P : (f + 1) * P],
+                rhs=dc[c][:, i, :].bitcast(FP8X4),
+                rhs_scale=dsc[c][:, i, :],
+                start=(i == 0),
+                stop=(i == G - 1),
+            )
+
+        def out_copy(c, f, eng):
+            lo, w = CHUNKS[c]
+            rest[c, f] = work.tile([P, 512 // w, w], F32, name="res", bufs=6, align_bytes=64)
+            if eng == "V":
+                nc.vector.tensor_copy(out=rest[c, f][:], in_=ob[c, f][:])
+            else:
+                nc.scalar.copy(out=rest[c, f][:], in_=ob[c, f][:])
+
+        def store(c, f):
+            lo, w = CHUNKS[c]
+            nt = 512 // w
+            nc.sync.dma_start(
+                out=out[f * P : (f + nt) * P, lo : lo + w].rearrange("(j p) n -> p j n", p=P), in_=rest[c, f][:]
+            )
+
+
+        est_half()
+        ones_p()
+        e_widen(1, 1, "S")
+        x_mul_psum(0)
+        e_widen(2, 2, "S")
+        e_widen(0, 1, "V")
+        x_mul_psum(1)
+        e_turn(0, 1)
+        e_mul(0, 0)
+        pb_copy()
+        e_turn(1, 1)
+        x_turn(0)
+        x_turn(1)
+        e_mul(1, 0)
+        x_copy(0)
+        x_mul(2)
+        x_copy(1)
+        e_turn(2, 2)
+        e_neg(0, 1)
+        x_turn(2)
+        x_mul(3)
+        x_quant1(0)
+        x_turn(3)
+        r_prep()
+        r_mul_s(0, 0)
+        e_quant(0, 1)
+        x_quant1(1)
+        e_widen(6, 2, "S")
+        e_neg(1, 1)
+        e_mul(2, 0)
+        r_mul(0, 2)
+        s1(0, 0, 1)
+        e_mul(3, 1)
+        s1(0, 0, 0)
+        e_quant(1, 1)
+        s1(1, 0, 1)
+        x_mul(4)
+        e_neg(2, 2)
+        e_widen(4, 2, "S")
+        x_copy(2)
+        x_mul(5)
+        x_copy(3)
+        s1(1, 0, 0)
+        x_turn(4)
+        r_mul(0, 3)
+        x_mul(6)
+        x_quant(1)
+        tanh(0, 0, 0)
+        x_copy(4)
+        e_turn(6, 2)
+        tanh(1, 0, 0)
+        x_turn(6)
+        x_mul(7)
+        e_turn(4, 2)
+        x_turn(5)
+        e_quant(2, 2)
+        s1(2, 1, 0)
+        x_copy(6)
+        s1(2, 0, 0)
+        e_mul(4, 0)
+        x_turn(7)
+        e_mul(6, 0)
+        e_mul(5, 1)
+        e_mul(7, 1)
+        gs_prep()
+        tanh(0, 0, 1)
+        e_neg(4, 2)
+        tanh(1, 0, 1)
+        diff(0, 0, 0, 2)
+        x_copy(5)
+        x_quant(2)
+        tanh(2, 0, 0)
+        tanh(2, 1, 0)
+        r_mul_s(0, 1)
+        s1(3, 0, 0)
+        s1(3, 0, 1)
+        tanh(3, 0, 0)
+        tanh(3, 0, 1)
+        e_quant(4, 2)
+        s1(2, 0, 1)
+        r_weave(0, 0)
+        r_weave(0, 2)
+        x_copy(7)
+        e_neg(6, 2)
+        tanh(2, 0, 1)
+        scale_s(0, 0, 0)
+        s1(5, 0, 0)
+        tanh(5, 0, 0)
+        s1(3, 1, 0)
+        r_weave(0, 1)
+        r_weave(0, 3)
+        x_quant(3)
+        s1(4, 0, 0)
+        e_quant(6, 2)
+        diff(0, 0, 2, 4)
+        tanh(4, 0, 0)
+        r_mul(1, 0)
+        r_mul(1, 1)
+        tanh(3, 1, 0)
+        s1(0, 1, 1)
+        tanh(0, 1, 1)
+        r_quant(0, 0, 1024)
+        r_mul(1, 3)
+        s1(4, 0, 1)
+        scale_s(0, 0, 1)
+        s1(5, 0, 1)
+        tanh(4, 0, 1)
+        s1(6, 0, 1)
+        scale_s(0, 0, 2)
+        tanh(5, 0, 1)
+        r_mul(1, 2)
+        s1(6, 0, 0)
+        s1(0, 1, 0)
+        tanh(6, 0, 1)
+        scale_s(0, 0, 3)
+        tanh(6, 0, 0)
+        tanh(0, 1, 0)
+        s1(7, 0, 0)
+        diff(1, 0, 0, 2)
+        scale_s(1, 0, 0)
+        tanh(7, 0, 0)
+        r_weave(1, 0)
+        s1(7, 0, 1)
+        tanh(7, 0, 1)
+        weave_d(0, 0, 0, 256)
+        s1(1, 1, 0)
+        tanh(1, 1, 0)
+        weave_d(0, 0, 256, 512)
+        r_weave(1, 2)
+        scale_s(1, 0, 1)
+        r_weave(1, 1)
+        s1(1, 1, 1)
+        tanh(1, 1, 1)
+        s1(3, 1, 1)
+        tanh(3, 1, 1)
+        s1(5, 1, 1)
+        diff(1, 0, 2, 4)
+        scale_s(1, 0, 2)
+        scale_s(1, 0, 3)
+        quant_d(0, 0)
+        s1(2, 1, 1)
+        tanh(5, 1, 1)
+        diff(0, 1, 0, 2)
+        s1(4, 1, 0)
+        r_weave(1, 3)
+        tanh(2, 1, 1)
+        s1(5, 1, 0)
+        weave_d(1, 0, 0, 256)
+        r_quant(1, 0, 1024)
+        tanh(4, 1, 0)
+        diff(0, 1, 2, 4)
+        scale_s(0, 1, 0)
+        s1(4, 1, 1)
+        weave_d(1, 0, 256, 512)
+        tanh(5, 1, 0)
+        tanh(4, 1, 1)
+        diff(1, 1, 0, 2)
+        scale_s(0, 1, 1)
+        scale_s(0, 1, 3)
+        s1(7, 1, 0)
+        s1(7, 1, 1)
+        scale_s(0, 1, 2)
+        tanh(7, 1, 1)
+        s1(6, 1, 1)
+        s1(6, 1, 0)
+        tanh(7, 1, 0)
+        s2(0, 5, 0, "m")
+        quant_d(1, 0)
+        tanh(6, 1, 0)
+        s2(0, 5, 1, "m")
+        s2(0, 1, 0, "m")
+        s2(0, 1, 1, "m")
+        weave_d(0, 1, 0, 256)
+        weave_d(0, 1, 256, 512)
+        scale_v(1, 1, 0)
+        s2(0, 2, 0, "m")
+        s2(0, 2, 1, "m")
+        quant_d(0, 2)
+        tanh(6, 1, 1)
+        diff(1, 1, 2, 4)
+        s2(0, 7, 0, "m")
+        s2(0, 7, 1, "m")
+        s2(0, 0, 0, "m")
+        s2(0, 0, 1, "m")
+        out_copy(0, 5, "S")
+        store(0, 5)
+        out_copy(0, 2, "S")
+        store(0, 2)
+        out_copy(0, 1, "S")
+        out_copy(0, 7, "S")
+        s2(0, 3, 0, "m")
+        s2(0, 3, 1, "m")
+        out_copy(0, 3, "S")
+        scale_v(1, 1, 1)
+        s2_last(2, 5, 0, "u")
+        scale_v(1, 1, 3)
+        scale_v(1, 1, 2)
+        weave_d(1, 1, 0, 256)
+        out_copy(0, 0, "S")
+        s2(0, 6, 0, "m")
+        quant_d(0, 1)
+        s2(0, 4, 0, "m")
+        store(0, 1)
+        store(0, 7)
+        s2(0, 6, 1, "m")
+        out_copy(0, 6, "S")
+        s2(0, 4, 1, "m")
+        out_copy(0, 4, "S")
+        s2(1, 0, 0, "m")
+        quant_d(1, 1)
+        s2_last(2, 1, 0, "u")
+        s2(1, 4, 0, "m")
+        weave_d(1, 1, 256, 512)
+        store(0, 3)
+        quant_d(1, 2)
+        s2(1, 0, 1, "m")
+        s2(1, 1, 0, "m")
+        s2(1, 1, 1, "m")
+        out_copy(1, 0, "S")
+        s2(1, 4, 1, "m")
+        s2(1, 5, 0, "m")
+        s2(1, 5, 1, "m")
+        s2_last(2, 0, 0, "m")
+        s2_last(2, 0, 1, "m")
+        copy_last(2, 0, "S")
+        store(0, 0)
+        s2_last(2, 1, 1, "u")
+        s2_last(2, 5, 1, "u")
+        s2_last(2, 2, 0, "m")
+        s2_last(2, 2, 1, "m")
+        s2_last(2, 3, 0, "u")
+        s2_last(2, 6, 0, "m")
+        s2_last(2, 3, 1, "u")
+        out_copy(1, 4, "S")
+        copy_last(2, 2, "S")
+        s2_last(2, 4, 0, "m")
+        s2_last(2, 4, 1, "m")
+        s2_last(2, 7, 0, "u")
+        store(0, 6)
+        copy_last(2, 1, "V")
+        store(0, 4)
+        store(1, 0)
+        s2_last(2, 6, 1, "m")
+        store(2, 0)
+        copy_last(2, 3, "V")
+        s2_last(2, 7, 1, "u")
+        s2(1, 6, 0, "m")
+        s2(1, 6, 1, "m")
+        store(1, 4)
+        store(2, 2)
+        copy_last(2, 4, "S")
+        copy_last(2, 5, "V")
+        copy_last(2, 6, "S")
+        copy_last(2, 7, "V")
+        store(2, 6)
+        store(2, 4)
+        s2(1, 7, 0, "m")
+        s2(1, 7, 1, "m")
+        out_copy(1, 6, "S")
+        store(1, 6)
+        s2(1, 2, 0, "m")
+        s2(1, 2, 1, "m")
+        s2(1, 3, 0, "m")
+        s2(1, 3, 1, "m")
+        out_copy(1, 2, "S")
+        store(1, 2)

@@ -22,8 +22,8 @@ FLOPS = 2 * N * D * H + 2 * N * O * H + 2 * N * D * H
 G = 2
 T = 4
 W = 512
-N_WARM = 5
-CHUNKS = ((0, 512), (512, 256), (768, 256))
+HALF = 256
+GROUPS = ((0, 1), (1, 1), (2, 2), (4, 2), (6, 2))
 
 
 def tile_centredequilibriumpropupdate_w4_kernel(
@@ -33,658 +33,368 @@ def tile_centredequilibriumpropupdate_w4_kernel(
     with ExitStack() as ctx:
         keep = ctx.enter_context(tc.tile_pool(name="keep", bufs=1))
         work = ctx.enter_context(tc.tile_pool(name="work", bufs=3))
-        psum = ctx.enter_context(tc.psum_pool(name="psum", bufs=4))
+        psum = ctx.enter_context(tc.psum_pool(name="psum", bufs=1))
         ctx.enter_context(tc.manual_schedule())
 
-        xt = [keep.tile([P, T, D], BF16, name="xt%d" % i, align_bytes=64) for i in range(G)]
-        eb = keep.tile([P, G, T, O], U8, name="eb", align_bytes=64)
-        prow = keep.tile([P, D], BF16, name="prow", align_bytes=64)
-        est = keep.tile([P, 4], F32, name="est", align_bytes=64)
-        zero = keep.tile([P, 512], BF16, name="zero", align_bytes=64)
-        ones_bf = keep.tile([P, P], BF16, name="ones_bf", align_bytes=64)
-        pbp = keep.tile([P, D], BF16, name="pbp", align_bytes=64)
-        w1t = keep.tile([P, 2, 2 * H], U8, name="w1t", align_bytes=64)
+        def bank(i):
+            return psum.tile([P, W], F32, name="bank%d" % i)
+
+        xt = {b0: keep.tile([P, n, D], BF16, name="xt%d" % b0, align_bytes=64) for b0, n in GROUPS}
+        xrow = {b0 + j: xt[b0][:, j, :] for b0, n in GROUPS for j in range(n)}
+        eb = [keep.tile([P, T, O], U8, name="eb%d" % i, align_bytes=64) for i in range(G)]
+        est = keep.tile([P, T], F32, name="est", align_bytes=64)
+        esp = keep.tile([P, O], F32, name="esp", align_bytes=64)
+        pt = keep.tile([P, 2, T], BF16, name="pt", align_bytes=64)
+        pfull = keep.tile([P, 2, P, T], BF16, name="pfull", align_bytes=64)
+        w1t = [keep.tile([P, 2, 2 * W], U8, name="w1t%d" % c, align_bytes=64) for c in range(2)]
         w2t = keep.tile([P, 2 * H], U8, name="w2t", align_bytes=64)
         wsc = keep.tile([P, 3, H], U8, name="wsc", align_bytes=64)
         rb = keep.tile([P, G, T], BF16, name="rb", align_bytes=64)
         gb = keep.tile([P, G, T], BF16, name="gb", align_bytes=64)
-        rf = keep.tile([P, G, T], F32, name="rf", align_bytes=64)
         gs = keep.tile([P, G, T], F32, name="gs", align_bytes=64)
         ident = keep.tile([P, P], F32, name="ident", align_bytes=64)
         warm = keep.tile([P, 2], F32, name="warm", align_bytes=64)
-        xc = keep.tile([P, 8, 2, P], U32, name="xc", align_bytes=64)
-        xs = keep.tile([P, 8, 2, P], U8, name="xs", align_bytes=64)
-        ec = keep.tile([P, 8, 2, P], U32, name="ec", align_bytes=64)
-        es = keep.tile([P, 8, 2, P], U8, name="es", align_bytes=64)
-        rc = keep.tile([P, G, D], U32, name="rc", align_bytes=64)
-        rs = keep.tile([P, G, D], U8, name="rs", align_bytes=64)
-        dc = [keep.tile([P, G, w], U32, name="dc%d" % c, align_bytes=64) for c, (lo, w) in enumerate(CHUNKS)]
-        dsc = [keep.tile([P, G, w], U8, name="dsc%d" % c, align_bytes=64) for c, (lo, w) in enumerate(CHUNKS)]
-        hpm = {
-            (i, c, s): keep.tile([P, T, W], F32, name="h%d%d%d" % (i, c, s), align_bytes=64)
-            for i in range(G)
-            for c in range(2)
-            for s in range(2)
-        }
+        qc = keep.tile([P, G * T, 4, P], U32, name="qc", align_bytes=64)
+        qs = keep.tile([P, G * T, 4, P], U8, name="qs", align_bytes=64)
+        rc = [keep.tile([P, D], U32, name="rc%d" % i, align_bytes=64) for i in range(G)]
+        rs = [keep.tile([P, D], U8, name="rs%d" % i, align_bytes=64) for i in range(G)]
+        dc = [keep.tile([P, H], U32, name="dc%d" % i, align_bytes=64) for i in range(G)]
+        ds = [keep.tile([P, H], U8, name="ds%d" % i, align_bytes=64) for i in range(G)]
+        xm = [keep.tile([P, T, D], BF16, name="xm%d" % i, align_bytes=64) for i in range(G)]
+        xw = [keep.tile([P, D, T], BF16, name="xw%d" % i, align_bytes=64) for i in range(G)]
 
         xv = x.rearrange("(g p t) d -> g p t d", g=G, p=P, t=T)
         ev = e_bytes.rearrange("(g p t) o -> g p t o", g=G, p=P, t=T)
         w1v = w1_words.rearrange("g p w -> p g w")
 
-        def load_w(lo, hi):
-            nc.sync.dma_start(out=w1t[:, :, 2 * lo : 2 * hi], in_=w1v[:, :, 2 * lo : 2 * hi])
-            nc.sync.dma_start(out=w2t[:, 2 * lo : 2 * hi], in_=w2_words[0, :, 2 * lo : 2 * hi])
+        def load_x(b0, n):
+            nc.sync.dma_start(out=xt[b0][:], in_=xv[b0 // T, :, b0 % T : b0 % T + n, :])
 
+        def load_w1(c):
+            nc.sync.dma_start(out=w1t[c][:], in_=w1v[:, :, 2 * W * c : 2 * W * (c + 1)])
 
-        nc.vector.memset(prow[:].bitcast(I32), 0)
-        nc.vector.memset(zero[:].bitcast(I32), 0)
-        nc.vector.memset(ones_bf[:], 1.0)
-        nc.vector.memset(warm[:], 0.0)
         nc.vector.memset(wsc[:].rearrange("p k n -> p (k n)").bitcast(I32), 0)
+        nc.vector.memset(warm[:], 0.0)
         nc.scalar.activation(out=warm[:, 1:2], in_=warm[:, 0:1], func=TANH)
+        nc.gpsimd.dma_start(out=pt[:], in_=p.rearrange("(k q t) -> q k t", k=2, q=P, t=T))
+        make_identity(nc, ident[:])
+        nc.gpsimd.dma_start(out=rb[:], in_=r.rearrange("(g p t) -> p g t", g=G, p=P, t=T))
+        nc.gpsimd.dma_start(out=gb[:], in_=g.rearrange("(g p t) -> p g t", g=G, p=P, t=T))
 
-        def load_x(i, t0, t1):
-            nc.gpsimd.dma_start(out=xt[i][:, t0:t1, :], in_=xv[i, :, t0:t1, :])
-
-        def load_e(i):
-            nc.sync.dma_start(out=eb[:, i, :, :], in_=ev[i])
-
-        def load_r():
-            nc.gpsimd.dma_start(out=rb[:], in_=r.rearrange("(g p t) -> p g t", g=G, p=P, t=T))
-
-        def load_g():
-            nc.gpsimd.dma_start(out=gb[:], in_=g.rearrange("(g p t) -> p g t", g=G, p=P, t=T))
-
-        def load_scales1():
-            for q in range(4):
-                nc.sync.dma_start(
-                    out=wsc[32 * q : 32 * q + 4, 0:2, :].bitcast(I32),
-                    in_=w1_scales[:, 4 * q : 4 * q + 4, :].rearrange("g q n -> q g n").bitcast(I32),
-                )
-        def load_scales2():
-            for q in range(4):
-                nc.sync.dma_start(
-                    out=wsc[32 * q : 32 * q + 4, 2, :].bitcast(I32), in_=w2_scales[0, 4 * q : 4 * q + 4, :].bitcast(I32)
-                )
-
-        def load_prow():
-            nc.sync.dma_start(out=prow[0:1, :], in_=p.rearrange("(o d) -> o d", o=1))
-
-        def load_est():
-            nc.sync.dma_start(out=est[:], in_=e_scale.rearrange("o (q t) -> q (o t)", t=4))
-
-        def make_ident():
-            make_identity(nc, ident[:])
-
-        load_x(0, 0, 1)
-        make_ident()
-        load_x(0, 1, 2)
-        load_x(0, 2, 4)
-        load_r()
-        load_g()
-        load_x(1, 0, 2)
-        load_x(1, 2, 4)
-        load_prow()
-        load_est()
-        load_e(0)
-        load_scales1()
-        load_w(0, W)
-        load_scales2()
-        load_e(1)
-        load_w(W, H)
-        wbank = psum.tile([P, 512], F32, name="u")
-        for j in range(N_WARM):
-            nc.tensor.matmul(wbank[:], lhsT=ones_bf[:], rhs=zero[:], start=True, stop=True)
-        xpw = {}
-        pbk = {}
-        eww = {}
-        xg = {}
-        eg = {}
-        xb = {}
-        ebk = {}
-
-        def ones_p():
-            pbk[0] = psum.tile([P, D], BF16, name="m")
-            for j in range(2):
-                nc.tensor.matmul(
-                    pbk[0][:, 512 * j : 512 * (j + 1)],
-                    lhsT=ones_bf[:],
-                    rhs=prow[:, 512 * j : 512 * (j + 1)],
-                    start=True,
-                    stop=True,
-                )
-
-        def pb_copy():
-            nc.scalar.copy(
-                out=pbp[:].rearrange("p (u q e) -> p u q e", u=2, e=2),
-                in_=pbk[0][:].rearrange("p (q u e) -> p u q e", u=2, e=2),
+        nc.sync.dma_start(out=est[:], in_=e_scale.rearrange("o (q t) -> q (o t)", t=T))
+        load_x(*GROUPS[0])
+        nc.sync.dma_start(out=eb[0][:], in_=ev[0])
+        load_x(*GROUPS[1])
+        for q in range(4):
+            nc.sync.dma_start(
+                out=wsc[32 * q : 32 * q + 4, 0:2, :].bitcast(I32),
+                in_=w1_scales[:, 4 * q : 4 * q + 4, :].rearrange("g q n -> q g n").bitcast(I32),
             )
+        load_w1(0)
+        nc.sync.dma_start(out=w2t[:], in_=w2_words[0])
+        for q in range(4):
+            nc.sync.dma_start(
+                out=wsc[32 * q : 32 * q + 4, 2, :].bitcast(I32), in_=w2_scales[0, 4 * q : 4 * q + 4, :].bitcast(I32)
+            )
+        load_w1(1)
+        load_x(*GROUPS[2])
+        nc.sync.dma_start(out=eb[1][:], in_=ev[1])
+        load_x(*GROUPS[3])
+        load_x(*GROUPS[4])
 
-        def est_half():
-            nc.vector.tensor_scalar(out=est[:], in0=est[:], scalar1=0.5, scalar2=None, op0=MULT)
+        ew = {}
+        xbank = {}
+        ebank = {}
+        qin = {}
 
-        def gs_prep():
-            nc.scalar.activation(
-                out=gs[:].rearrange("p g t -> p (g t)"),
-                in_=gb[:].rearrange("p g t -> p (g t)"),
-                func=COPY,
-                scale=1.0 / 32.0,
+        def e_mul(b):
+            ew[b] = work.tile([P, O], BF16, name="ew", bufs=4, align_bytes=64)
+            nc.vector.tensor_tensor(out=ew[b][:], in0=eb[b // T][:, b % T, :].bitcast(E4M3), in1=esp[:], op=MULT)
+
+        def x_turn(b, i):
+            xbank[b] = bank(i)
+            words = xrow[b].bitcast(F32)
+            for k in range(2):
+                for u in range(2):
+                    lo = P * (2 * u + k)
+                    nc.tensor.transpose(xbank[b][:, lo : lo + P], words[:, 256 * k + u : 256 * (k + 1) : 2], ident[:])
+
+        def e_turn(b0, n, i):
+            ebank[b0] = bank(i)
+            for j in range(n):
+                words = ew[b0 + j][:].bitcast(F32)
+                for u in range(2):
+                    lo = P * (2 * j + u)
+                    nc.tensor.transpose(ebank[b0][:, lo : lo + P], words[:, u:256:2], ident[:])
+
+        def new_qin(b0, n):
+            tile = work.tile([P, n, 4, P * T], BF16, name="qin", bufs=3, align_bytes=64)
+            qin[b0, n] = tile
+            for j in range(n):
+                qin[b0 + j] = tile[:, j]
+
+        def e_copy(b0, n):
+            nc.scalar.copy(
+                out=qin[b0, n][:, :, 2, :].bitcast(F32).rearrange("p j (n u) -> p j n u", u=2),
+                in_=ebank[b0][:, 0 : 2 * P * n].rearrange("p (j u n) -> p j n u", j=n, u=2),
             )
 
         def x_mul(b):
-            xp = work.tile([P, D], BF16, name="xp", align_bytes=64)
             nc.vector.tensor_tensor(
-                out=xp[:].rearrange("p (u q e) -> p u q e", u=2, e=2),
-                in0=xt[b // T][:, b % T, :].rearrange("p (q u e) -> p u q e", u=2, e=2),
-                in1=pbp[:].rearrange("p (u q e) -> p u q e", u=2, e=2),
-                op=MULT,
-            )
-            xpw[b] = xp
-
-        def x_mul_psum(b):
-            xp = work.tile([P, D], BF16, name="xp", align_bytes=64)
-            nc.vector.tensor_tensor(
-                out=xp[:].rearrange("p (u q e) -> p u q e", u=2, e=2),
-                in0=xt[b // T][:, b % T, :].rearrange("p (q u e) -> p u q e", u=2, e=2),
-                in1=pbk[0][:].rearrange("p (q u e) -> p u q e", u=2, e=2),
-                op=MULT,
-            )
-            xpw[b] = xp
-
-        def e_widen(b, n, eng):
-            ew = work.tile([P, n, O], BF16, name="ew%d" % n, bufs=2, align_bytes=64)
-            src = eb[:, b // T, b % T : b % T + n, :].bitcast(E4M3)
-            if eng == "V":
-                nc.vector.tensor_copy(out=ew[:], in_=src)
-            else:
-                nc.scalar.copy(out=ew[:], in_=src)
-            for j in range(n):
-                eww[b + j] = ew[:, j, :]
-
-        def e_mul(b, j):
-            if b % 2 == 0:
-                eg[b // 2] = work.tile([P, 2, 2, P, 4], BF16, name="eg", bufs=2, align_bytes=64)
-            src = ebk[b - j][:, j].bitcast(BF16)
-            nc.vector.tensor_tensor(
-                out=eg[b // 2][:, b % 2, 0].rearrange("p n (u e) -> p n u e", u=2),
-                in0=src.rearrange("p u (n e) -> p n u e", e=2),
-                in1=est[:].unsqueeze(1).to_broadcast([P, P, 4]).rearrange("p n (u e) -> p n u e", u=2),
+                out=qin[b][:, 0:2, :].rearrange("p k (n u e) -> p (k n) u e", u=2, e=2),
+                in0=xbank[b][:].bitcast(BF16).rearrange("p (u m e) -> p m u e", u=2, e=2),
+                in1=pfull[:].rearrange("p k n (u e) -> p (k n) u e", u=2),
                 op=MULT,
             )
 
-        def x_turn(b):
-            xb[b] = psum.tile([P, 2, 2, P], F32, name="m")
-            words = xpw[b][:].bitcast(F32)
-            for k in range(2):
-                for u in range(2):
-                    nc.tensor.transpose(xb[b][:, k, u, :], words[:, 256 * u + 128 * k : 256 * u + 128 * (k + 1)], ident[:])
-
-        def x_copy(b):
-            if b % 2 == 0:
-                xg[b // 2] = work.tile([P, 2, 2, P, 4], BF16, name="xg", bufs=2, align_bytes=64)
-            grouped = xg[b // 2][:, b % 2].rearrange("p k n j -> p k (n j)").bitcast(F32)
-            nc.scalar.copy(
-                out=grouped.rearrange("p k (n u) -> p k n u", u=2), in_=xb[b][:].rearrange("p k u n -> p k n u")
+        def e_neg(b0, n):
+            nc.vector.tensor_scalar(
+                out=qin[b0, n][:, :, 3, :], in0=qin[b0, n][:, :, 2, :], scalar1=-1.0, scalar2=None, op0=MULT
             )
 
-        def e_turn(b, n):
-            ebk[b] = psum.tile([P, n, 2, P], F32, name="m")
-            for j in range(n):
-                words = eww[b + j].bitcast(F32)
-                for u in range(2):
-                    nc.tensor.transpose(ebk[b][:, j, u, :], words[:, u:256:2], ident[:])
-
-        def x_quant(q):
+        def quant(b, lo, hi):
             nc.vector.quantize_mx(
-                out=xc[:, 2 * q : 2 * q + 2].rearrange("p b k n -> p (b k n)").bitcast(FP8X4),
-                scales=xs[:, 2 * q : 2 * q + 2].rearrange("p b k n -> p (b k n)"),
-                in_=xg[q][:].rearrange("p b k n j -> p (b k n j)"),
+                out=qc[:, b, lo:hi, :].rearrange("p k n -> p (k n)").bitcast(FP8X4),
+                scales=qs[:, b, lo:hi, :].rearrange("p k n -> p (k n)"),
+                in_=qin[b][:, lo:hi, :].rearrange("p k m -> p (k m)"),
             )
 
-        def x_quant1(b):
-            nc.vector.quantize_mx(
-                out=xc[:, b].rearrange("p k n -> p (k n)").bitcast(FP8X4),
-                scales=xs[:, b].rearrange("p k n -> p (k n)"),
-                in_=xg[b // 2][:, b % 2].rearrange("p k n j -> p (k n j)"),
-            )
+        def r_mul(b):
+            i, t = divmod(b, T)
+            nc.vector.tensor_scalar(out=xm[i][:, t, :], in0=xrow[b], scalar1=rb[:, i, t : t + 1], scalar2=None, op0=MULT)
 
-        def e_neg(b, n):
-            h = b % 2
-            flat = eg[b // 2][:, h : h + n].rearrange("p b s n j -> p b s (n j)")
-            nc.vector.tensor_scalar(out=flat[:, :, 1], in0=flat[:, :, 0], scalar1=-1.0, scalar2=None, op0=MULT)
+        def weave(copy, dst, src):
+            copy(out=dst.rearrange("p (n j) t -> p n t j", j=4), in_=src.rearrange("p t (n j) -> p n t j", j=4))
 
-        def e_quant(b, n):
-            h = b % 2
+        def r_weave(i, lo, hi, copy):
+            weave(copy, xw[i][:, lo:hi, :], xm[i][:, :, lo:hi])
+
+        def r_quant(i, h):
             nc.vector.quantize_mx(
-                out=ec[:, b : b + n].rearrange("p b s n -> p (b s n)").bitcast(FP8X4),
-                scales=es[:, b : b + n].rearrange("p b s n -> p (b s n)"),
-                in_=eg[b // 2][:, h : h + n].rearrange("p b s n j -> p (b s n j)"),
+                out=rc[i][:, h * W : (h + 1) * W].bitcast(FP8X4),
+                scales=rs[i][:, h * W : (h + 1) * W],
+                in_=xw[i][:, h * W : (h + 1) * W, :].rearrange("p n t -> p (n t)"),
             )
 
         ub = {}
+        hid = {}
 
-        def s1(b, c, s):
-            lo, hi = c * W, (c + 1) * W
-            ub[b, c, s] = psum.tile([P, W], F32, name="u")
-            for k in range(2):
-                nc.tensor.matmul_mx(
-                    out=ub[b, c, s][:],
-                    lhsT=xc[:, b, k, :].bitcast(FP8X4),
-                    lhsT_scale=xs[:, b, k, :],
-                    rhs=w1t[:, k, 2 * lo : 2 * hi].bitcast(FP4X4),
-                    rhs_scale=wsc[:, k, lo:hi],
-                    start=(k == 0),
-                    stop=False,
-                )
+        def f_pass(b, c, s):
             nc.tensor.matmul_mx(
                 out=ub[b, c, s][:],
-                lhsT=ec[:, b, s, :].bitcast(FP8X4),
-                lhsT_scale=es[:, b, s, :],
-                rhs=w2t[:, 2 * lo : 2 * hi].bitcast(FP4X4),
-                rhs_scale=wsc[:, 2, lo:hi],
+                lhsT=qc[:, b, 2 + s, :].bitcast(FP8X4),
+                lhsT_scale=qs[:, b, 2 + s, :],
+                rhs=w2t[:, 2 * W * c : 2 * W * (c + 1)].bitcast(FP4X4),
+                rhs_scale=wsc[:, 2, c * W : (c + 1) * W],
                 start=False,
                 stop=True,
             )
 
         def tanh(b, c, s):
-            nc.scalar.activation(out=hpm[b // T, c, s][:, b % T, :], in_=ub[b, c, s][:], func=TANH)
+            i, t = divmod(b, T)
+            if (i, c, s) not in hid:
+                hid[i, c, s] = work.tile([P, T, W], F32, name="hid%d" % s, bufs=3, align_bytes=64)
+            nc.scalar.activation(out=hid[i, c, s][:, t, :], in_=ub[b, c, s][:], func=TANH)
+
+        def unit(b, c):
+            for s in range(2):
+                ub[b, c, s] = bank(2 * (len(ub) // 2 % 2) + s)
+                for k in range(2):
+                    nc.tensor.matmul_mx(
+                        out=ub[b, c, s][:],
+                        lhsT=qc[:, b, k, :].bitcast(FP8X4),
+                        lhsT_scale=qs[:, b, k, :],
+                        rhs=w1t[c][:, k, :].bitcast(FP4X4),
+                        rhs_scale=wsc[:, k, c * W : (c + 1) * W],
+                        start=(k == 0),
+                        stop=False,
+                    )
+                f_pass(b, c, s)
+                tanh(b, c, s)
 
         db = {}
         dg = {}
 
         def diff(i, c, t0, t1):
             nc.vector.tensor_tensor(
-                out=hpm[i, c, 0][:, t0:t1, :], in0=hpm[i, c, 0][:, t0:t1, :], in1=hpm[i, c, 1][:, t0:t1, :], op=SUB
+                out=hid[i, c, 0][:, t0:t1, :], in0=hid[i, c, 0][:, t0:t1, :], in1=hid[i, c, 1][:, t0:t1, :], op=SUB
             )
 
-        def new_db(i, c):
+        def scale(i, c, t):
             if (i, c) not in db:
-                db[i, c] = work.tile([P, T, W], BF16, name="db", bufs=3, align_bytes=64)
+                db[i, c] = work.tile([P, T, W], BF16, name="db", bufs=4, align_bytes=64)
+            nc.vector.tensor_scalar(
+                out=db[i, c][:, t, :], in0=hid[i, c, 0][:, t, :], scalar1=gs[:, i, t : t + 1], scalar2=None, op0=MULT
+            )
 
         def scale_s(i, c, t):
-            new_db(i, c)
-            nc.scalar.activation(out=db[i, c][:, t, :], in_=hpm[i, c, 0][:, t, :], func=COPY, scale=gs[:, i, t : t + 1])
+            if (i, c) not in db:
+                db[i, c] = work.tile([P, T, W], BF16, name="db", bufs=4, align_bytes=64)
+            nc.scalar.activation(out=db[i, c][:, t, :], in_=hid[i, c, 0][:, t, :], func=COPY, scale=gs[:, i, t : t + 1])
 
-        def scale_v(i, c, t):
-            new_db(i, c)
-            nc.vector.tensor_scalar(
-                out=db[i, c][:, t, :], in0=hpm[i, c, 0][:, t, :], scalar1=gs[:, i, t : t + 1], scalar2=None, op0=MULT
-            )
+        def d_weave(i, c, lo, hi):
+            if (i, c) not in dg:
+                dg[i, c] = work.tile([P, W, T], BF16, name="dg", bufs=2, align_bytes=64)
+            weave(nc.vector.tensor_copy, dg[i, c][:, lo:hi, :], db[i, c][:, :, lo:hi])
 
-        def weave_d(i, c, lo, hi):
-            if lo == 0:
-                dg[i, c] = work.tile([P, W, T], BF16, name="dg", bufs=3, align_bytes=64)
-            nc.vector.tensor_copy(
-                out=dg[i, c][:, lo:hi, :].rearrange("p (n j) t -> p n t j", j=4),
-                in_=db[i, c][:, :, lo:hi].rearrange("p t (n j) -> p n t j", j=4),
-            )
-
-        def quant_d(i, c):
-            lo, w = CHUNKS[c]
+        def d_quant(i, c, lo, hi):
             nc.vector.quantize_mx(
-                out=dc[c][:, i, :].bitcast(FP8X4),
-                scales=dsc[c][:, i, :],
-                in_=dg[i, lo // W][:, lo % W : lo % W + w, :].rearrange("p n t -> p (n t)"),
+                out=dc[i][:, c * W + lo : c * W + hi].bitcast(FP8X4),
+                scales=ds[i][:, c * W + lo : c * W + hi],
+                in_=dg[i, c][:, lo:hi, :].rearrange("p n t -> p (n t)"),
             )
 
-        xm = {}
-        xw = {}
-
-        def new_xw(i):
-            if i not in xw:
-                xw[i] = work.tile([P, D, T], BF16, name="xw", bufs=2, align_bytes=64)
-
-        def r_mul(i, t):
-            if i not in xm:
-                xm[i] = work.tile([P, T, D], BF16, name="xm", bufs=1, align_bytes=64)
-            nc.vector.tensor_scalar(
-                out=xm[i][:, t, :], in0=xt[i][:, t, :], scalar1=rb[:, i, t : t + 1], scalar2=None, op0=MULT
-            )
-
-        def r_prep():
-            nc.scalar.activation(
-                out=rf[:].rearrange("p g t -> p (g t)"), in_=rb[:].rearrange("p g t -> p (g t)"), func=COPY
-            )
-
-        def r_mul_s(i, t):
-            if i not in xm:
-                xm[i] = work.tile([P, T, D], BF16, name="xm", bufs=1, align_bytes=64)
-            nc.scalar.activation(out=xm[i][:, t, :], in_=xt[i][:, t, :], func=COPY, scale=rf[:, i, t : t + 1])
-
-        def r_weave(i, q):
-            new_xw(i)
-            w = D // 4
-            nc.vector.tensor_copy(
-                out=xw[i][:, q * w : (q + 1) * w, :].rearrange("p (n j) t -> p n t j", j=4),
-                in_=xm[i][:, :, q * w : (q + 1) * w].rearrange("p t (n j) -> p n t j", j=4),
-            )
-
-        def r_quant(i, lo, hi):
-            nc.vector.quantize_mx(
-                out=rc[:, i, lo:hi].bitcast(FP8X4), scales=rs[:, i, lo:hi], in_=xw[i][:, lo:hi, :].rearrange("p n t -> p (n t)")
-            )
-
-        ob = {}
-        rest = {}
-
-        def s2_last(c, f, i, tag):
-            lo, w = CHUNKS[c]
-            if i == 0:
-                ob[c, f] = psum.tile([P, w], F32, name=tag)
+        def s2_pass(dst, f, i, lo, hi, start, stop):
             nc.tensor.matmul_mx(
-                out=ob[c, f][:],
-                lhsT=rc[:, i, f * P : (f + 1) * P].bitcast(FP8X4),
-                lhsT_scale=rs[:, i, f * P : (f + 1) * P],
-                rhs=dc[c][:, i, :].bitcast(FP8X4),
-                rhs_scale=dsc[c][:, i, :],
-                start=(i == 0),
-                stop=(i == G - 1),
+                out=dst,
+                lhsT=rc[i][:, f * P : (f + 1) * P].bitcast(FP8X4),
+                lhsT_scale=rs[i][:, f * P : (f + 1) * P],
+                rhs=dc[i][:, lo:hi].bitcast(FP8X4),
+                rhs_scale=ds[i][:, lo:hi],
+                start=start,
+                stop=stop,
             )
 
-        def copy_last(c, f, eng):
-            lo, w = CHUNKS[c]
-            if f % 2 == 0:
-                rest[c, f] = work.tile([P, 2, w], F32, name="resl", bufs=4, align_bytes=64)
-            dst = rest[c, f - f % 2][:, f % 2, :]
-            if eng == "V":
-                nc.vector.tensor_copy(out=dst, in_=ob[c, f][:])
-            else:
-                nc.scalar.copy(out=dst, in_=ob[c, f][:])
-
-        def s2(c, f, i, tag):
-            lo, w = CHUNKS[c]
-            nt = 512 // w
-            if i == 0 and f % nt == 0:
-                ob[c, f] = psum.tile([P, nt, w], F32, name=tag)
-            nc.tensor.matmul_mx(
-                out=ob[c, f - f % nt][:, f % nt, :],
-                lhsT=rc[:, i, f * P : (f + 1) * P].bitcast(FP8X4),
-                lhsT_scale=rs[:, i, f * P : (f + 1) * P],
-                rhs=dc[c][:, i, :].bitcast(FP8X4),
-                rhs_scale=dsc[c][:, i, :],
-                start=(i == 0),
-                stop=(i == G - 1),
-            )
-
-        def out_copy(c, f, eng):
-            lo, w = CHUNKS[c]
-            rest[c, f] = work.tile([P, 512 // w, w], F32, name="res", bufs=6, align_bytes=64)
-            if eng == "V":
-                nc.vector.tensor_copy(out=rest[c, f][:], in_=ob[c, f][:])
-            else:
-                nc.scalar.copy(out=rest[c, f][:], in_=ob[c, f][:])
-
-        def store(c, f):
-            lo, w = CHUNKS[c]
-            nt = 512 // w
+        def put_out(acc, copy, f0, nf, lo, hi):
+            res = work.tile([P, W], F32, name="res", bufs=8, align_bytes=64)
+            copy(out=res[:], in_=acc[:])
             nc.sync.dma_start(
-                out=out[f * P : (f + nt) * P, lo : lo + w].rearrange("(j p) n -> p j n", p=P), in_=rest[c, f][:]
+                out=out[f0 * P : (f0 + nf) * P, lo:hi].rearrange("(j p) n -> p j n", p=P),
+                in_=res[:].rearrange("p (j n) -> p j n", j=nf),
             )
 
+        def turn(b):
+            e_turn(b, 1, 6 + b % 2)
+            x_turn(b, 4 + b % 2)
+            new_qin(b, 1)
+            e_copy(b, 1)
 
-        est_half()
-        ones_p()
-        e_widen(1, 1, "S")
-        x_mul_psum(0)
-        e_widen(2, 2, "S")
-        e_widen(0, 1, "V")
-        x_mul_psum(1)
-        e_turn(0, 1)
-        e_mul(0, 0)
-        pb_copy()
-        e_turn(1, 1)
-        x_turn(0)
-        x_turn(1)
-        e_mul(1, 0)
-        x_copy(0)
-        x_mul(2)
-        x_copy(1)
-        e_turn(2, 2)
+        sbank = bank(7)
+        for t in range(T):
+            nc.tensor.transpose(sbank[:, t * P : (t + 1) * P], est[:, t : t + 1].to_broadcast([P, P]), ident[:])
+        nc.scalar.activation(
+            out=esp[:].rearrange("p (n t) -> p n t", t=T),
+            in_=sbank[:].rearrange("p (t n) -> p n t", t=T),
+            func=COPY,
+            scale=0.5,
+        )
+        nc.vector.tensor_copy(out=pfull[:], in_=pt[:].unsqueeze(2).to_broadcast([P, 2, P, T]))
+        x_turn(0, 4)
+        new_qin(0, 1)
+        new_qin(1, 1)
+        e_mul(0)
+        e_turn(0, 1, 6)
+        e_copy(0, 1)
+        x_turn(1, 5)
+        x_mul(0)
+        e_mul(1)
+        e_turn(1, 1, 7)
+        e_copy(1, 1)
+        quant(0, 0, 2)
         e_neg(0, 1)
-        x_turn(2)
-        x_mul(3)
-        x_quant1(0)
-        x_turn(3)
-        r_prep()
-        r_mul_s(0, 0)
-        e_quant(0, 1)
-        x_quant1(1)
-        e_widen(6, 2, "S")
+        x_mul(1)
+        quant(0, 2, 4)
         e_neg(1, 1)
-        e_mul(2, 0)
-        r_mul(0, 2)
-        s1(0, 0, 1)
-        e_mul(3, 1)
-        s1(0, 0, 0)
-        e_quant(1, 1)
-        s1(1, 0, 1)
-        x_mul(4)
-        e_neg(2, 2)
-        e_widen(4, 2, "S")
-        x_copy(2)
-        x_mul(5)
-        x_copy(3)
-        s1(1, 0, 0)
-        x_turn(4)
-        r_mul(0, 3)
-        x_mul(6)
-        x_quant(1)
-        tanh(0, 0, 0)
-        x_copy(4)
-        e_turn(6, 2)
-        tanh(1, 0, 0)
-        x_turn(6)
-        x_mul(7)
-        e_turn(4, 2)
-        x_turn(5)
-        e_quant(2, 2)
-        s1(2, 1, 0)
-        x_copy(6)
-        s1(2, 0, 0)
-        e_mul(4, 0)
-        x_turn(7)
-        e_mul(6, 0)
-        e_mul(5, 1)
-        e_mul(7, 1)
-        gs_prep()
-        tanh(0, 0, 1)
-        e_neg(4, 2)
-        tanh(1, 0, 1)
-        diff(0, 0, 0, 2)
-        x_copy(5)
-        x_quant(2)
-        tanh(2, 0, 0)
-        tanh(2, 1, 0)
-        r_mul_s(0, 1)
-        s1(3, 0, 0)
-        s1(3, 0, 1)
-        tanh(3, 0, 0)
-        tanh(3, 0, 1)
-        e_quant(4, 2)
-        s1(2, 0, 1)
-        r_weave(0, 0)
-        r_weave(0, 2)
-        x_copy(7)
-        e_neg(6, 2)
-        tanh(2, 0, 1)
+        e_mul(2)
+        r_mul(0)
+        quant(1, 0, 4)
+        for b in range(1, T):
+            r_mul(b)
+        e_mul(3)
+        r_mul(4)
+        r_mul(5)
+        pieces = [(i, q * HALF, (q + 1) * HALF) for i in range(G) for q in range(D // HALF)]
+        on_scalar = pieces[0:4] + pieces[6:8]
+        units = [(T * i + t, c) for i in range(G) for c in range(2) for t in range(T)]
+        nc.scalar.activation(
+            out=gs[:].rearrange("p g t -> p (g t)"), in_=gb[:].rearrange("p g t -> p (g t)"), func=COPY, scale=1.0 / 32.0
+        )
+        for k in range(6):
+            b = k + 2
+            unit(*units[k])
+            turn(b)
+            r_weave(*on_scalar[k], nc.scalar.copy)
+            x_mul(b)
+            if b + 2 < G * T:
+                e_mul(b + 2)
+            else:
+                diff(0, 0, 2 * (k - 4), 2 * (k - 4) + 2)
+            e_neg(b, 1)
+            if k == 0:
+                r_mul(6)
+                r_mul(7)
+            elif k < 3:
+                r_weave(*pieces[3 + k], nc.vector.tensor_copy)
+            else:
+                r_quant(*divmod(k - 3, 2))
+            quant(b, 0, 4)
+
+        def rest(i, c):
+            scale(i, c, 2)
+            scale(i, c, 3)
+
+        unit(*units[6])
         scale_s(0, 0, 0)
-        s1(5, 0, 0)
-        tanh(5, 0, 0)
-        s1(3, 1, 0)
-        r_weave(0, 1)
-        r_weave(0, 3)
-        x_quant(3)
-        s1(4, 0, 0)
-        e_quant(6, 2)
-        diff(0, 0, 2, 4)
-        tanh(4, 0, 0)
-        r_mul(1, 0)
-        r_mul(1, 1)
-        tanh(3, 1, 0)
-        s1(0, 1, 1)
-        tanh(0, 1, 1)
-        r_quant(0, 0, 1024)
-        r_mul(1, 3)
-        s1(4, 0, 1)
-        scale_s(0, 0, 1)
-        s1(5, 0, 1)
-        tanh(4, 0, 1)
-        s1(6, 0, 1)
-        scale_s(0, 0, 2)
-        tanh(5, 0, 1)
-        r_mul(1, 2)
-        s1(6, 0, 0)
-        s1(0, 1, 0)
-        tanh(6, 0, 1)
-        scale_s(0, 0, 3)
-        tanh(6, 0, 0)
-        tanh(0, 1, 0)
-        s1(7, 0, 0)
-        diff(1, 0, 0, 2)
-        scale_s(1, 0, 0)
-        tanh(7, 0, 0)
-        r_weave(1, 0)
-        s1(7, 0, 1)
-        tanh(7, 0, 1)
-        weave_d(0, 0, 0, 256)
-        s1(1, 1, 0)
-        tanh(1, 1, 0)
-        weave_d(0, 0, 256, 512)
-        r_weave(1, 2)
-        scale_s(1, 0, 1)
-        r_weave(1, 1)
-        s1(1, 1, 1)
-        tanh(1, 1, 1)
-        s1(3, 1, 1)
-        tanh(3, 1, 1)
-        s1(5, 1, 1)
-        diff(1, 0, 2, 4)
-        scale_s(1, 0, 2)
-        scale_s(1, 0, 3)
-        quant_d(0, 0)
-        s1(2, 1, 1)
-        tanh(5, 1, 1)
+        rest(0, 0)
+        r_quant(1, 1)
         diff(0, 1, 0, 2)
-        s1(4, 1, 0)
-        r_weave(1, 3)
-        tanh(2, 1, 1)
-        s1(5, 1, 0)
-        weave_d(1, 0, 0, 256)
-        r_quant(1, 0, 1024)
-        tanh(4, 1, 0)
+        unit(*units[7])
+        scale_s(0, 0, 1)
         diff(0, 1, 2, 4)
+        d_weave(0, 0, 0, W)
+        rest(0, 1)
+        d_quant(0, 0, 0, W)
+        unit(*units[8])
         scale_s(0, 1, 0)
-        s1(4, 1, 1)
-        weave_d(1, 0, 256, 512)
-        tanh(5, 1, 0)
-        tanh(4, 1, 1)
-        diff(1, 1, 0, 2)
+        unit(*units[9])
         scale_s(0, 1, 1)
-        scale_s(0, 1, 3)
-        s1(7, 1, 0)
-        s1(7, 1, 1)
-        scale_s(0, 1, 2)
-        tanh(7, 1, 1)
-        s1(6, 1, 1)
-        s1(6, 1, 0)
-        tanh(7, 1, 0)
-        s2(0, 5, 0, "m")
-        quant_d(1, 0)
-        tanh(6, 1, 0)
-        s2(0, 5, 1, "m")
-        s2(0, 1, 0, "m")
-        s2(0, 1, 1, "m")
-        weave_d(0, 1, 0, 256)
-        weave_d(0, 1, 256, 512)
-        scale_v(1, 1, 0)
-        s2(0, 2, 0, "m")
-        s2(0, 2, 1, "m")
-        quant_d(0, 2)
-        tanh(6, 1, 1)
-        diff(1, 1, 2, 4)
-        s2(0, 7, 0, "m")
-        s2(0, 7, 1, "m")
-        s2(0, 0, 0, "m")
-        s2(0, 0, 1, "m")
-        out_copy(0, 5, "S")
-        store(0, 5)
-        out_copy(0, 2, "S")
-        store(0, 2)
-        out_copy(0, 1, "S")
-        out_copy(0, 7, "S")
-        s2(0, 3, 0, "m")
-        s2(0, 3, 1, "m")
-        out_copy(0, 3, "S")
-        scale_v(1, 1, 1)
-        s2_last(2, 5, 0, "u")
-        scale_v(1, 1, 3)
-        scale_v(1, 1, 2)
-        weave_d(1, 1, 0, 256)
-        out_copy(0, 0, "S")
-        s2(0, 6, 0, "m")
-        quant_d(0, 1)
-        s2(0, 4, 0, "m")
-        store(0, 1)
-        store(0, 7)
-        s2(0, 6, 1, "m")
-        out_copy(0, 6, "S")
-        s2(0, 4, 1, "m")
-        out_copy(0, 4, "S")
-        s2(1, 0, 0, "m")
-        quant_d(1, 1)
-        s2_last(2, 1, 0, "u")
-        s2(1, 4, 0, "m")
-        weave_d(1, 1, 256, 512)
-        store(0, 3)
-        quant_d(1, 2)
-        s2(1, 0, 1, "m")
-        s2(1, 1, 0, "m")
-        s2(1, 1, 1, "m")
-        out_copy(1, 0, "S")
-        s2(1, 4, 1, "m")
-        s2(1, 5, 0, "m")
-        s2(1, 5, 1, "m")
-        s2_last(2, 0, 0, "m")
-        s2_last(2, 0, 1, "m")
-        copy_last(2, 0, "S")
-        store(0, 0)
-        s2_last(2, 1, 1, "u")
-        s2_last(2, 5, 1, "u")
-        s2_last(2, 2, 0, "m")
-        s2_last(2, 2, 1, "m")
-        s2_last(2, 3, 0, "u")
-        s2_last(2, 6, 0, "m")
-        s2_last(2, 3, 1, "u")
-        out_copy(1, 4, "S")
-        copy_last(2, 2, "S")
-        s2_last(2, 4, 0, "m")
-        s2_last(2, 4, 1, "m")
-        s2_last(2, 7, 0, "u")
-        store(0, 6)
-        copy_last(2, 1, "V")
-        store(0, 4)
-        store(1, 0)
-        s2_last(2, 6, 1, "m")
-        store(2, 0)
-        copy_last(2, 3, "V")
-        s2_last(2, 7, 1, "u")
-        s2(1, 6, 0, "m")
-        s2(1, 6, 1, "m")
-        store(1, 4)
-        store(2, 2)
-        copy_last(2, 4, "S")
-        copy_last(2, 5, "V")
-        copy_last(2, 6, "S")
-        copy_last(2, 7, "V")
-        store(2, 6)
-        store(2, 4)
-        s2(1, 7, 0, "m")
-        s2(1, 7, 1, "m")
-        out_copy(1, 6, "S")
-        store(1, 6)
-        s2(1, 2, 0, "m")
-        s2(1, 2, 1, "m")
-        s2(1, 3, 0, "m")
-        s2(1, 3, 1, "m")
-        out_copy(1, 2, "S")
-        store(1, 2)
+        diff(1, 0, 0, 2)
+        d_weave(0, 1, 0, W)
+        unit(*units[10])
+        unit(*units[11])
+        scale_s(1, 0, 0)
+        diff(1, 0, 2, 4)
+        d_quant(0, 1, 0, W)
+        rest(1, 0)
+        unit(*units[12])
+        scale_s(1, 0, 1)
+        d_weave(1, 0, 0, W)
+        unit(*units[13])
+        diff(1, 1, 0, 2)
+        d_quant(1, 0, 0, W)
+        unit(*units[14])
+        diff(1, 1, 2, 3)
+        scale(1, 1, 0)
+        scale(1, 1, 1)
+        scale(1, 1, 2)
+        unit(*units[15])
+        diff(1, 1, 3, 4)
+        scale(1, 1, 3)
+        d_weave(1, 1, 0, HALF)
+        d_weave(1, 1, HALF, W)
+        d_quant(1, 1, 0, HALF)
+        d_quant(1, 1, HALF, W)
+
+        for f in range(D // P):
+            acc = bank(4 + f % 4)
+            for i in range(G):
+                s2_pass(acc[:], f, i, 0, W, i == 0, i == G - 1)
+            put_out(acc, nc.scalar.copy, f, 1, 0, W)
+
+        def pair_passes(acc, j, i, lo):
+            for m in range(2):
+                first, last = (i, m) == (0, 0), (i, m) == (G - 1, 1)
+                s2_pass(acc[:, m * HALF : (m + 1) * HALF], 2 * j + m, i, lo, lo + HALF, first, last)
+
+        copies = (nc.vector.tensor_copy, nc.scalar.copy)
+        accs = [bank(j) for j in range(4)]
+        for j in range(4):
+            pair_passes(accs[j], j, 0, W)
+        for j in range(4):
+            pair_passes(accs[j], j, 1, W)
+            put_out(accs[j], copies[j % 2], 2 * j, 2, W, W + HALF)
+        for j in range(4):
+            acc = bank(4 + j)
+            for i in range(G):
+                pair_passes(acc, j, i, W + HALF)
+            put_out(acc, copies[j % 2], 2 * j, 2, W + HALF, H)

@@ -43,7 +43,7 @@ def tile_centredequilibriumpropupdate_w4_kernel(
         xrow = {b0 + j: xt[b0][:, j, :] for b0, n in GROUPS for j in range(n)}
         eb = [keep.tile([P, T, O], U8, name="eb%d" % i, align_bytes=64) for i in range(G)]
         est = keep.tile([P, T], F32, name="est", align_bytes=64)
-        esp = keep.tile([P, O], F32, name="esp", align_bytes=64)
+        esp = keep.tile([P, 2, O], F32, name="esp", align_bytes=64)
         pt = keep.tile([P, 2, T], BF16, name="pt", align_bytes=64)
         pfull = keep.tile([P, 2, P, T], BF16, name="pfull", align_bytes=64)
         w1t = [keep.tile([P, 2, 2 * W], U8, name="w1t%d" % c, align_bytes=64) for c in range(2)]
@@ -51,6 +51,7 @@ def tile_centredequilibriumpropupdate_w4_kernel(
         wsc = keep.tile([P, 3, H], U8, name="wsc", align_bytes=64)
         rb = keep.tile([P, G, T], BF16, name="rb", align_bytes=64)
         gb = keep.tile([P, G, T], BF16, name="gb", align_bytes=64)
+        rf = keep.tile([P, G, T], F32, name="rf", align_bytes=64)
         gs = keep.tile([P, G, T], F32, name="gs", align_bytes=64)
         ident = keep.tile([P, P], F32, name="ident", align_bytes=64)
         warm = keep.tile([P, 2], F32, name="warm", align_bytes=64)
@@ -76,40 +77,47 @@ def tile_centredequilibriumpropupdate_w4_kernel(
         nc.vector.memset(wsc[:].rearrange("p k n -> p (k n)").bitcast(I32), 0)
         nc.vector.memset(warm[:], 0.0)
         nc.scalar.activation(out=warm[:, 1:2], in_=warm[:, 0:1], func=TANH)
-        nc.gpsimd.dma_start(out=pt[:], in_=p.rearrange("(k q t) -> q k t", k=2, q=P, t=T))
         make_identity(nc, ident[:])
-        nc.gpsimd.dma_start(out=rb[:], in_=r.rearrange("(g p t) -> p g t", g=G, p=P, t=T))
-        nc.gpsimd.dma_start(out=gb[:], in_=g.rearrange("(g p t) -> p g t", g=G, p=P, t=T))
 
-        nc.sync.dma_start(out=est[:], in_=e_scale.rearrange("o (q t) -> q (o t)", t=T))
         load_x(*GROUPS[0])
-        nc.sync.dma_start(out=eb[0][:], in_=ev[0])
+        nc.sync.dma_start(out=pt[:], in_=p.rearrange("(k q t) -> q k t", k=2, q=P, t=T))
+        nc.sync.dma_start(out=rb[:], in_=r.rearrange("(g p t) -> p g t", g=G, p=P, t=T))
+        nc.sync.dma_start(out=est[:], in_=e_scale.rearrange("o (q t) -> q (o t)", t=T))
         load_x(*GROUPS[1])
+        nc.sync.dma_start(out=eb[0][:], in_=ev[0])
+        load_w1(0)
+        load_x(*GROUPS[2])
         for q in range(4):
             nc.sync.dma_start(
                 out=wsc[32 * q : 32 * q + 4, 0:2, :].bitcast(I32),
                 in_=w1_scales[:, 4 * q : 4 * q + 4, :].rearrange("g q n -> q g n").bitcast(I32),
             )
-        load_w1(0)
         nc.sync.dma_start(out=w2t[:], in_=w2_words[0])
         for q in range(4):
             nc.sync.dma_start(
                 out=wsc[32 * q : 32 * q + 4, 2, :].bitcast(I32), in_=w2_scales[0, 4 * q : 4 * q + 4, :].bitcast(I32)
             )
-        load_w1(1)
-        load_x(*GROUPS[2])
         nc.sync.dma_start(out=eb[1][:], in_=ev[1])
         load_x(*GROUPS[3])
+        load_w1(1)
         load_x(*GROUPS[4])
+        nc.sync.dma_start(out=gb[:], in_=g.rearrange("(g p t) -> p g t", g=G, p=P, t=T))
 
         ew = {}
         xbank = {}
         ebank = {}
         qin = {}
 
-        def e_mul(b):
-            ew[b] = work.tile([P, O], BF16, name="ew", bufs=4, align_bytes=64)
-            nc.vector.tensor_tensor(out=ew[b][:], in0=eb[b // T][:, b % T, :].bitcast(E4M3), in1=esp[:], op=MULT)
+        def e_mul(b0, n):
+            tile = work.tile([P, n * O], BF16, name="ew", bufs=3, align_bytes=64)
+            nc.vector.tensor_tensor(
+                out=tile[:],
+                in0=eb[b0 // T][:, b0 % T : b0 % T + n, :].rearrange("p j o -> p (j o)").bitcast(E4M3),
+                in1=esp[:, 0:n, :].rearrange("p j o -> p (j o)"),
+                op=MULT,
+            )
+            for j in range(n):
+                ew[b0 + j] = tile[:, j * O : (j + 1) * O]
 
         def x_turn(b, i):
             xbank[b] = bank(i)
@@ -122,13 +130,13 @@ def tile_centredequilibriumpropupdate_w4_kernel(
         def e_turn(b0, n, i):
             ebank[b0] = bank(i)
             for j in range(n):
-                words = ew[b0 + j][:].bitcast(F32)
+                words = ew[b0 + j].bitcast(F32)
                 for u in range(2):
                     lo = P * (2 * j + u)
                     nc.tensor.transpose(ebank[b0][:, lo : lo + P], words[:, u:256:2], ident[:])
 
         def new_qin(b0, n):
-            tile = work.tile([P, n, 4, P * T], BF16, name="qin", bufs=3, align_bytes=64)
+            tile = work.tile([P, n, 4, P * T], BF16, name="qin", bufs=2, align_bytes=64)
             qin[b0, n] = tile
             for j in range(n):
                 qin[b0 + j] = tile[:, j]
@@ -159,9 +167,20 @@ def tile_centredequilibriumpropupdate_w4_kernel(
                 in_=qin[b][:, lo:hi, :].rearrange("p k m -> p (k m)"),
             )
 
+        def quant_pair(b0):
+            nc.vector.quantize_mx(
+                out=qc[:, b0 : b0 + 2].rearrange("p b k n -> p (b k n)").bitcast(FP8X4),
+                scales=qs[:, b0 : b0 + 2].rearrange("p b k n -> p (b k n)"),
+                in_=qin[b0, 2][:].rearrange("p b k m -> p (b k m)"),
+            )
+
         def r_mul(b):
             i, t = divmod(b, T)
             nc.vector.tensor_scalar(out=xm[i][:, t, :], in0=xrow[b], scalar1=rb[:, i, t : t + 1], scalar2=None, op0=MULT)
+
+        def r_mul_s(b):
+            i, t = divmod(b, T)
+            nc.scalar.activation(out=xm[i][:, t, :], in_=xrow[b], func=COPY, scale=rf[:, i, t : t + 1])
 
         def weave(copy, dst, src):
             copy(out=dst.rearrange("p (n j) t -> p n t j", j=4), in_=src.rearrange("p t (n j) -> p n t j", j=4))
@@ -169,11 +188,9 @@ def tile_centredequilibriumpropupdate_w4_kernel(
         def r_weave(i, lo, hi, copy):
             weave(copy, xw[i][:, lo:hi, :], xm[i][:, :, lo:hi])
 
-        def r_quant(i, h):
+        def r_quant(i):
             nc.vector.quantize_mx(
-                out=rc[i][:, h * W : (h + 1) * W].bitcast(FP8X4),
-                scales=rs[i][:, h * W : (h + 1) * W],
-                in_=xw[i][:, h * W : (h + 1) * W, :].rearrange("p n t -> p (n t)"),
+                out=rc[i][:].bitcast(FP8X4), scales=rs[i][:], in_=xw[i][:].rearrange("p n t -> p (n t)")
             )
 
         ub = {}
@@ -193,49 +210,52 @@ def tile_centredequilibriumpropupdate_w4_kernel(
         def tanh(b, c, s):
             i, t = divmod(b, T)
             if (i, c, s) not in hid:
-                hid[i, c, s] = work.tile([P, T, W], F32, name="hid%d" % s, bufs=3, align_bytes=64)
+                hid[i, c, s] = work.tile([P, T, W], F32, name="hid%d" % s, bufs=4, align_bytes=64)
             nc.scalar.activation(out=hid[i, c, s][:, t, :], in_=ub[b, c, s][:], func=TANH)
+
+        def a_passes(b, c, s):
+            ub[b, c, s] = bank(len(ub) % 4)
+            for k in range(2):
+                nc.tensor.matmul_mx(
+                    out=ub[b, c, s][:],
+                    lhsT=qc[:, b, k, :].bitcast(FP8X4),
+                    lhsT_scale=qs[:, b, k, :],
+                    rhs=w1t[c][:, k, :].bitcast(FP4X4),
+                    rhs_scale=wsc[:, k, c * W : (c + 1) * W],
+                    start=(k == 0),
+                    stop=False,
+                )
 
         def unit(b, c):
             for s in range(2):
-                ub[b, c, s] = bank(2 * (len(ub) // 2 % 2) + s)
-                for k in range(2):
-                    nc.tensor.matmul_mx(
-                        out=ub[b, c, s][:],
-                        lhsT=qc[:, b, k, :].bitcast(FP8X4),
-                        lhsT_scale=qs[:, b, k, :],
-                        rhs=w1t[c][:, k, :].bitcast(FP4X4),
-                        rhs_scale=wsc[:, k, c * W : (c + 1) * W],
-                        start=(k == 0),
-                        stop=False,
-                    )
+                a_passes(b, c, s)
                 f_pass(b, c, s)
                 tanh(b, c, s)
 
-        db = {}
         dg = {}
 
-        def diff(i, c, t0, t1):
+        def diff(i, c, lo, hi):
             nc.vector.tensor_tensor(
-                out=hid[i, c, 0][:, t0:t1, :], in0=hid[i, c, 0][:, t0:t1, :], in1=hid[i, c, 1][:, t0:t1, :], op=SUB
+                out=hid[i, c, 0][:, :, lo:hi], in0=hid[i, c, 0][:, :, lo:hi], in1=hid[i, c, 1][:, :, lo:hi], op=SUB
             )
 
-        def scale(i, c, t):
-            if (i, c) not in db:
-                db[i, c] = work.tile([P, T, W], BF16, name="db", bufs=4, align_bytes=64)
-            nc.vector.tensor_scalar(
-                out=db[i, c][:, t, :], in0=hid[i, c, 0][:, t, :], scalar1=gs[:, i, t : t + 1], scalar2=None, op0=MULT
+        def diff_rows(i, c, t0, t1, lo, hi):
+            nc.vector.tensor_tensor(
+                out=hid[i, c, 0][:, t0:t1, lo:hi],
+                in0=hid[i, c, 0][:, t0:t1, lo:hi],
+                in1=hid[i, c, 1][:, t0:t1, lo:hi],
+                op=SUB,
             )
 
-        def scale_s(i, c, t):
-            if (i, c) not in db:
-                db[i, c] = work.tile([P, T, W], BF16, name="db", bufs=4, align_bytes=64)
-            nc.scalar.activation(out=db[i, c][:, t, :], in_=hid[i, c, 0][:, t, :], func=COPY, scale=gs[:, i, t : t + 1])
-
-        def d_weave(i, c, lo, hi):
+        def d_scale(i, c, lo, hi):
             if (i, c) not in dg:
-                dg[i, c] = work.tile([P, W, T], BF16, name="dg", bufs=2, align_bytes=64)
-            weave(nc.vector.tensor_copy, dg[i, c][:, lo:hi, :], db[i, c][:, :, lo:hi])
+                dg[i, c] = work.tile([P, W, T], BF16, name="dg", bufs=3, align_bytes=64)
+            nc.vector.tensor_tensor(
+                out=dg[i, c][:, lo:hi, :].rearrange("p (n j) t -> p n t j", j=4),
+                in0=hid[i, c, 0][:, :, lo:hi].rearrange("p t (n j) -> p n t j", j=4),
+                in1=gs[:, i, :].unsqueeze(1).unsqueeze(3).to_broadcast([P, (hi - lo) // 4, T, 4]),
+                op=MULT,
+            )
 
         def d_quant(i, c, lo, hi):
             nc.vector.quantize_mx(
@@ -263,123 +283,143 @@ def tile_centredequilibriumpropupdate_w4_kernel(
                 in_=res[:].rearrange("p (j n) -> p j n", j=nf),
             )
 
-        def turn(b):
-            e_turn(b, 1, 6 + b % 2)
-            x_turn(b, 4 + b % 2)
-            new_qin(b, 1)
-            e_copy(b, 1)
-
+        nc.vector.tensor_copy(out=pfull[:], in_=pt[:].unsqueeze(2).to_broadcast([P, 2, P, T]))
+        nc.vector.tensor_copy(out=rf[:], in_=rb[:])
+        r_mul_s(0)
+        x_turn(0, 4)
         sbank = bank(7)
         for t in range(T):
             nc.tensor.transpose(sbank[:, t * P : (t + 1) * P], est[:, t : t + 1].to_broadcast([P, P]), ident[:])
-        nc.scalar.activation(
-            out=esp[:].rearrange("p (n t) -> p n t", t=T),
-            in_=sbank[:].rearrange("p (t n) -> p n t", t=T),
-            func=COPY,
-            scale=0.5,
-        )
-        nc.vector.tensor_copy(out=pfull[:], in_=pt[:].unsqueeze(2).to_broadcast([P, 2, P, T]))
-        x_turn(0, 4)
-        new_qin(0, 1)
-        new_qin(1, 1)
-        e_mul(0)
-        e_turn(0, 1, 6)
-        e_copy(0, 1)
+        for j in range(2):
+            nc.scalar.activation(
+                out=esp[:, j, :].rearrange("p (n t) -> p n t", t=T),
+                in_=sbank[:].rearrange("p (t n) -> p n t", t=T),
+                func=COPY,
+                scale=0.5,
+            )
         x_turn(1, 5)
+        new_qin(0, 2)
         x_mul(0)
-        e_mul(1)
-        e_turn(1, 1, 7)
-        e_copy(1, 1)
+        r_mul(1)
         quant(0, 0, 2)
-        e_neg(0, 1)
+        e_mul(0, 1)
+        e_mul(1, 1)
         x_mul(1)
+        r_mul_s(2)
+        for s in range(2):
+            a_passes(0, 0, s)
+        e_turn(0, 2, 6)
+        x_turn(2, 4)
+        e_copy(0, 2)
+        r_mul_s(3)
+        e_mul(2, 2)
+        quant(1, 0, 2)
+        new_qin(2, 2)
+        x_mul(2)
+        e_neg(0, 2)
+        e_mul(4, 2)
         quant(0, 2, 4)
-        e_neg(1, 1)
-        e_mul(2)
-        r_mul(0)
-        quant(1, 0, 4)
-        for b in range(1, T):
-            r_mul(b)
-        e_mul(3)
+        quant(1, 2, 4)
+        for s in range(2):
+            a_passes(1, 0, s)
+        e_turn(2, 2, 7)
+        x_turn(3, 5)
+        e_copy(2, 2)
+        cuts = [0, HALF, W] + list(range(D, D + W + HALF + 1, P))
+        done = [0]
+
+        def xr_piece():
+            if done[0] < len(cuts) - 1:
+                lo, hi = cuts[done[0]], cuts[done[0] + 1]
+                done[0] = done[0] + 1
+                hi = min(hi, lo + HALF)
+                r_weave(lo // D, lo % D, (hi - 1) % D + 1, nc.scalar.copy)
+
+        xr_piece()
+        for b in range(2):
+            for s in range(2):
+                f_pass(b, 0, s)
+                tanh(b, 0, s)
+        x_mul(3)
+        e_neg(2, 2)
         r_mul(4)
+        quant_pair(2)
         r_mul(5)
-        pieces = [(i, q * HALF, (q + 1) * HALF) for i in range(G) for q in range(D // HALF)]
-        on_scalar = pieces[0:4] + pieces[6:8]
-        units = [(T * i + t, c) for i in range(G) for c in range(2) for t in range(T)]
         nc.scalar.activation(
             out=gs[:].rearrange("p g t -> p (g t)"), in_=gb[:].rearrange("p g t -> p (g t)"), func=COPY, scale=1.0 / 32.0
         )
-        for k in range(6):
-            b = k + 2
-            unit(*units[k])
-            turn(b)
-            r_weave(*on_scalar[k], nc.scalar.copy)
-            x_mul(b)
-            if b + 2 < G * T:
-                e_mul(b + 2)
-            else:
-                diff(0, 0, 2 * (k - 4), 2 * (k - 4) + 2)
-            e_neg(b, 1)
-            if k == 0:
-                r_mul(6)
-                r_mul(7)
-            elif k < 3:
-                r_weave(*pieces[3 + k], nc.vector.tensor_copy)
-            else:
-                r_quant(*divmod(k - 3, 2))
-            quant(b, 0, 4)
 
-        def rest(i, c):
-            scale(i, c, 2)
-            scale(i, c, 3)
+        def step(b, c):
+            unit(b, c)
+            xr_piece()
 
-        unit(*units[6])
-        scale_s(0, 0, 0)
-        rest(0, 0)
-        r_quant(1, 1)
-        diff(0, 1, 0, 2)
-        unit(*units[7])
-        scale_s(0, 0, 1)
-        diff(0, 1, 2, 4)
-        d_weave(0, 0, 0, W)
-        rest(0, 1)
+        def first_turn(b0):
+            e_turn(b0, 2, 6 + b0 // 2 % 2)
+            x_turn(b0, 4)
+            new_qin(b0, 2)
+            e_copy(b0, 2)
+
+        first_turn(4)
+        x_mul(4)
+        e_mul(6, 2)
+        e_neg(4, 2)
+        r_mul(6)
+        r_mul(7)
+        step(0, 1)
+        x_turn(5, 5)
+        x_mul(5)
+        r_weave(0, W + HALF, D, nc.vector.tensor_copy)
+        step(2, 0)
+        first_turn(6)
+        x_mul(6)
+        quant_pair(4)
+        e_neg(6, 2)
+        step(3, 0)
+        x_turn(7, 5)
+        x_mul(7)
+        diff(0, 0, 0, W)
+        quant_pair(6)
+        d_scale(0, 0, 0, W)
+        step(1, 1)
+        step(4, 0)
+        step(5, 0)
+        r_quant(0)
         d_quant(0, 0, 0, W)
-        unit(*units[8])
-        scale_s(0, 1, 0)
-        unit(*units[9])
-        scale_s(0, 1, 1)
-        diff(1, 0, 0, 2)
-        d_weave(0, 1, 0, W)
-        unit(*units[10])
-        unit(*units[11])
-        scale_s(1, 0, 0)
-        diff(1, 0, 2, 4)
-        d_quant(0, 1, 0, W)
-        rest(1, 0)
-        unit(*units[12])
-        scale_s(1, 0, 1)
-        d_weave(1, 0, 0, W)
-        unit(*units[13])
-        diff(1, 1, 0, 2)
+        diff_rows(1, 0, 0, 2, 0, W)
+        r_weave(1, W + HALF, D, nc.vector.tensor_copy)
+        step(2, 1)
+        diff_rows(0, 1, 0, 3, 0, W)
+        step(6, 0)
+        step(7, 0)
+        r_quant(1)
+        diff_rows(1, 0, 2, 4, 0, W)
+        step(3, 1)
+        diff_rows(0, 1, 3, 4, 0, W)
+        d_scale(1, 0, 0, W)
+        step(4, 1)
+        step(5, 1)
+        d_scale(0, 1, 0, HALF)
         d_quant(1, 0, 0, W)
-        unit(*units[14])
-        diff(1, 1, 2, 3)
-        scale(1, 1, 0)
-        scale(1, 1, 1)
-        scale(1, 1, 2)
-        unit(*units[15])
-        diff(1, 1, 3, 4)
-        scale(1, 1, 3)
-        d_weave(1, 1, 0, HALF)
-        d_weave(1, 1, HALF, W)
-        d_quant(1, 1, 0, HALF)
-        d_quant(1, 1, HALF, W)
+        step(6, 1)
+        diff_rows(1, 1, 0, 3, 0, W)
 
-        for f in range(D // P):
+        def first_half(f):
             acc = bank(4 + f % 4)
             for i in range(G):
                 s2_pass(acc[:], f, i, 0, W, i == 0, i == G - 1)
             put_out(acc, nc.scalar.copy, f, 1, 0, W)
+
+        step(7, 1)
+        diff_rows(1, 1, 3, 4, 0, W)
+        d_quant(0, 1, 0, HALF)
+        d_scale(1, 1, 0, HALF)
+        d_scale(0, 1, HALF, W)
+        d_quant(1, 1, 0, HALF)
+        d_scale(1, 1, HALF, W)
+        d_quant(0, 1, HALF, W)
+        d_quant(1, 1, HALF, W)
+        for f in range(D // P):
+            first_half(f)
 
         def pair_passes(acc, j, i, lo):
             for m in range(2):
@@ -387,14 +427,11 @@ def tile_centredequilibriumpropupdate_w4_kernel(
                 s2_pass(acc[:, m * HALF : (m + 1) * HALF], 2 * j + m, i, lo, lo + HALF, first, last)
 
         copies = (nc.vector.tensor_copy, nc.scalar.copy)
-        accs = [bank(j) for j in range(4)]
-        for j in range(4):
-            pair_passes(accs[j], j, 0, W)
-        for j in range(4):
-            pair_passes(accs[j], j, 1, W)
-            put_out(accs[j], copies[j % 2], 2 * j, 2, W, W + HALF)
-        for j in range(4):
-            acc = bank(4 + j)
-            for i in range(G):
-                pair_passes(acc, j, i, W + HALF)
-            put_out(acc, copies[j % 2], 2 * j, 2, W + HALF, H)
+        for h in range(2):
+            lo = W + h * HALF
+            accs = [bank(4 * h + j) for j in range(4)]
+            for j in range(4):
+                pair_passes(accs[j], j, 0, lo)
+            for j in range(4):
+                pair_passes(accs[j], j, 1, lo)
+                put_out(accs[j], copies[(j + 1) % 2 if h else 1], 2 * j, 2, lo, lo + HALF)

@@ -51,7 +51,6 @@ def tile_centredequilibriumpropupdate_w4_kernel(
         wsc = keep.tile([P, 3, H], U8, name="wsc", align_bytes=64)
         rb = keep.tile([P, G, T], BF16, name="rb", align_bytes=64)
         gb = keep.tile([P, G, T], BF16, name="gb", align_bytes=64)
-        rf = keep.tile([P, G, T], F32, name="rf", align_bytes=64)
         gs = keep.tile([P, G, T], F32, name="gs", align_bytes=64)
         ident = keep.tile([P, P], F32, name="ident", align_bytes=64)
         warm = keep.tile([P, 2], F32, name="warm", align_bytes=64)
@@ -178,10 +177,6 @@ def tile_centredequilibriumpropupdate_w4_kernel(
             i, t = divmod(b, T)
             nc.vector.tensor_scalar(out=xm[i][:, t, :], in0=xrow[b], scalar1=rb[:, i, t : t + 1], scalar2=None, op0=MULT)
 
-        def r_mul_s(b):
-            i, t = divmod(b, T)
-            nc.scalar.activation(out=xm[i][:, t, :], in_=xrow[b], func=COPY, scale=rf[:, i, t : t + 1])
-
         def weave(copy, dst, src):
             copy(out=dst.rearrange("p (n j) t -> p n t j", j=4), in_=src.rearrange("p t (n j) -> p n t j", j=4))
 
@@ -276,16 +271,20 @@ def tile_centredequilibriumpropupdate_w4_kernel(
             )
 
         def put_out(acc, copy, f0, nf, lo, hi):
-            res = work.tile([P, W], F32, name="res", bufs=8, align_bytes=64)
+            res = work.tile([P, W], F32, name="res", bufs=10, align_bytes=64)
             copy(out=res[:], in_=acc[:])
             nc.sync.dma_start(
                 out=out[f0 * P : (f0 + nf) * P, lo:hi].rearrange("(j p) n -> p j n", p=P),
                 in_=res[:].rearrange("p (j n) -> p j n", j=nf),
             )
 
+        pieces = [(i, q * HALF, (q + 1) * HALF) for i in range(G) for q in range(D // HALF)]
+
+        def xr_piece(copy):
+            r_weave(*pieces.pop(0), copy)
+
         nc.vector.tensor_copy(out=pfull[:], in_=pt[:].unsqueeze(2).to_broadcast([P, 2, P, T]))
-        nc.vector.tensor_copy(out=rf[:], in_=rb[:])
-        r_mul_s(0)
+        r_mul(0)
         x_turn(0, 4)
         sbank = bank(7)
         for t in range(T):
@@ -305,13 +304,15 @@ def tile_centredequilibriumpropupdate_w4_kernel(
         e_mul(0, 1)
         e_mul(1, 1)
         x_mul(1)
-        r_mul_s(2)
+        r_mul(2)
+        r_mul(3)
         for s in range(2):
             a_passes(0, 0, s)
         e_turn(0, 2, 6)
         x_turn(2, 4)
+        xr_piece(nc.scalar.copy)
         e_copy(0, 2)
-        r_mul_s(3)
+        xr_piece(nc.scalar.copy)
         e_mul(2, 2)
         quant(1, 0, 2)
         new_qin(2, 2)
@@ -325,17 +326,6 @@ def tile_centredequilibriumpropupdate_w4_kernel(
         e_turn(2, 2, 7)
         x_turn(3, 5)
         e_copy(2, 2)
-        cuts = [0, HALF, W] + list(range(D, D + W + HALF + 1, P))
-        done = [0]
-
-        def xr_piece():
-            if done[0] < len(cuts) - 1:
-                lo, hi = cuts[done[0]], cuts[done[0] + 1]
-                done[0] = done[0] + 1
-                hi = min(hi, lo + HALF)
-                r_weave(lo // D, lo % D, (hi - 1) % D + 1, nc.scalar.copy)
-
-        xr_piece()
         for b in range(2):
             for s in range(2):
                 f_pass(b, 0, s)
@@ -349,10 +339,6 @@ def tile_centredequilibriumpropupdate_w4_kernel(
             out=gs[:].rearrange("p g t -> p (g t)"), in_=gb[:].rearrange("p g t -> p (g t)"), func=COPY, scale=1.0 / 32.0
         )
 
-        def step(b, c):
-            unit(b, c)
-            xr_piece()
-
         def first_turn(b0):
             e_turn(b0, 2, 6 + b0 // 2 % 2)
             x_turn(b0, 4)
@@ -362,45 +348,49 @@ def tile_centredequilibriumpropupdate_w4_kernel(
         first_turn(4)
         x_mul(4)
         e_mul(6, 2)
-        e_neg(4, 2)
         r_mul(6)
         r_mul(7)
-        step(0, 1)
+        e_neg(4, 2)
+        unit(0, 1)
+        xr_piece(nc.scalar.copy)
         x_turn(5, 5)
         x_mul(5)
-        r_weave(0, W + HALF, D, nc.vector.tensor_copy)
-        step(2, 0)
+        xr_piece(nc.vector.tensor_copy)
+        quant_pair(4)
+        unit(2, 0)
         first_turn(6)
         x_mul(6)
-        quant_pair(4)
+        xr_piece(nc.vector.tensor_copy)
         e_neg(6, 2)
-        step(3, 0)
+        r_quant(0)
+        unit(3, 0)
+        xr_piece(nc.scalar.copy)
         x_turn(7, 5)
         x_mul(7)
-        diff(0, 0, 0, W)
+        xr_piece(nc.vector.tensor_copy)
         quant_pair(6)
+        diff(0, 0, 0, W)
+        xr_piece(nc.vector.tensor_copy)
         d_scale(0, 0, 0, W)
-        step(1, 1)
-        step(4, 0)
-        step(5, 0)
-        r_quant(0)
+        unit(1, 1)
+        unit(4, 0)
+        unit(5, 0)
+        r_quant(1)
         d_quant(0, 0, 0, W)
         diff_rows(1, 0, 0, 2, 0, W)
-        r_weave(1, W + HALF, D, nc.vector.tensor_copy)
-        step(2, 1)
+        unit(2, 1)
         diff_rows(0, 1, 0, 3, 0, W)
-        step(6, 0)
-        step(7, 0)
-        r_quant(1)
+        unit(6, 0)
+        unit(7, 0)
         diff_rows(1, 0, 2, 4, 0, W)
-        step(3, 1)
+        unit(3, 1)
         diff_rows(0, 1, 3, 4, 0, W)
         d_scale(1, 0, 0, W)
-        step(4, 1)
-        step(5, 1)
+        unit(4, 1)
+        unit(5, 1)
         d_scale(0, 1, 0, HALF)
         d_quant(1, 0, 0, W)
-        step(6, 1)
+        unit(6, 1)
         diff_rows(1, 1, 0, 3, 0, W)
 
         def first_half(f):
@@ -409,7 +399,7 @@ def tile_centredequilibriumpropupdate_w4_kernel(
                 s2_pass(acc[:], f, i, 0, W, i == 0, i == G - 1)
             put_out(acc, nc.scalar.copy, f, 1, 0, W)
 
-        step(7, 1)
+        unit(7, 1)
         diff_rows(1, 1, 3, 4, 0, W)
         d_quant(0, 1, 0, HALF)
         d_scale(1, 1, 0, HALF)
@@ -434,4 +424,4 @@ def tile_centredequilibriumpropupdate_w4_kernel(
                 pair_passes(accs[j], j, 0, lo)
             for j in range(4):
                 pair_passes(accs[j], j, 1, lo)
-                put_out(accs[j], copies[(j + 1) % 2 if h else 1], 2 * j, 2, lo, lo + HALF)
+                put_out(accs[j], copies[(j + 1) % 2], 2 * j, 2, lo, lo + HALF)

@@ -51,11 +51,12 @@ def tile_centredequilibriumpropupdate_w4_kernel(
         wsc = keep.tile([P, 3, H], U8, name="wsc", align_bytes=64)
         rb = keep.tile([P, G, T], BF16, name="rb", align_bytes=64)
         gb = keep.tile([P, G, T], BF16, name="gb", align_bytes=64)
+        rf = keep.tile([P, G, T], F32, name="rf", align_bytes=64)
         gs = keep.tile([P, G, T], F32, name="gs", align_bytes=64)
         ident = keep.tile([P, P], F32, name="ident", align_bytes=64)
         warm = keep.tile([P, 2], F32, name="warm", align_bytes=64)
-        qc = keep.tile([P, G * T, 4, P], U32, name="qc", align_bytes=64)
-        qs = keep.tile([P, G * T, 4, P], U8, name="qs", align_bytes=64)
+        qc = keep.tile([P, G * T // 2, 8, P], U32, name="qc", align_bytes=64)
+        qs = keep.tile([P, G * T // 2, 8, P], U8, name="qs", align_bytes=64)
         rc = [keep.tile([P, D], U32, name="rc%d" % i, align_bytes=64) for i in range(G)]
         rs = [keep.tile([P, D], U8, name="rs%d" % i, align_bytes=64) for i in range(G)]
         dc = [keep.tile([P, H], U32, name="dc%d" % i, align_bytes=64) for i in range(G)]
@@ -91,12 +92,12 @@ def tile_centredequilibriumpropupdate_w4_kernel(
                 out=wsc[32 * q : 32 * q + 4, 0:2, :].bitcast(I32),
                 in_=w1_scales[:, 4 * q : 4 * q + 4, :].rearrange("g q n -> q g n").bitcast(I32),
             )
+        nc.sync.dma_start(out=eb[1][:], in_=ev[1])
         nc.sync.dma_start(out=w2t[:], in_=w2_words[0])
         for q in range(4):
             nc.sync.dma_start(
                 out=wsc[32 * q : 32 * q + 4, 2, :].bitcast(I32), in_=w2_scales[0, 4 * q : 4 * q + 4, :].bitcast(I32)
             )
-        nc.sync.dma_start(out=eb[1][:], in_=ev[1])
         load_x(*GROUPS[3])
         load_w1(1)
         load_x(*GROUPS[4])
@@ -108,7 +109,7 @@ def tile_centredequilibriumpropupdate_w4_kernel(
         qin = {}
 
         def e_mul(b0, n):
-            tile = work.tile([P, n * O], BF16, name="ew", bufs=3, align_bytes=64)
+            tile = work.tile([P, n * O], BF16, name="ew", bufs=4, align_bytes=64)
             nc.vector.tensor_tensor(
                 out=tile[:],
                 in0=eb[b0 // T][:, b0 % T : b0 % T + n, :].rearrange("p j o -> p (j o)").bitcast(E4M3),
@@ -134,48 +135,46 @@ def tile_centredequilibriumpropupdate_w4_kernel(
                     lo = P * (2 * j + u)
                     nc.tensor.transpose(ebank[b0][:, lo : lo + P], words[:, u:256:2], ident[:])
 
-        def new_qin(b0, n):
-            tile = work.tile([P, n, 4, P * T], BF16, name="qin", bufs=2, align_bytes=64)
-            qin[b0, n] = tile
-            for j in range(n):
-                qin[b0 + j] = tile[:, j]
+        def slot(b, k):
+            return 2 * (b % 2) + k if k < 2 else 2 * k + b % 2
 
-        def e_copy(b0, n):
+        def new_qin(b0):
+            qin[b0 // 2] = work.tile([P, 8, P * T], BF16, name="qin", bufs=2, align_bytes=64)
+
+        def e_copy(b0):
             nc.scalar.copy(
-                out=qin[b0, n][:, :, 2, :].bitcast(F32).rearrange("p j (n u) -> p j n u", u=2),
-                in_=ebank[b0][:, 0 : 2 * P * n].rearrange("p (j u n) -> p j n u", j=n, u=2),
+                out=qin[b0 // 2][:, 4:6, :].bitcast(F32).rearrange("p j (n u) -> p j n u", u=2),
+                in_=ebank[b0][:].rearrange("p (j u n) -> p j n u", j=2, u=2),
             )
 
         def x_mul(b):
+            lo = slot(b, 0)
             nc.vector.tensor_tensor(
-                out=qin[b][:, 0:2, :].rearrange("p k (n u e) -> p (k n) u e", u=2, e=2),
+                out=qin[b // 2][:, lo : lo + 2, :].rearrange("p k (n u e) -> p (k n) u e", u=2, e=2),
                 in0=xbank[b][:].bitcast(BF16).rearrange("p (u m e) -> p m u e", u=2, e=2),
                 in1=pfull[:].rearrange("p k n (u e) -> p (k n) u e", u=2),
                 op=MULT,
             )
 
-        def e_neg(b0, n):
+        def e_neg(b0):
             nc.vector.tensor_scalar(
-                out=qin[b0, n][:, :, 3, :], in0=qin[b0, n][:, :, 2, :], scalar1=-1.0, scalar2=None, op0=MULT
+                out=qin[b0 // 2][:, 6:8, :], in0=qin[b0 // 2][:, 4:6, :], scalar1=-1.0, scalar2=None, op0=MULT
             )
 
-        def quant(b, lo, hi):
+        def quant(b0, lo, hi):
             nc.vector.quantize_mx(
-                out=qc[:, b, lo:hi, :].rearrange("p k n -> p (k n)").bitcast(FP8X4),
-                scales=qs[:, b, lo:hi, :].rearrange("p k n -> p (k n)"),
-                in_=qin[b][:, lo:hi, :].rearrange("p k m -> p (k m)"),
-            )
-
-        def quant_pair(b0):
-            nc.vector.quantize_mx(
-                out=qc[:, b0 : b0 + 2].rearrange("p b k n -> p (b k n)").bitcast(FP8X4),
-                scales=qs[:, b0 : b0 + 2].rearrange("p b k n -> p (b k n)"),
-                in_=qin[b0, 2][:].rearrange("p b k m -> p (b k m)"),
+                out=qc[:, b0 // 2, lo:hi, :].rearrange("p k n -> p (k n)").bitcast(FP8X4),
+                scales=qs[:, b0 // 2, lo:hi, :].rearrange("p k n -> p (k n)"),
+                in_=qin[b0 // 2][:, lo:hi, :].rearrange("p k m -> p (k m)"),
             )
 
         def r_mul(b):
             i, t = divmod(b, T)
             nc.vector.tensor_scalar(out=xm[i][:, t, :], in0=xrow[b], scalar1=rb[:, i, t : t + 1], scalar2=None, op0=MULT)
+
+        def r_mul_s(b):
+            i, t = divmod(b, T)
+            nc.scalar.activation(out=xm[i][:, t, :], in_=xrow[b], func=COPY, scale=rf[:, i, t : t + 1])
 
         def weave(copy, dst, src):
             copy(out=dst.rearrange("p (n j) t -> p n t j", j=4), in_=src.rearrange("p t (n j) -> p n t j", j=4))
@@ -194,8 +193,8 @@ def tile_centredequilibriumpropupdate_w4_kernel(
         def f_pass(b, c, s):
             nc.tensor.matmul_mx(
                 out=ub[b, c, s][:],
-                lhsT=qc[:, b, 2 + s, :].bitcast(FP8X4),
-                lhsT_scale=qs[:, b, 2 + s, :],
+                lhsT=qc[:, b // 2, slot(b, 2 + s), :].bitcast(FP8X4),
+                lhsT_scale=qs[:, b // 2, slot(b, 2 + s), :],
                 rhs=w2t[:, 2 * W * c : 2 * W * (c + 1)].bitcast(FP4X4),
                 rhs_scale=wsc[:, 2, c * W : (c + 1) * W],
                 start=False,
@@ -213,8 +212,8 @@ def tile_centredequilibriumpropupdate_w4_kernel(
             for k in range(2):
                 nc.tensor.matmul_mx(
                     out=ub[b, c, s][:],
-                    lhsT=qc[:, b, k, :].bitcast(FP8X4),
-                    lhsT_scale=qs[:, b, k, :],
+                    lhsT=qc[:, b // 2, slot(b, k), :].bitcast(FP8X4),
+                    lhsT_scale=qs[:, b // 2, slot(b, k), :],
                     rhs=w1t[c][:, k, :].bitcast(FP4X4),
                     rhs_scale=wsc[:, k, c * W : (c + 1) * W],
                     start=(k == 0),
@@ -280,10 +279,11 @@ def tile_centredequilibriumpropupdate_w4_kernel(
 
         pieces = [(i, q * HALF, (q + 1) * HALF) for i in range(G) for q in range(D // HALF)]
 
-        def xr_piece(copy):
-            r_weave(*pieces.pop(0), copy)
+        def xr_piece():
+            r_weave(*pieces.pop(0), nc.scalar.copy)
 
         nc.vector.tensor_copy(out=pfull[:], in_=pt[:].unsqueeze(2).to_broadcast([P, 2, P, T]))
+        nc.vector.tensor_copy(out=rf[:], in_=rb[:])
         r_mul(0)
         x_turn(0, 4)
         sbank = bank(7)
@@ -297,44 +297,44 @@ def tile_centredequilibriumpropupdate_w4_kernel(
                 scale=0.5,
             )
         x_turn(1, 5)
-        new_qin(0, 2)
+        new_qin(0)
         x_mul(0)
         r_mul(1)
         quant(0, 0, 2)
         e_mul(0, 1)
         e_mul(1, 1)
         x_mul(1)
-        r_mul(2)
-        r_mul(3)
+        r_mul_s(2)
+        r_mul_s(3)
         for s in range(2):
             a_passes(0, 0, s)
         e_turn(0, 2, 6)
         x_turn(2, 4)
-        xr_piece(nc.scalar.copy)
-        e_copy(0, 2)
-        xr_piece(nc.scalar.copy)
+        xr_piece()
+        e_copy(0)
+        xr_piece()
         e_mul(2, 2)
-        quant(1, 0, 2)
-        new_qin(2, 2)
-        x_mul(2)
-        e_neg(0, 2)
-        e_mul(4, 2)
         quant(0, 2, 4)
-        quant(1, 2, 4)
+        e_mul(4, 2)
+        new_qin(2)
+        x_mul(2)
+        e_neg(0)
+        r_mul(4)
+        quant(0, 4, 8)
         for s in range(2):
             a_passes(1, 0, s)
         e_turn(2, 2, 7)
         x_turn(3, 5)
-        e_copy(2, 2)
+        e_copy(2)
+        xr_piece()
         for b in range(2):
             for s in range(2):
                 f_pass(b, 0, s)
                 tanh(b, 0, s)
         x_mul(3)
-        e_neg(2, 2)
-        r_mul(4)
-        quant_pair(2)
+        e_neg(2)
         r_mul(5)
+        quant(2, 0, 8)
         nc.scalar.activation(
             out=gs[:].rearrange("p g t -> p (g t)"), in_=gb[:].rearrange("p g t -> p (g t)"), func=COPY, scale=1.0 / 32.0
         )
@@ -342,86 +342,92 @@ def tile_centredequilibriumpropupdate_w4_kernel(
         def first_turn(b0):
             e_turn(b0, 2, 6 + b0 // 2 % 2)
             x_turn(b0, 4)
-            new_qin(b0, 2)
-            e_copy(b0, 2)
+            new_qin(b0)
+            e_copy(b0)
 
+        e_mul(6, 2)
         first_turn(4)
         x_mul(4)
-        e_mul(6, 2)
         r_mul(6)
+        e_neg(4)
         r_mul(7)
-        e_neg(4, 2)
         unit(0, 1)
-        xr_piece(nc.scalar.copy)
+        xr_piece()
         x_turn(5, 5)
         x_mul(5)
-        xr_piece(nc.vector.tensor_copy)
-        quant_pair(4)
+        diff_rows(0, 0, 0, 2, 0, W)
+        quant(4, 0, 8)
         unit(2, 0)
         first_turn(6)
         x_mul(6)
-        xr_piece(nc.vector.tensor_copy)
-        e_neg(6, 2)
         r_quant(0)
+        e_neg(6)
         unit(3, 0)
-        xr_piece(nc.scalar.copy)
+        xr_piece()
         x_turn(7, 5)
         x_mul(7)
-        xr_piece(nc.vector.tensor_copy)
-        quant_pair(6)
-        diff(0, 0, 0, W)
-        xr_piece(nc.vector.tensor_copy)
-        d_scale(0, 0, 0, W)
+        diff_rows(0, 0, 2, 4, 0, W)
+        quant(6, 0, 8)
         unit(1, 1)
-        unit(4, 0)
-        unit(5, 0)
-        r_quant(1)
+        xr_piece()
+        d_scale(0, 0, 0, W)
+        r_weave(1, W + HALF, D, nc.vector.tensor_copy)
         d_quant(0, 0, 0, W)
+        diff_rows(0, 1, 0, 2, 0, W)
+        for b in range(T, 2 * T):
+            unit(b, 0)
+            if b % 2 == 0:
+                lo = W + (b - T) // 2 * P
+                r_weave(1, lo, lo + P, nc.scalar.copy)
         diff_rows(1, 0, 0, 2, 0, W)
-        unit(2, 1)
-        diff_rows(0, 1, 0, 3, 0, W)
-        unit(6, 0)
-        unit(7, 0)
+        r_quant(1)
         diff_rows(1, 0, 2, 4, 0, W)
+        unit(2, 1)
         unit(3, 1)
-        diff_rows(0, 1, 3, 4, 0, W)
+        diff_rows(0, 1, 2, 3, 0, W)
         d_scale(1, 0, 0, W)
-        unit(4, 1)
-        unit(5, 1)
-        d_scale(0, 1, 0, HALF)
+        diff_rows(0, 1, 3, 4, 0, W)
         d_quant(1, 0, 0, W)
-        unit(6, 1)
-        diff_rows(1, 1, 0, 3, 0, W)
-
-        def first_half(f):
+        d_scale(0, 1, 0, HALF)
+        for b in range(T, 2 * T - 1):
+            unit(b, 1)
+        diff_rows(1, 1, 0, 3, 0, HALF)
+        d_quant(0, 1, 0, HALF)
+        unit(2 * T - 1, 1)
+        diff_rows(1, 1, 3, 4, 0, HALF)
+        diff_rows(1, 1, 0, 4, HALF, HALF + P)
+        for f in range(D // P):
             acc = bank(4 + f % 4)
             for i in range(G):
                 s2_pass(acc[:], f, i, 0, W, i == 0, i == G - 1)
             put_out(acc, nc.scalar.copy, f, 1, 0, W)
-
-        unit(7, 1)
-        diff_rows(1, 1, 3, 4, 0, W)
-        d_quant(0, 1, 0, HALF)
         d_scale(1, 1, 0, HALF)
         d_scale(0, 1, HALF, W)
         d_quant(1, 1, 0, HALF)
-        d_scale(1, 1, HALF, W)
+        d_scale(1, 1, HALF, HALF + P)
         d_quant(0, 1, HALF, W)
-        d_quant(1, 1, HALF, W)
-        for f in range(D // P):
-            first_half(f)
+        diff_rows(1, 1, 0, 4, HALF + P, W)
+        d_quant(1, 1, HALF, HALF + P)
+        d_scale(1, 1, HALF + P, W)
+        d_quant(1, 1, HALF + P, W)
 
-        def pair_passes(acc, j, i, lo):
-            for m in range(2):
-                first, last = (i, m) == (0, 0), (i, m) == (G - 1, 1)
-                s2_pass(acc[:, m * HALF : (m + 1) * HALF], 2 * j + m, i, lo, lo + HALF, first, last)
+        copies = (nc.scalar.copy, nc.vector.tensor_copy)
+        free = list(range(8))
+        chunks = []
+        for lo, hi in ((W, W + HALF), (W + HALF, W + HALF + P), (W + HALF + P, H)):
+            nf = W // (hi - lo)
+            chunks.append((lo, hi, nf, [bank(free.pop(0)) for j in range(D // P // nf)]))
 
-        copies = (nc.vector.tensor_copy, nc.scalar.copy)
-        for h in range(2):
-            lo = W + h * HALF
-            accs = [bank(4 * h + j) for j in range(4)]
-            for j in range(4):
-                pair_passes(accs[j], j, 0, lo)
-            for j in range(4):
-                pair_passes(accs[j], j, 1, lo)
-                put_out(accs[j], copies[(j + 1) % 2], 2 * j, 2, lo, lo + HALF)
+        def bank_passes(acc, f0, nf, i, lo, hi):
+            for m in range(nf):
+                first, last = (i, m) == (0, 0), (i, m) == (G - 1, nf - 1)
+                s2_pass(acc[:, m * (hi - lo) : (m + 1) * (hi - lo)], f0 + m, i, lo, hi, first, last)
+
+        for n, (lo, hi, nf, accs) in enumerate(chunks):
+            if n < 2:
+                for mlo, mhi, mnf, maccs in chunks[n : 2 * n + 1]:
+                    for j, acc in enumerate(maccs):
+                        bank_passes(acc, mnf * j, mnf, 0, mlo, mhi)
+            for j, acc in enumerate(accs):
+                bank_passes(acc, nf * j, nf, 1, lo, hi)
+                put_out(acc, copies[j % 2 if n else 0], nf * j, nf, lo, hi)

@@ -395,7 +395,7 @@ def tile_centredequilibriumpropupdate_w4_kernel(
         d_quant(0, 1, 0, HALF)
         unit(2 * T - 1, 1)
         diff_rows(1, 1, 3, 4, 0, HALF)
-        diff_rows(1, 1, 0, 4, HALF, HALF + P)
+        diff_rows(1, 1, 0, 4, HALF, W)
         for f in range(D // P):
             acc = bank(4 + f % 4)
             for i in range(G):
@@ -404,17 +404,14 @@ def tile_centredequilibriumpropupdate_w4_kernel(
         d_scale(1, 1, 0, HALF)
         d_scale(0, 1, HALF, W)
         d_quant(1, 1, 0, HALF)
-        d_scale(1, 1, HALF, HALF + P)
+        d_scale(1, 1, HALF, W)
         d_quant(0, 1, HALF, W)
-        diff_rows(1, 1, 0, 4, HALF + P, W)
-        d_quant(1, 1, HALF, HALF + P)
-        d_scale(1, 1, HALF + P, W)
-        d_quant(1, 1, HALF + P, W)
+        d_quant(1, 1, HALF, W)
 
         copies = (nc.scalar.copy, nc.vector.tensor_copy)
         free = list(range(8))
         chunks = []
-        for lo, hi in ((W, W + HALF), (W + HALF, W + HALF + P), (W + HALF + P, H)):
+        for lo, hi in ((W, W + HALF), (W + HALF, H)):
             nf = W // (hi - lo)
             chunks.append((lo, hi, nf, [bank(free.pop(0)) for j in range(D // P // nf)]))
 
@@ -424,10 +421,9 @@ def tile_centredequilibriumpropupdate_w4_kernel(
                 s2_pass(acc[:, m * (hi - lo) : (m + 1) * (hi - lo)], f0 + m, i, lo, hi, first, last)
 
         for n, (lo, hi, nf, accs) in enumerate(chunks):
-            if n < 2:
-                for mlo, mhi, mnf, maccs in chunks[n : 2 * n + 1]:
-                    for j, acc in enumerate(maccs):
-                        bank_passes(acc, mnf * j, mnf, 0, mlo, mhi)
             for j, acc in enumerate(accs):
+                if j % 2 == 0:
+                    bank_passes(acc, nf * j, nf, 0, lo, hi)
+                    bank_passes(accs[j + 1], nf * (j + 1), nf, 0, lo, hi)
                 bank_passes(acc, nf * j, nf, 1, lo, hi)
-                put_out(acc, copies[j % 2 if n else 0], nf * j, nf, lo, hi)
+                put_out(acc, copies[(j + 1) % 2 if n else j // 3], nf * j, nf, lo, hi)

@@ -391,11 +391,10 @@ def tile_centredequilibriumpropupdate_w4_kernel(
         d_scale(0, 1, 0, HALF)
         for b in range(T, 2 * T - 1):
             unit(b, 1)
-        diff_rows(1, 1, 0, 3, 0, HALF)
-        d_quant(0, 1, 0, HALF)
+        diff_rows(1, 1, 0, 3, 0, W)
         unit(2 * T - 1, 1)
-        diff_rows(1, 1, 3, 4, 0, HALF)
-        diff_rows(1, 1, 0, 4, HALF, W)
+        diff_rows(1, 1, 3, 4, 0, W)
+        d_quant(0, 1, 0, HALF)
         for f in range(D // P):
             acc = bank(4 + f % 4)
             for i in range(G):

@@ -54,7 +54,6 @@ def tile_centredequilibriumpropupdate_w4_kernel(
         rf = keep.tile([P, G, T], F32, name="rf", align_bytes=64)
         gs = keep.tile([P, G, T], F32, name="gs", align_bytes=64)
         ident = keep.tile([P, P], F32, name="ident", align_bytes=64)
-        warm = keep.tile([P, 2], F32, name="warm", align_bytes=64)
         qc = keep.tile([P, G * T // 2, 8, P], U32, name="qc", align_bytes=64)
         qs = keep.tile([P, G * T // 2, 8, P], U8, name="qs", align_bytes=64)
         rc = [keep.tile([P, D], U32, name="rc%d" % i, align_bytes=64) for i in range(G)]
@@ -75,8 +74,6 @@ def tile_centredequilibriumpropupdate_w4_kernel(
             nc.sync.dma_start(out=w1t[c][:], in_=w1v[:, :, 2 * W * c : 2 * W * (c + 1)])
 
         nc.vector.memset(wsc[:].rearrange("p k n -> p (k n)").bitcast(I32), 0)
-        nc.vector.memset(warm[:], 0.0)
-        nc.scalar.activation(out=warm[:, 1:2], in_=warm[:, 0:1], func=TANH)
         make_identity(nc, ident[:])
 
         load_x(*GROUPS[0])

@@ -23,7 +23,8 @@ G = 2
 T = 4
 W = 512
 HALF = 256
-GROUPS = ((0, 1), (1, 1), (2, 2), (4, 2), (6, 2))
+X_LOADS = ((0, 1), (1, 1), (2, 2), (4, 2), (6, 2))
+E_LOADS = ((0, 2), (2, 2), (4, 4))
 
 
 def tile_centredequilibriumpropupdate_w4_kernel(
@@ -39,19 +40,18 @@ def tile_centredequilibriumpropupdate_w4_kernel(
         def bank(i):
             return psum.tile([P, W], F32, name="bank%d" % i)
 
-        xt = {b0: keep.tile([P, n, D], BF16, name="xt%d" % b0, align_bytes=64) for b0, n in GROUPS}
-        xrow = {b0 + j: xt[b0][:, j, :] for b0, n in GROUPS for j in range(n)}
-        eb = [keep.tile([P, T, O], U8, name="eb%d" % i, align_bytes=64) for i in range(G)]
+        xt = {b0: keep.tile([P, n, D], BF16, name="xt%d" % b0, align_bytes=64) for b0, n in X_LOADS}
+        xrow = {b0 + j: xt[b0][:, j, :] for b0, n in X_LOADS for j in range(n)}
+        eb = {b0: keep.tile([P, n * O], U8, name="eb%d" % b0, align_bytes=64) for b0, n in E_LOADS}
+        epair = {b0 + j: eb[b0][:, j * O : (j + 2) * O] for b0, n in E_LOADS for j in range(0, n, 2)}
         est = keep.tile([P, T], F32, name="est", align_bytes=64)
-        esp = keep.tile([P, 2, O], F32, name="esp", align_bytes=64)
         pt = keep.tile([P, 2, T], BF16, name="pt", align_bytes=64)
-        pfull = keep.tile([P, 2, P, T], BF16, name="pfull", align_bytes=64)
         w1t = [keep.tile([P, 2, 2 * W], U8, name="w1t%d" % c, align_bytes=64) for c in range(2)]
         w2t = keep.tile([P, 2 * H], U8, name="w2t", align_bytes=64)
         wsc = keep.tile([P, 3, H], U8, name="wsc", align_bytes=64)
         rb = keep.tile([P, G, T], BF16, name="rb", align_bytes=64)
-        gb = keep.tile([P, G, T], BF16, name="gb", align_bytes=64)
         rf = keep.tile([P, G, T], F32, name="rf", align_bytes=64)
+        gb = keep.tile([P, G, T], BF16, name="gb", align_bytes=64)
         gs = keep.tile([P, G, T], F32, name="gs", align_bytes=64)
         ident = keep.tile([P, P], F32, name="ident", align_bytes=64)
         qc = keep.tile([P, G * T // 2, 8, P], U32, name="qc", align_bytes=64)
@@ -64,40 +64,43 @@ def tile_centredequilibriumpropupdate_w4_kernel(
         xw = [keep.tile([P, D, T], BF16, name="xw%d" % i, align_bytes=64) for i in range(G)]
 
         xv = x.rearrange("(g p t) d -> g p t d", g=G, p=P, t=T)
-        ev = e_bytes.rearrange("(g p t) o -> g p t o", g=G, p=P, t=T)
+        ev = e_bytes.rearrange("(g p t) o -> g p (t o)", g=G, p=P, t=T)
         w1v = w1_words.rearrange("g p w -> p g w")
 
         def load_x(b0, n):
             nc.sync.dma_start(out=xt[b0][:], in_=xv[b0 // T, :, b0 % T : b0 % T + n, :])
+
+        def load_e(b0, n):
+            nc.sync.dma_start(out=eb[b0][:], in_=ev[b0 // T, :, b0 % T * O : (b0 % T + n) * O])
 
         def load_w1(c):
             nc.sync.dma_start(out=w1t[c][:], in_=w1v[:, :, 2 * W * c : 2 * W * (c + 1)])
 
         nc.vector.memset(wsc[:].rearrange("p k n -> p (k n)").bitcast(I32), 0)
         make_identity(nc, ident[:])
-
-        load_x(*GROUPS[0])
+        load_x(*X_LOADS[0])
         nc.sync.dma_start(out=pt[:], in_=p.rearrange("(k q t) -> q k t", k=2, q=P, t=T))
-        nc.sync.dma_start(out=rb[:], in_=r.rearrange("(g p t) -> p g t", g=G, p=P, t=T))
+        load_e(*E_LOADS[0])
+        load_x(*X_LOADS[1])
         nc.sync.dma_start(out=est[:], in_=e_scale.rearrange("o (q t) -> q (o t)", t=T))
-        load_x(*GROUPS[1])
-        nc.sync.dma_start(out=eb[0][:], in_=ev[0])
-        load_w1(0)
-        load_x(*GROUPS[2])
+        load_x(*X_LOADS[2])
+        nc.sync.dma_start(out=rb[:], in_=r.rearrange("(g p t) -> p g t", g=G, p=P, t=T))
         for q in range(4):
             nc.sync.dma_start(
                 out=wsc[32 * q : 32 * q + 4, 0:2, :].bitcast(I32),
                 in_=w1_scales[:, 4 * q : 4 * q + 4, :].rearrange("g q n -> q g n").bitcast(I32),
             )
-        nc.sync.dma_start(out=eb[1][:], in_=ev[1])
+        load_w1(0)
+        load_e(*E_LOADS[1])
         nc.sync.dma_start(out=w2t[:], in_=w2_words[0])
         for q in range(4):
             nc.sync.dma_start(
                 out=wsc[32 * q : 32 * q + 4, 2, :].bitcast(I32), in_=w2_scales[0, 4 * q : 4 * q + 4, :].bitcast(I32)
             )
-        load_x(*GROUPS[3])
+        load_e(*E_LOADS[2])
+        load_x(*X_LOADS[3])
         load_w1(1)
-        load_x(*GROUPS[4])
+        load_x(*X_LOADS[4])
         nc.sync.dma_start(out=gb[:], in_=g.rearrange("(g p t) -> p g t", g=G, p=P, t=T))
 
         ew = {}
@@ -105,16 +108,11 @@ def tile_centredequilibriumpropupdate_w4_kernel(
         ebank = {}
         qin = {}
 
-        def e_mul(b0, n):
-            tile = work.tile([P, n * O], BF16, name="ew", bufs=4, align_bytes=64)
-            nc.vector.tensor_tensor(
-                out=tile[:],
-                in0=eb[b0 // T][:, b0 % T : b0 % T + n, :].rearrange("p j o -> p (j o)").bitcast(E4M3),
-                in1=esp[:, 0:n, :].rearrange("p j o -> p (j o)"),
-                op=MULT,
+        def e_widen(b0):
+            ew[b0] = work.tile([P, 2, O], BF16, name="ew", bufs=4, align_bytes=64)
+            nc.scalar.activation(
+                out=ew[b0][:].rearrange("p j o -> p (j o)"), in_=epair[b0].bitcast(E4M3), func=COPY, scale=0.5
             )
-            for j in range(n):
-                ew[b0 + j] = tile[:, j * O : (j + 1) * O]
 
         def x_turn(b, i):
             xbank[b] = bank(i)
@@ -124,12 +122,12 @@ def tile_centredequilibriumpropupdate_w4_kernel(
                     lo = P * (2 * u + k)
                     nc.tensor.transpose(xbank[b][:, lo : lo + P], words[:, 256 * k + u : 256 * (k + 1) : 2], ident[:])
 
-        def e_turn(b0, n, i):
+        def e_turn(b0, i):
             ebank[b0] = bank(i)
-            for j in range(n):
-                words = ew[b0 + j].bitcast(F32)
+            for j in range(2):
+                words = ew[b0][:, j, :].bitcast(F32)
                 for u in range(2):
-                    lo = P * (2 * j + u)
+                    lo = P * (2 * u + j)
                     nc.tensor.transpose(ebank[b0][:, lo : lo + P], words[:, u:256:2], ident[:])
 
         def slot(b, k):
@@ -138,18 +136,20 @@ def tile_centredequilibriumpropupdate_w4_kernel(
         def new_qin(b0):
             qin[b0 // 2] = work.tile([P, 8, P * T], BF16, name="qin", bufs=2, align_bytes=64)
 
-        def e_copy(b0):
-            nc.scalar.copy(
-                out=qin[b0 // 2][:, 4:6, :].bitcast(F32).rearrange("p j (n u) -> p j n u", u=2),
-                in_=ebank[b0][:].rearrange("p (j u n) -> p j n u", j=2, u=2),
-            )
-
         def x_mul(b):
             lo = slot(b, 0)
             nc.vector.tensor_tensor(
-                out=qin[b // 2][:, lo : lo + 2, :].rearrange("p k (n u e) -> p (k n) u e", u=2, e=2),
-                in0=xbank[b][:].bitcast(BF16).rearrange("p (u m e) -> p m u e", u=2, e=2),
-                in1=pfull[:].rearrange("p k n (u e) -> p (k n) u e", u=2),
+                out=qin[b // 2][:, lo : lo + 2, :].rearrange("p k (n u e) -> p k n u e", u=2, e=2),
+                in0=xbank[b][:].bitcast(BF16).rearrange("p (u k n e) -> p k n u e", u=2, k=2, e=2),
+                in1=pt[:].rearrange("p k (u e) -> p k u e", u=2).unsqueeze(2).to_broadcast([P, 2, P, 2, 2]),
+                op=MULT,
+            )
+
+        def e_mul(b0):
+            nc.vector.tensor_tensor(
+                out=qin[b0 // 2][:, 4:6, :].rearrange("p j (n u e) -> p (j n) u e", u=2, e=2),
+                in0=ebank[b0][:].bitcast(BF16).rearrange("p (u m e) -> p m u e", u=2, e=2),
+                in1=est[:].rearrange("p (u e) -> p u e", u=2).unsqueeze(1).to_broadcast([P, 2 * P, 2, 2]),
                 op=MULT,
             )
 
@@ -186,73 +186,80 @@ def tile_centredequilibriumpropupdate_w4_kernel(
 
         ub = {}
         hid = {}
+        turn = [0]
 
-        def f_pass(b, c, s):
-            nc.tensor.matmul_mx(
-                out=ub[b, c, s][:],
-                lhsT=qc[:, b // 2, slot(b, 2 + s), :].bitcast(FP8X4),
-                lhsT_scale=qs[:, b // 2, slot(b, 2 + s), :],
-                rhs=w2t[:, 2 * W * c : 2 * W * (c + 1)].bitcast(FP4X4),
-                rhs_scale=wsc[:, 2, c * W : (c + 1) * W],
-                start=False,
-                stop=True,
-            )
+        def next_bank(count):
+            turn[0] = (turn[0] + 1) % count
+            return bank(turn[0])
 
-        def tanh(b, c, s):
-            i, t = divmod(b, T)
-            if (i, c, s) not in hid:
-                hid[i, c, s] = work.tile([P, T, W], F32, name="hid%d" % s, bufs=4, align_bytes=64)
-            nc.scalar.activation(out=hid[i, c, s][:, t, :], in_=ub[b, c, s][:], func=TANH)
-
-        def a_passes(b, c, s):
-            ub[b, c, s] = bank(len(ub) % 4)
+        def a_passes(dst, b, lo, hi):
+            c = lo // W
             for k in range(2):
                 nc.tensor.matmul_mx(
-                    out=ub[b, c, s][:],
+                    out=dst,
                     lhsT=qc[:, b // 2, slot(b, k), :].bitcast(FP8X4),
                     lhsT_scale=qs[:, b // 2, slot(b, k), :],
-                    rhs=w1t[c][:, k, :].bitcast(FP4X4),
-                    rhs_scale=wsc[:, k, c * W : (c + 1) * W],
+                    rhs=w1t[c][:, k, 2 * (lo - c * W) : 2 * (hi - c * W)].bitcast(FP4X4),
+                    rhs_scale=wsc[:, k, lo:hi],
                     start=(k == 0),
                     stop=False,
                 )
 
-        def unit(b, c):
+        def f_pass(dst, b, s, lo, hi):
+            nc.tensor.matmul_mx(
+                out=dst,
+                lhsT=qc[:, b // 2, slot(b, 2 + s), :].bitcast(FP8X4),
+                lhsT_scale=qs[:, b // 2, slot(b, 2 + s), :],
+                rhs=w2t[:, 2 * lo : 2 * hi].bitcast(FP4X4),
+                rhs_scale=wsc[:, 2, lo:hi],
+                start=False,
+                stop=True,
+            )
+
+        def hid_tile(i, lo, hi):
+            if (i, lo) not in hid:
+                hid[i, lo] = keep.tile([P, T, 2, hi - lo], F32, name="hid%d_%d" % (i, lo), align_bytes=64)
+            return hid[i, lo]
+
+        def tanh(src, b, s, lo):
+            nc.scalar.activation(out=hid_tile(b // T, lo, lo + W)[:, b % T, s, :], in_=src, func=TANH)
+
+        def unit(b, c, count):
             for s in range(2):
-                a_passes(b, c, s)
-                f_pass(b, c, s)
-                tanh(b, c, s)
+                acc = next_bank(count)
+                a_passes(acc[:], b, c * W, (c + 1) * W)
+                f_pass(acc[:], b, s, c * W, (c + 1) * W)
+                tanh(acc[:], b, s, c * W)
+
+        def narrow_unit(b, lo):
+            acc = next_bank(8)
+            for s in range(2):
+                a_passes(acc[:, s * HALF : (s + 1) * HALF], b, lo, lo + HALF)
+                f_pass(acc[:, s * HALF : (s + 1) * HALF], b, s, lo, lo + HALF)
+            nc.scalar.activation(
+                out=hid_tile(b // T, lo, lo + HALF)[:, b % T, :, :].rearrange("p s n -> p (s n)"), in_=acc[:], func=TANH
+            )
 
         dg = {}
 
-        def diff(i, c, lo, hi):
-            nc.vector.tensor_tensor(
-                out=hid[i, c, 0][:, :, lo:hi], in0=hid[i, c, 0][:, :, lo:hi], in1=hid[i, c, 1][:, :, lo:hi], op=SUB
-            )
+        def diff(i, lo, t0, t1):
+            tile = hid[i, lo]
+            nc.vector.tensor_tensor(out=tile[:, t0:t1, 0, :], in0=tile[:, t0:t1, 0, :], in1=tile[:, t0:t1, 1, :], op=SUB)
 
-        def diff_rows(i, c, t0, t1, lo, hi):
+        def d_scale(i, base, lo, hi):
+            dg[i, lo] = work.tile([P, hi - lo, T], BF16, name="dg", bufs=3, align_bytes=64)
             nc.vector.tensor_tensor(
-                out=hid[i, c, 0][:, t0:t1, lo:hi],
-                in0=hid[i, c, 0][:, t0:t1, lo:hi],
-                in1=hid[i, c, 1][:, t0:t1, lo:hi],
-                op=SUB,
-            )
-
-        def d_scale(i, c, lo, hi):
-            if (i, c) not in dg:
-                dg[i, c] = work.tile([P, W, T], BF16, name="dg", bufs=3, align_bytes=64)
-            nc.vector.tensor_tensor(
-                out=dg[i, c][:, lo:hi, :].rearrange("p (n j) t -> p n t j", j=4),
-                in0=hid[i, c, 0][:, :, lo:hi].rearrange("p t (n j) -> p n t j", j=4),
+                out=dg[i, lo][:].rearrange("p (n j) t -> p n t j", j=4),
+                in0=hid[i, base][:, :, 0, lo - base : hi - base].rearrange("p t (n j) -> p n t j", j=4),
                 in1=gs[:, i, :].unsqueeze(1).unsqueeze(3).to_broadcast([P, (hi - lo) // 4, T, 4]),
                 op=MULT,
             )
 
-        def d_quant(i, c, lo, hi):
+        def d_quant(i, lo, hi):
             nc.vector.quantize_mx(
-                out=dc[i][:, c * W + lo : c * W + hi].bitcast(FP8X4),
-                scales=ds[i][:, c * W + lo : c * W + hi],
-                in_=dg[i, c][:, lo:hi, :].rearrange("p n t -> p (n t)"),
+                out=dc[i][:, lo:hi].bitcast(FP8X4),
+                scales=ds[i][:, lo:hi],
+                in_=dg[i, lo][:].rearrange("p n t -> p (n t)"),
             )
 
         def s2_pass(dst, f, i, lo, hi, start, stop):
@@ -267,159 +274,154 @@ def tile_centredequilibriumpropupdate_w4_kernel(
             )
 
         def put_out(acc, copy, f0, nf, lo, hi):
-            res = work.tile([P, W], F32, name="res", bufs=10, align_bytes=64)
+            res = work.tile([P, W], F32, name="res", bufs=8, align_bytes=64)
             copy(out=res[:], in_=acc[:])
             nc.sync.dma_start(
                 out=out[f0 * P : (f0 + nf) * P, lo:hi].rearrange("(j p) n -> p j n", p=P),
                 in_=res[:].rearrange("p (j n) -> p j n", j=nf),
             )
 
+        def bank_passes(acc, f0, i, lo):
+            for m in range(2):
+                first, last = (i, m) == (0, 0), (i, m) == (G - 1, 1)
+                s2_pass(acc[:, m * HALF : (m + 1) * HALF], f0 + m, i, lo, lo + HALF, first, last)
+
         pieces = [(i, q * HALF, (q + 1) * HALF) for i in range(G) for q in range(D // HALF)]
 
         def xr_piece():
             r_weave(*pieces.pop(0), nc.scalar.copy)
 
-        nc.vector.tensor_copy(out=pfull[:], in_=pt[:].unsqueeze(2).to_broadcast([P, 2, P, T]))
-        nc.vector.tensor_copy(out=rf[:], in_=rb[:])
-        r_mul(0)
-        x_turn(0, 4)
-        sbank = bank(7)
-        for t in range(T):
-            nc.tensor.transpose(sbank[:, t * P : (t + 1) * P], est[:, t : t + 1].to_broadcast([P, P]), ident[:])
-        for j in range(2):
-            nc.scalar.activation(
-                out=esp[:, j, :].rearrange("p (n t) -> p n t", t=T),
-                in_=sbank[:].rearrange("p (t n) -> p n t", t=T),
-                func=COPY,
-                scale=0.5,
-            )
-        x_turn(1, 5)
-        new_qin(0)
-        x_mul(0)
-        r_mul(1)
-        quant(0, 0, 2)
-        e_mul(0, 1)
-        e_mul(1, 1)
-        x_mul(1)
-        r_mul_s(2)
-        r_mul_s(3)
-        for s in range(2):
-            a_passes(0, 0, s)
-        e_turn(0, 2, 6)
-        x_turn(2, 4)
-        xr_piece()
-        e_copy(0)
-        xr_piece()
-        e_mul(2, 2)
-        quant(0, 2, 4)
-        e_mul(4, 2)
-        new_qin(2)
-        x_mul(2)
-        e_neg(0)
-        r_mul(4)
-        quant(0, 4, 8)
-        for s in range(2):
-            a_passes(1, 0, s)
-        e_turn(2, 2, 7)
-        x_turn(3, 5)
-        e_copy(2)
-        xr_piece()
-        for b in range(2):
-            for s in range(2):
-                f_pass(b, 0, s)
-                tanh(b, 0, s)
-        x_mul(3)
-        e_neg(2)
-        r_mul(5)
-        quant(2, 0, 8)
-        nc.scalar.activation(
-            out=gs[:].rearrange("p g t -> p (g t)"), in_=gb[:].rearrange("p g t -> p (g t)"), func=COPY, scale=1.0 / 32.0
-        )
 
-        def first_turn(b0):
-            e_turn(b0, 2, 6 + b0 // 2 % 2)
-            x_turn(b0, 4)
-            new_qin(b0)
-            e_copy(b0)
-
-        e_mul(6, 2)
-        first_turn(4)
-        x_mul(4)
-        r_mul(6)
-        e_neg(4)
-        r_mul(7)
-        unit(0, 1)
-        xr_piece()
-        x_turn(5, 5)
-        x_mul(5)
-        diff_rows(0, 0, 0, 2, 0, W)
-        quant(4, 0, 8)
-        unit(2, 0)
-        first_turn(6)
-        x_mul(6)
-        r_quant(0)
-        e_neg(6)
-        unit(3, 0)
-        xr_piece()
-        x_turn(7, 5)
-        x_mul(7)
-        diff_rows(0, 0, 2, 4, 0, W)
-        quant(6, 0, 8)
-        unit(1, 1)
-        xr_piece()
-        d_scale(0, 0, 0, W)
-        r_weave(1, W + HALF, D, nc.vector.tensor_copy)
-        d_quant(0, 0, 0, W)
-        diff_rows(0, 1, 0, 2, 0, W)
-        for b in range(T, 2 * T):
-            unit(b, 0)
-            if b % 2 == 0:
-                lo = W + (b - T) // 2 * P
-                r_weave(1, lo, lo + P, nc.scalar.copy)
-        diff_rows(1, 0, 0, 2, 0, W)
-        r_quant(1)
-        diff_rows(1, 0, 2, 4, 0, W)
-        unit(2, 1)
-        unit(3, 1)
-        diff_rows(0, 1, 2, 3, 0, W)
-        d_scale(1, 0, 0, W)
-        diff_rows(0, 1, 3, 4, 0, W)
-        d_quant(1, 0, 0, W)
-        d_scale(0, 1, 0, HALF)
-        for b in range(T, 2 * T - 1):
-            unit(b, 1)
-        diff_rows(1, 1, 0, 3, 0, W)
-        unit(2 * T - 1, 1)
-        diff_rows(1, 1, 3, 4, 0, W)
-        d_quant(0, 1, 0, HALF)
-        for f in range(D // P):
-            acc = bank(4 + f % 4)
+        def wide_out(f):
+            acc = next_bank(8)
             for i in range(G):
                 s2_pass(acc[:], f, i, 0, W, i == 0, i == G - 1)
             put_out(acc, nc.scalar.copy, f, 1, 0, W)
-        d_scale(1, 1, 0, HALF)
-        d_scale(0, 1, HALF, W)
-        d_quant(1, 1, 0, HALF)
-        d_scale(1, 1, HALF, W)
-        d_quant(0, 1, HALF, W)
-        d_quant(1, 1, HALF, W)
 
-        copies = (nc.scalar.copy, nc.vector.tensor_copy)
-        free = list(range(8))
-        chunks = []
-        for lo, hi in ((W, W + HALF), (W + HALF, H)):
-            nf = W // (hi - lo)
-            chunks.append((lo, hi, nf, [bank(free.pop(0)) for j in range(D // P // nf)]))
-
-        def bank_passes(acc, f0, nf, i, lo, hi):
-            for m in range(nf):
-                first, last = (i, m) == (0, 0), (i, m) == (G - 1, nf - 1)
-                s2_pass(acc[:, m * (hi - lo) : (m + 1) * (hi - lo)], f0 + m, i, lo, hi, first, last)
-
-        for n, (lo, hi, nf, accs) in enumerate(chunks):
-            for j, acc in enumerate(accs):
-                if j % 2 == 0:
-                    bank_passes(acc, nf * j, nf, 0, lo, hi)
-                    bank_passes(accs[j + 1], nf * (j + 1), nf, 0, lo, hi)
-                bank_passes(acc, nf * j, nf, 1, lo, hi)
-                put_out(acc, copies[(j + 1) % 2 if n else j // 3], nf * j, nf, lo, hi)
+        x_turn(0, 4)
+        e_widen(0)
+        x_turn(1, 5)
+        new_qin(0)
+        x_mul(0)
+        quant(0, 0, 2)
+        e_turn(0, 6)
+        nc.vector.tensor_copy(out=rf[:], in_=rb[:])
+        r_mul_s(0)
+        x_turn(2, 7)
+        x_turn(3, 3)
+        first = [bank(j) for j in range(2)]
+        for s in range(2):
+            a_passes(first[s][:], 0, 0, W)
+        x_mul(1)
+        e_mul(0)
+        quant(0, 2, 4)
+        e_neg(0)
+        r_mul(2)
+        quant(0, 4, 8)
+        e_widen(2)
+        r_mul_s(1)
+        e_turn(2, 4)
+        first.extend([bank(2), bank(5)])
+        for s in range(2):
+            a_passes(first[2 + s][:], 1, 0, W)
+        new_qin(2)
+        x_mul(2)
+        r_mul(3)
+        x_mul(3)
+        e_mul(2)
+        e_widen(4)
+        xr_piece()
+        r_mul(4)
+        e_neg(2)
+        r_mul(5)
+        quant(2, 0, 8)
+        for j in range(4):
+            f_pass(first[j][:], j // 2, j % 2, 0, W)
+            tanh(first[j][:], j // 2, j % 2, 0)
+        x_turn(4, 6)
+        x_turn(5, 7)
+        e_turn(4, 4)
+        e_widen(6)
+        xr_piece()
+        turn[0] = 3
+        new_qin(4)
+        x_mul(4)
+        x_mul(5)
+        e_mul(4)
+        r_mul(6)
+        e_neg(4)
+        r_mul(7)
+        quant(4, 0, 8)
+        unit(2, 0, 4)
+        xr_piece()
+        unit(3, 0, 4)
+        xr_piece()
+        x_turn(6, 5)
+        x_turn(7, 6)
+        e_turn(6, 7)
+        nc.scalar.activation(
+            out=gs[:].rearrange("p g t -> p (g t)"), in_=gb[:].rearrange("p g t -> p (g t)"), func=COPY, scale=1.0 / 32.0
+        )
+        diff(0, 0, 0, 2)
+        new_qin(6)
+        x_mul(6)
+        x_mul(7)
+        e_mul(6)
+        diff(0, 0, 2, 3)
+        e_neg(6)
+        diff(0, 0, 3, 4)
+        quant(6, 0, 8)
+        unit(4, 0, 4)
+        xr_piece()
+        unit(5, 0, 4)
+        xr_piece()
+        unit(0, 1, 8)
+        d_scale(0, 0, 0, W)
+        diff(1, 0, 0, 2)
+        d_quant(0, 0, W)
+        r_quant(0)
+        unit(6, 0, 8)
+        unit(7, 0, 8)
+        diff(0, W, 0, 1)
+        diff(1, 0, 2, 4)
+        xr_piece()
+        unit(1, 1, 8)
+        xr_piece()
+        d_scale(1, 0, 0, W)
+        diff(0, W, 1, 2)
+        r_quant(1)
+        d_quant(1, 0, W)
+        unit(2, 1, 8)
+        unit(3, 1, 8)
+        diff(0, W, 2, 4)
+        for b in range(T, 2 * T):
+            narrow_unit(b, W)
+        diff(1, W, 0, 2)
+        d_scale(0, W, W, H)
+        diff(1, W, 2, 4)
+        d_quant(0, W, H)
+        d_scale(1, W, W, W + HALF)
+        for f in range(6):
+            wide_out(f)
+        last = W + HALF
+        for b in range(T, 2 * T):
+            narrow_unit(b, last)
+        diff(1, last, 0, 2)
+        d_quant(1, W, W + HALF)
+        diff(1, last, 2, 4)
+        d_scale(1, last, last, H)
+        d_quant(1, last, H)
+        for f in range(6, 8):
+            wide_out(f)
+        for j in range(4):
+            acc = next_bank(8)
+            for i in range(G):
+                bank_passes(acc, 2 * j, i, W)
+            put_out(acc, nc.scalar.copy, 2 * j, 2, W, last)
+        accs = [next_bank(8) for j in range(4)]
+        for j in range(4):
+            if j % 2 == 0:
+                bank_passes(accs[j], 2 * j, 0, last)
+                bank_passes(accs[j + 1], 2 * j + 2, 0, last)
+            bank_passes(accs[j], 2 * j, 1, last)
+            put_out(accs[j], (nc.scalar.copy, nc.vector.tensor_copy)[j % 2], 2 * j, 2, last, H)

@@ -12,6 +12,7 @@ E4M3 = mybir.dt.float8_e4m3fn
 FP8X4 = mybir.dt.float8_e4m3fn_x4
 FP4X4 = mybir.dt.float4_e2m1fn_x4
 MULT = mybir.AluOpType.mult
+ADD = mybir.AluOpType.add
 SUB = mybir.AluOpType.subtract
 TANH = mybir.ActivationFunctionType.Tanh
 COPY = mybir.ActivationFunctionType.Copy
@@ -25,6 +26,7 @@ W = 512
 HALF = 256
 X_LOADS = ((0, 1), (1, 1), (2, 2), (4, 2), (6, 2))
 E_LOADS = ((0, 2), (2, 2), (4, 4))
+CUT = 384
 
 
 def tile_centredequilibriumpropupdate_w4_kernel(
@@ -61,7 +63,7 @@ def tile_centredequilibriumpropupdate_w4_kernel(
         dc = [keep.tile([P, H], U32, name="dc%d" % i, align_bytes=64) for i in range(G)]
         ds = [keep.tile([P, H], U8, name="ds%d" % i, align_bytes=64) for i in range(G)]
         xm = [keep.tile([P, T, D], BF16, name="xm%d" % i, align_bytes=64) for i in range(G)]
-        xw = [keep.tile([P, D, T], BF16, name="xw%d" % i, align_bytes=64) for i in range(G)]
+        xw = [keep.tile([P, D, T], BF16, name="xw%d" % i, tag="xw%d" % i, align_bytes=64) for i in range(G)]
 
         xv = x.rearrange("(g p t) d -> g p t d", g=G, p=P, t=T)
         ev = e_bytes.rearrange("(g p t) o -> g p (t o)", g=G, p=P, t=T)
@@ -81,17 +83,17 @@ def tile_centredequilibriumpropupdate_w4_kernel(
         load_x(*X_LOADS[0])
         nc.sync.dma_start(out=pt[:], in_=p.rearrange("(k q t) -> q k t", k=2, q=P, t=T))
         load_e(*E_LOADS[0])
+        nc.sync.dma_start(out=rb[:], in_=r.rearrange("(g p t) -> p g t", g=G, p=P, t=T))
         load_x(*X_LOADS[1])
         nc.sync.dma_start(out=est[:], in_=e_scale.rearrange("o (q t) -> q (o t)", t=T))
         load_x(*X_LOADS[2])
-        nc.sync.dma_start(out=rb[:], in_=r.rearrange("(g p t) -> p g t", g=G, p=P, t=T))
+        load_e(*E_LOADS[1])
         for q in range(4):
             nc.sync.dma_start(
                 out=wsc[32 * q : 32 * q + 4, 0:2, :].bitcast(I32),
                 in_=w1_scales[:, 4 * q : 4 * q + 4, :].rearrange("g q n -> q g n").bitcast(I32),
             )
         load_w1(0)
-        load_e(*E_LOADS[1])
         nc.sync.dma_start(out=w2t[:], in_=w2_words[0])
         for q in range(4):
             nc.sync.dma_start(
@@ -99,9 +101,9 @@ def tile_centredequilibriumpropupdate_w4_kernel(
             )
         load_e(*E_LOADS[2])
         load_x(*X_LOADS[3])
+        nc.sync.dma_start(out=gb[:], in_=g.rearrange("(g p t) -> p g t", g=G, p=P, t=T))
         load_w1(1)
         load_x(*X_LOADS[4])
-        nc.sync.dma_start(out=gb[:], in_=g.rearrange("(g p t) -> p g t", g=G, p=P, t=T))
 
         ew = {}
         xbank = {}
@@ -134,7 +136,7 @@ def tile_centredequilibriumpropupdate_w4_kernel(
             return 2 * (b % 2) + k if k < 2 else 2 * k + b % 2
 
         def new_qin(b0):
-            qin[b0 // 2] = work.tile([P, 8, P * T], BF16, name="qin", bufs=2, align_bytes=64)
+            qin[b0 // 2] = keep.tile([P, 8, P * T], BF16, name="qin%d" % b0, tag="qin%d" % (b0 // 2 % 2), align_bytes=64)
 
         def x_mul(b):
             lo = slot(b, 0)
@@ -165,9 +167,21 @@ def tile_centredequilibriumpropupdate_w4_kernel(
                 in_=qin[b0 // 2][:, lo:hi, :].rearrange("p k m -> p (k m)"),
             )
 
-        def r_mul(b):
+        def r_mul(b, lo=0, hi=D):
             i, t = divmod(b, T)
-            nc.vector.tensor_scalar(out=xm[i][:, t, :], in0=xrow[b], scalar1=rb[:, i, t : t + 1], scalar2=None, op0=MULT)
+            nc.vector.tensor_scalar(
+                out=xm[i][:, t, lo:hi], in0=xrow[b][:, lo:hi], scalar1=rb[:, i, t : t + 1], scalar2=None, op0=MULT
+            )
+
+        def g_weave(i, lo, hi):
+            nc.gpsimd.tensor_scalar(
+                out=xw[i][:, lo:hi, :],
+                in0=xm[i][:, :, lo:hi].rearrange("p t n -> p n t"),
+                scalar1=1.0,
+                scalar2=0.0,
+                op0=MULT,
+                op1=ADD,
+            )
 
         def r_mul_s(b):
             i, t = divmod(b, T)
@@ -218,7 +232,7 @@ def tile_centredequilibriumpropupdate_w4_kernel(
 
         def hid_tile(i, lo, hi):
             if (i, lo) not in hid:
-                hid[i, lo] = keep.tile([P, T, 2, hi - lo], F32, name="hid%d_%d" % (i, lo), align_bytes=64)
+                hid[i, lo] = keep.tile([P, T, 2, hi - lo], F32, name="hid%d_%d" % (i, lo), tag="hid%d_%d" % (i, lo), align_bytes=64)
             return hid[i, lo]
 
         def tanh(src, b, s, lo):
@@ -232,7 +246,7 @@ def tile_centredequilibriumpropupdate_w4_kernel(
                 tanh(acc[:], b, s, c * W)
 
         def narrow_unit(b, lo):
-            acc = next_bank(8)
+            acc = next_bank(7)
             for s in range(2):
                 a_passes(acc[:, s * HALF : (s + 1) * HALF], b, lo, lo + HALF)
                 f_pass(acc[:, s * HALF : (s + 1) * HALF], b, s, lo, lo + HALF)
@@ -242,16 +256,23 @@ def tile_centredequilibriumpropupdate_w4_kernel(
 
         dg = {}
 
-        def diff(i, lo, t0, t1):
+        dif = {}
+
+        def new_dif(i, lo, hi, tag):
+            dif[i, lo] = keep.tile([P, T, hi - lo], F32, name="dif%d_%d" % (i, lo), tag=tag, align_bytes=64)
+
+        def diff(i, lo, t0, t1, c0=0, c1=None, engine=nc.vector):
             tile = hid[i, lo]
-            nc.vector.tensor_tensor(out=tile[:, t0:t1, 0, :], in0=tile[:, t0:t1, 0, :], in1=tile[:, t0:t1, 1, :], op=SUB)
+            engine.tensor_tensor(
+                out=dif[i, lo][:, t0:t1, c0:c1], in0=tile[:, t0:t1, 0, c0:c1], in1=tile[:, t0:t1, 1, c0:c1], op=SUB
+            )
 
         def d_scale(i, base, lo, hi):
             dg[i, lo] = work.tile([P, hi - lo, T], BF16, name="dg", bufs=3, align_bytes=64)
             nc.vector.tensor_tensor(
                 out=dg[i, lo][:].rearrange("p (n j) t -> p n t j", j=4),
-                in0=hid[i, base][:, :, 0, lo - base : hi - base].rearrange("p t (n j) -> p n t j", j=4),
-                in1=gs[:, i, :].unsqueeze(1).unsqueeze(3).to_broadcast([P, (hi - lo) // 4, T, 4]),
+                in0=dif[i, base][:, :, lo - base : hi - base].rearrange("p t (n j) -> p n t j", j=4),
+                in1=gp[:, i * T : (i + 1) * T].unsqueeze(1).unsqueeze(3).to_broadcast([P, (hi - lo) // 4, T, 4]),
                 op=MULT,
             )
 
@@ -286,14 +307,9 @@ def tile_centredequilibriumpropupdate_w4_kernel(
                 first, last = (i, m) == (0, 0), (i, m) == (G - 1, 1)
                 s2_pass(acc[:, m * HALF : (m + 1) * HALF], f0 + m, i, lo, lo + HALF, first, last)
 
-        pieces = [(i, q * HALF, (q + 1) * HALF) for i in range(G) for q in range(D // HALF)]
-
-        def xr_piece():
-            r_weave(*pieces.pop(0), nc.scalar.copy)
-
 
         def wide_out(f):
-            acc = next_bank(8)
+            acc = next_bank(7)
             for i in range(G):
                 s2_pass(acc[:], f, i, 0, W, i == 0, i == G - 1)
             put_out(acc, nc.scalar.copy, f, 1, 0, W)
@@ -303,12 +319,14 @@ def tile_centredequilibriumpropupdate_w4_kernel(
         x_turn(1, 5)
         new_qin(0)
         x_mul(0)
+        nc.vector.tensor_copy(out=rf[:], in_=rb[:])
         quant(0, 0, 2)
         e_turn(0, 6)
-        nc.vector.tensor_copy(out=rf[:], in_=rb[:])
+        e_widen(2)
         r_mul_s(0)
         x_turn(2, 7)
         x_turn(3, 3)
+        e_turn(2, 4)
         first = [bank(j) for j in range(2)]
         for s in range(2):
             a_passes(first[s][:], 0, 0, W)
@@ -318,19 +336,18 @@ def tile_centredequilibriumpropupdate_w4_kernel(
         e_neg(0)
         r_mul(2)
         quant(0, 4, 8)
-        e_widen(2)
         r_mul_s(1)
-        e_turn(2, 4)
         first.extend([bank(2), bank(5)])
         for s in range(2):
             a_passes(first[2 + s][:], 1, 0, W)
         new_qin(2)
+        r_mul(3, 0, 720)
+        g_weave(0, 0, 336)
         x_mul(2)
-        r_mul(3)
         x_mul(3)
         e_mul(2)
         e_widen(4)
-        xr_piece()
+        r_weave(0, 336, 720, nc.scalar.copy)
         r_mul(4)
         e_neg(2)
         r_mul(5)
@@ -342,28 +359,33 @@ def tile_centredequilibriumpropupdate_w4_kernel(
         x_turn(5, 7)
         e_turn(4, 4)
         e_widen(6)
-        xr_piece()
+        nc.scalar.activation(
+            out=gs[:].rearrange("p g t -> p (g t)"), in_=gb[:].rearrange("p g t -> p (g t)"), func=COPY, scale=1.0 / 32.0
+        )
         turn[0] = 3
         new_qin(4)
+        r_mul(3, 720, D)
+        g_weave(0, 720, D)
         x_mul(4)
         x_mul(5)
         e_mul(4)
         r_mul(6)
         e_neg(4)
-        r_mul(7)
+        r_mul(7, 352, D)
         quant(4, 0, 8)
         unit(2, 0, 4)
-        xr_piece()
         unit(3, 0, 4)
-        xr_piece()
-        x_turn(6, 5)
-        x_turn(7, 6)
-        e_turn(6, 7)
-        nc.scalar.activation(
-            out=gs[:].rearrange("p g t -> p (g t)"), in_=gb[:].rearrange("p g t -> p (g t)"), func=COPY, scale=1.0 / 32.0
-        )
+        r_weave(1, 352, 688, nc.scalar.copy)
+        x_turn(6, 4)
+        x_turn(7, 5)
+        e_turn(6, 6)
+        gp = bank(7)
+        nc.tensor.matmul(gp[:, 0 : G * T], lhsT=ident[:], rhs=gs[:].rearrange("p g t -> p (g t)"), start=True, stop=True)
+        new_dif(0, 0, W, "dif0")
         diff(0, 0, 0, 2)
         new_qin(6)
+        r_mul(7, 0, 352)
+        g_weave(1, 0, 352)
         x_mul(6)
         x_mul(7)
         e_mul(6)
@@ -372,33 +394,34 @@ def tile_centredequilibriumpropupdate_w4_kernel(
         diff(0, 0, 3, 4)
         quant(6, 0, 8)
         unit(4, 0, 4)
-        xr_piece()
         unit(5, 0, 4)
-        xr_piece()
-        unit(0, 1, 8)
+        r_weave(1, 688, D, nc.scalar.copy)
+        unit(0, 1, 7)
+        new_dif(1, 0, W, "qin1")
+        diff(1, 0, 0, 2, 0, CUT, nc.gpsimd)
         d_scale(0, 0, 0, W)
-        diff(1, 0, 0, 2)
+        diff(1, 0, 0, 2, CUT)
         d_quant(0, 0, W)
-        r_quant(0)
-        unit(6, 0, 8)
-        unit(7, 0, 8)
-        diff(0, W, 0, 1)
-        diff(1, 0, 2, 4)
-        xr_piece()
-        unit(1, 1, 8)
-        xr_piece()
-        d_scale(1, 0, 0, W)
-        diff(0, W, 1, 2)
         r_quant(1)
+        unit(6, 0, 7)
+        unit(7, 0, 7)
+        diff(1, 0, 2, 4)
+        unit(1, 1, 7)
+        r_quant(0)
+        new_dif(0, W, H, "xw0")
+        diff(0, W, 0, 2, 0, CUT, nc.gpsimd)
+        d_scale(1, 0, 0, W)
+        diff(0, W, 0, 2, CUT)
         d_quant(1, 0, W)
-        unit(2, 1, 8)
-        unit(3, 1, 8)
+        unit(2, 1, 7)
+        unit(3, 1, 7)
         diff(0, W, 2, 4)
         for b in range(T, 2 * T):
             narrow_unit(b, W)
-        diff(1, W, 0, 2)
+        new_dif(1, W, W + HALF, "hid0_512")
+        diff(1, W, 0, 3, engine=nc.gpsimd)
         d_scale(0, W, W, H)
-        diff(1, W, 2, 4)
+        diff(1, W, 3, 4)
         d_quant(0, W, H)
         d_scale(1, W, W, W + HALF)
         for f in range(6):
@@ -406,19 +429,20 @@ def tile_centredequilibriumpropupdate_w4_kernel(
         last = W + HALF
         for b in range(T, 2 * T):
             narrow_unit(b, last)
-        diff(1, last, 0, 2)
+        new_dif(1, last, H, "xw1")
         d_quant(1, W, W + HALF)
-        diff(1, last, 2, 4)
+        diff(1, last, 0, 3)
+        diff(1, last, 3, 4)
         d_scale(1, last, last, H)
         d_quant(1, last, H)
         for f in range(6, 8):
             wide_out(f)
         for j in range(4):
-            acc = next_bank(8)
+            acc = next_bank(7)
             for i in range(G):
                 bank_passes(acc, 2 * j, i, W)
             put_out(acc, nc.scalar.copy, 2 * j, 2, W, last)
-        accs = [next_bank(8) for j in range(4)]
+        accs = [next_bank(7) for j in range(4)]
         for j in range(4):
             if j % 2 == 0:
                 bank_passes(accs[j], 2 * j, 0, last)

@@ -52,7 +52,6 @@ def tile_centredequilibriumpropupdate_w4_kernel(
         w2t = keep.tile([P, 2 * H], U8, name="w2t", align_bytes=64)
         wsc = keep.tile([P, 3, H], U8, name="wsc", align_bytes=64)
         rb = keep.tile([P, G, T], BF16, name="rb", align_bytes=64)
-        rf = keep.tile([P, G, T], F32, name="rf", align_bytes=64)
         gb = keep.tile([P, G, T], BF16, name="gb", align_bytes=64)
         gs = keep.tile([P, G, T], F32, name="gs", align_bytes=64)
         ident = keep.tile([P, P], F32, name="ident", align_bytes=64)
@@ -94,12 +93,12 @@ def tile_centredequilibriumpropupdate_w4_kernel(
                 in_=w1_scales[:, 4 * q : 4 * q + 4, :].rearrange("g q n -> q g n").bitcast(I32),
             )
         load_w1(0)
+        load_e(*E_LOADS[2])
         nc.sync.dma_start(out=w2t[:], in_=w2_words[0])
         for q in range(4):
             nc.sync.dma_start(
                 out=wsc[32 * q : 32 * q + 4, 2, :].bitcast(I32), in_=w2_scales[0, 4 * q : 4 * q + 4, :].bitcast(I32)
             )
-        load_e(*E_LOADS[2])
         load_x(*X_LOADS[3])
         nc.sync.dma_start(out=gb[:], in_=g.rearrange("(g p t) -> p g t", g=G, p=P, t=T))
         load_w1(1)
@@ -123,6 +122,20 @@ def tile_centredequilibriumpropupdate_w4_kernel(
                 for u in range(2):
                     lo = P * (2 * u + k)
                     nc.tensor.transpose(xbank[b][:, lo : lo + P], words[:, 256 * k + u : 256 * (k + 1) : 2], ident[:])
+
+        sorted_x = {}
+
+        def x_sort(b0):
+            sorted_x[b0] = work.tile([P, 2, W], F32, name="xs", bufs=1, align_bytes=64)
+            nc.scalar.copy(
+                out=sorted_x[b0][:].rearrange("p j (u m) -> p j m u", u=2),
+                in_=xt[b0][:].bitcast(F32).rearrange("p j (m u) -> p j m u", u=2),
+            )
+
+        def x_turn_sorted(b, i):
+            xbank[b] = bank(i)
+            for lo in range(0, W, P):
+                nc.tensor.transpose(xbank[b][:, lo : lo + P], sorted_x[b - b % 2][:, b % 2, lo : lo + P], ident[:])
 
         def e_turn(b0, i):
             ebank[b0] = bank(i)
@@ -182,10 +195,6 @@ def tile_centredequilibriumpropupdate_w4_kernel(
                 op0=MULT,
                 op1=ADD,
             )
-
-        def r_mul_s(b):
-            i, t = divmod(b, T)
-            nc.scalar.activation(out=xm[i][:, t, :], in_=xrow[b], func=COPY, scale=rf[:, i, t : t + 1])
 
         def weave(copy, dst, src):
             copy(out=dst.rearrange("p (n j) t -> p n t j", j=4), in_=src.rearrange("p t (n j) -> p n t j", j=4))
@@ -319,11 +328,10 @@ def tile_centredequilibriumpropupdate_w4_kernel(
         x_turn(1, 5)
         new_qin(0)
         x_mul(0)
-        nc.vector.tensor_copy(out=rf[:], in_=rb[:])
+        r_mul(0)
         quant(0, 0, 2)
         e_turn(0, 6)
         e_widen(2)
-        r_mul_s(0)
         x_turn(2, 7)
         x_turn(3, 3)
         e_turn(2, 4)
@@ -331,23 +339,25 @@ def tile_centredequilibriumpropupdate_w4_kernel(
         for s in range(2):
             a_passes(first[s][:], 0, 0, W)
         x_mul(1)
+        r_mul(1)
         e_mul(0)
         quant(0, 2, 4)
         e_neg(0)
         r_mul(2)
         quant(0, 4, 8)
-        r_mul_s(1)
+        e_widen(4)
+        e_widen(6)
         first.extend([bank(2), bank(5)])
         for s in range(2):
             a_passes(first[2 + s][:], 1, 0, W)
         new_qin(2)
-        r_mul(3, 0, 720)
-        g_weave(0, 0, 336)
+        r_mul(3, 0, 592)
+        g_weave(0, HALF, 592)
         x_mul(2)
         x_mul(3)
         e_mul(2)
-        e_widen(4)
-        r_weave(0, 336, 720, nc.scalar.copy)
+        x_sort(4)
+        r_weave(0, 0, HALF, nc.scalar.copy)
         r_mul(4)
         e_neg(2)
         r_mul(5)
@@ -355,60 +365,62 @@ def tile_centredequilibriumpropupdate_w4_kernel(
         for j in range(4):
             f_pass(first[j][:], j // 2, j % 2, 0, W)
             tanh(first[j][:], j // 2, j % 2, 0)
-        x_turn(4, 6)
-        x_turn(5, 7)
+        x_turn_sorted(4, 6)
+        x_turn_sorted(5, 7)
         e_turn(4, 4)
-        e_widen(6)
+        x_sort(6)
         nc.scalar.activation(
             out=gs[:].rearrange("p g t -> p (g t)"), in_=gb[:].rearrange("p g t -> p (g t)"), func=COPY, scale=1.0 / 32.0
         )
         turn[0] = 3
         new_qin(4)
-        r_mul(3, 720, D)
-        g_weave(0, 720, D)
+        r_mul(3, 592, D)
+        g_weave(0, 592, 944)
         x_mul(4)
         x_mul(5)
         e_mul(4)
         r_mul(6)
         e_neg(4)
-        r_mul(7, 352, D)
+        r_mul(7, 336, D)
         quant(4, 0, 8)
         unit(2, 0, 4)
         unit(3, 0, 4)
-        r_weave(1, 352, 688, nc.scalar.copy)
-        x_turn(6, 4)
-        x_turn(7, 5)
+        r_weave(0, 944, D, nc.scalar.copy)
+        x_turn_sorted(6, 4)
+        x_turn_sorted(7, 5)
         e_turn(6, 6)
         gp = bank(7)
         nc.tensor.matmul(gp[:, 0 : G * T], lhsT=ident[:], rhs=gs[:].rearrange("p g t -> p (g t)"), start=True, stop=True)
         new_dif(0, 0, W, "dif0")
-        diff(0, 0, 0, 2)
         new_qin(6)
-        r_mul(7, 0, 352)
-        g_weave(1, 0, 352)
+        r_mul(7, 0, 336)
+        g_weave(1, 0, 336)
+        r_weave(1, 336, W, nc.scalar.copy)
         x_mul(6)
         x_mul(7)
         e_mul(6)
-        diff(0, 0, 2, 3)
+        diff(0, 0, 0, 1)
         e_neg(6)
-        diff(0, 0, 3, 4)
+        diff(0, 0, 1, 2)
         quant(6, 0, 8)
+        diff(0, 0, 2, 4)
+        r_quant(0)
         unit(4, 0, 4)
         unit(5, 0, 4)
-        r_weave(1, 688, D, nc.scalar.copy)
+        r_weave(1, W, W + HALF, nc.scalar.copy)
         unit(0, 1, 7)
-        new_dif(1, 0, W, "qin1")
+        new_dif(1, 0, W, "xw0")
         diff(1, 0, 0, 2, 0, CUT, nc.gpsimd)
         d_scale(0, 0, 0, W)
         diff(1, 0, 0, 2, CUT)
         d_quant(0, 0, W)
-        r_quant(1)
+        r_weave(1, W + HALF, D, nc.scalar.copy)
         unit(6, 0, 7)
         unit(7, 0, 7)
         diff(1, 0, 2, 4)
         unit(1, 1, 7)
-        r_quant(0)
-        new_dif(0, W, H, "xw0")
+        r_quant(1)
+        new_dif(0, W, H, "xw1")
         diff(0, W, 0, 2, 0, CUT, nc.gpsimd)
         d_scale(1, 0, 0, W)
         diff(0, W, 0, 2, CUT)
@@ -429,12 +441,16 @@ def tile_centredequilibriumpropupdate_w4_kernel(
         last = W + HALF
         for b in range(T, 2 * T):
             narrow_unit(b, last)
-        new_dif(1, last, H, "xw1")
+        new_dif(1, last, H, "qin0")
         d_quant(1, W, W + HALF)
-        diff(1, last, 0, 3)
-        diff(1, last, 3, 4)
-        d_scale(1, last, last, H)
-        d_quant(1, last, H)
+        diff(1, last, 0, 2)
+        diff(1, last, 2, 3)
+        for lo in (0, P):
+            diff(1, last, 3, 4, lo, lo + P)
+        for lo in (last, last + P):
+            d_scale(1, last, lo, lo + P)
+        for lo in (last, last + P):
+            d_quant(1, lo, lo + P)
         for f in range(6, 8):
             wide_out(f)
         for j in range(4):

@@ -26,7 +26,7 @@ W = 512
 HALF = 256
 X_LOADS = ((0, 1), (1, 1), (2, 2), (4, 2), (6, 2))
 E_LOADS = ((0, 2), (2, 2), (4, 4))
-CUT = 384
+CUT = 768
 
 
 def tile_centredequilibriumpropupdate_w4_kernel(
@@ -52,6 +52,7 @@ def tile_centredequilibriumpropupdate_w4_kernel(
         w2t = keep.tile([P, 2 * H], U8, name="w2t", align_bytes=64)
         wsc = keep.tile([P, 3, H], U8, name="wsc", align_bytes=64)
         rb = keep.tile([P, G, T], BF16, name="rb", align_bytes=64)
+        rf = keep.tile([P, 1], F32, name="rf", align_bytes=64)
         gb = keep.tile([P, G, T], BF16, name="gb", align_bytes=64)
         gs = keep.tile([P, G, T], F32, name="gs", align_bytes=64)
         ident = keep.tile([P, P], F32, name="ident", align_bytes=64)
@@ -241,11 +242,11 @@ def tile_centredequilibriumpropupdate_w4_kernel(
 
         def hid_tile(i, lo, hi):
             if (i, lo) not in hid:
-                hid[i, lo] = keep.tile([P, T, 2, hi - lo], F32, name="hid%d_%d" % (i, lo), tag="hid%d_%d" % (i, lo), align_bytes=64)
+                hid[i, lo] = keep.tile([P, 2, T, hi - lo], F32, name="hid%d_%d" % (i, lo), tag="hid%d_%d" % (i, lo), align_bytes=64)
             return hid[i, lo]
 
         def tanh(src, b, s, lo):
-            nc.scalar.activation(out=hid_tile(b // T, lo, lo + W)[:, b % T, s, :], in_=src, func=TANH)
+            nc.scalar.activation(out=hid_tile(b // T, lo, lo + W)[:, s, b % T, :], in_=src, func=TANH)
 
         def unit(b, c, count):
             for s in range(2):
@@ -260,7 +261,9 @@ def tile_centredequilibriumpropupdate_w4_kernel(
                 a_passes(acc[:, s * HALF : (s + 1) * HALF], b, lo, lo + HALF)
                 f_pass(acc[:, s * HALF : (s + 1) * HALF], b, s, lo, lo + HALF)
             nc.scalar.activation(
-                out=hid_tile(b // T, lo, lo + HALF)[:, b % T, :, :].rearrange("p s n -> p (s n)"), in_=acc[:], func=TANH
+                out=hid_tile(b // T, lo, lo + HALF)[:, :, b % T, :],
+                in_=acc[:].rearrange("p (s n) -> p s n", s=2),
+                func=TANH,
             )
 
         dg = {}
@@ -270,10 +273,13 @@ def tile_centredequilibriumpropupdate_w4_kernel(
         def new_dif(i, lo, hi, tag):
             dif[i, lo] = keep.tile([P, T, hi - lo], F32, name="dif%d_%d" % (i, lo), tag=tag, align_bytes=64)
 
-        def diff(i, lo, t0, t1, c0=0, c1=None, engine=nc.vector):
-            tile = hid[i, lo]
+        def diff(i, lo, m0, m1, engine=nc.vector):
+            both = hid[i, lo][:].rearrange("p s t n -> p s (t n)")
             engine.tensor_tensor(
-                out=dif[i, lo][:, t0:t1, c0:c1], in0=tile[:, t0:t1, 0, c0:c1], in1=tile[:, t0:t1, 1, c0:c1], op=SUB
+                out=dif[i, lo][:].rearrange("p t n -> p (t n)")[:, m0:m1],
+                in0=both[:, 0, m0:m1],
+                in1=both[:, 1, m0:m1],
+                op=SUB,
             )
 
         def d_scale(i, base, lo, hi):
@@ -331,7 +337,9 @@ def tile_centredequilibriumpropupdate_w4_kernel(
         r_mul(0)
         quant(0, 0, 2)
         e_turn(0, 6)
+        nc.scalar.copy(out=rf[:], in_=rb[:, 0, 1:2])
         e_widen(2)
+        nc.scalar.activation(out=xm[0][:, 1, :], in_=xrow[1], func=COPY, scale=rf[:])
         x_turn(2, 7)
         x_turn(3, 3)
         e_turn(2, 4)
@@ -339,7 +347,6 @@ def tile_centredequilibriumpropupdate_w4_kernel(
         for s in range(2):
             a_passes(first[s][:], 0, 0, W)
         x_mul(1)
-        r_mul(1)
         e_mul(0)
         quant(0, 2, 4)
         e_neg(0)
@@ -381,59 +388,55 @@ def tile_centredequilibriumpropupdate_w4_kernel(
         e_mul(4)
         r_mul(6)
         e_neg(4)
-        r_mul(7, 336, D)
+        r_mul(7)
         quant(4, 0, 8)
+        unit(0, 1, 4)
         unit(2, 0, 4)
-        unit(3, 0, 4)
         r_weave(0, 944, D, nc.scalar.copy)
         x_turn_sorted(6, 4)
         x_turn_sorted(7, 5)
         e_turn(6, 6)
         gp = bank(7)
         nc.tensor.matmul(gp[:, 0 : G * T], lhsT=ident[:], rhs=gs[:].rearrange("p g t -> p (g t)"), start=True, stop=True)
-        new_dif(0, 0, W, "dif0")
+        new_dif(0, 0, W, "qin0")
+        diff(0, 0, 0, CUT, nc.gpsimd)
         new_qin(6)
-        r_mul(7, 0, 336)
-        g_weave(1, 0, 336)
-        r_weave(1, 336, W, nc.scalar.copy)
+        r_weave(1, 336, 688, nc.scalar.copy)
+        unit(3, 0, 4)
         x_mul(6)
         x_mul(7)
         e_mul(6)
-        diff(0, 0, 0, 1)
         e_neg(6)
-        diff(0, 0, 1, 2)
         quant(6, 0, 8)
-        diff(0, 0, 2, 4)
+        diff(0, 0, CUT, T * W)
         r_quant(0)
         unit(4, 0, 4)
         unit(5, 0, 4)
-        r_weave(1, W, W + HALF, nc.scalar.copy)
-        unit(0, 1, 7)
+        r_weave(1, 688, D, nc.scalar.copy)
         new_dif(1, 0, W, "xw0")
-        diff(1, 0, 0, 2, 0, CUT, nc.gpsimd)
+        diff(1, 0, 0, CUT, nc.gpsimd)
         d_scale(0, 0, 0, W)
-        diff(1, 0, 0, 2, CUT)
         d_quant(0, 0, W)
-        r_weave(1, W + HALF, D, nc.scalar.copy)
         unit(6, 0, 7)
         unit(7, 0, 7)
-        diff(1, 0, 2, 4)
+        r_weave(1, 0, 336, nc.scalar.copy)
+        diff(1, 0, CUT, T * W)
         unit(1, 1, 7)
         r_quant(1)
         new_dif(0, W, H, "xw1")
-        diff(0, W, 0, 2, 0, CUT, nc.gpsimd)
+        diff(0, W, 0, CUT, nc.gpsimd)
         d_scale(1, 0, 0, W)
-        diff(0, W, 0, 2, CUT)
-        d_quant(1, 0, W)
         unit(2, 1, 7)
         unit(3, 1, 7)
-        diff(0, W, 2, 4)
+        diff(0, W, CUT, 2 * W)
+        d_quant(1, 0, W)
+        diff(0, W, 2 * W, T * W)
         for b in range(T, 2 * T):
             narrow_unit(b, W)
         new_dif(1, W, W + HALF, "hid0_512")
-        diff(1, W, 0, 3, engine=nc.gpsimd)
+        diff(1, W, 0, CUT, nc.gpsimd)
         d_scale(0, W, W, H)
-        diff(1, W, 3, 4)
+        diff(1, W, CUT, T * HALF)
         d_quant(0, W, H)
         d_scale(1, W, W, W + HALF)
         for f in range(6):
@@ -441,12 +444,11 @@ def tile_centredequilibriumpropupdate_w4_kernel(
         last = W + HALF
         for b in range(T, 2 * T):
             narrow_unit(b, last)
-        new_dif(1, last, H, "qin0")
+        new_dif(1, last, H, "qin1")
         d_quant(1, W, W + HALF)
-        diff(1, last, 0, 2)
-        diff(1, last, 2, 3)
-        for lo in (0, P):
-            diff(1, last, 3, 4, lo, lo + P)
+        diff(1, last, 0, 2 * HALF)
+        diff(1, last, 2 * HALF, 3 * HALF)
+        diff(1, last, 3 * HALF, T * HALF)
         for lo in (last, last + P):
             d_scale(1, last, lo, lo + P)
         for lo in (last, last + P):

@@ -26,7 +26,7 @@ W = 512
 HALF = 256
 X_LOADS = ((0, 1), (1, 1), (2, 2), (4, 2), (6, 2))
 E_LOADS = ((0, 2), (2, 2), (4, 4))
-CUT = 768
+CUT = 640
 
 
 def tile_centredequilibriumpropupdate_w4_kernel(
@@ -83,11 +83,11 @@ def tile_centredequilibriumpropupdate_w4_kernel(
         load_x(*X_LOADS[0])
         nc.sync.dma_start(out=pt[:], in_=p.rearrange("(k q t) -> q k t", k=2, q=P, t=T))
         load_e(*E_LOADS[0])
-        nc.sync.dma_start(out=rb[:], in_=r.rearrange("(g p t) -> p g t", g=G, p=P, t=T))
         load_x(*X_LOADS[1])
+        nc.sync.dma_start(out=rb[:], in_=r.rearrange("(g p t) -> p g t", g=G, p=P, t=T))
+        load_e(*E_LOADS[1])
         nc.sync.dma_start(out=est[:], in_=e_scale.rearrange("o (q t) -> q (o t)", t=T))
         load_x(*X_LOADS[2])
-        load_e(*E_LOADS[1])
         for q in range(4):
             nc.sync.dma_start(
                 out=wsc[32 * q : 32 * q + 4, 0:2, :].bitcast(I32),
@@ -95,14 +95,14 @@ def tile_centredequilibriumpropupdate_w4_kernel(
             )
         load_w1(0)
         load_e(*E_LOADS[2])
+        load_x(*X_LOADS[3])
         nc.sync.dma_start(out=w2t[:], in_=w2_words[0])
         for q in range(4):
             nc.sync.dma_start(
                 out=wsc[32 * q : 32 * q + 4, 2, :].bitcast(I32), in_=w2_scales[0, 4 * q : 4 * q + 4, :].bitcast(I32)
             )
-        load_x(*X_LOADS[3])
-        nc.sync.dma_start(out=gb[:], in_=g.rearrange("(g p t) -> p g t", g=G, p=P, t=T))
         load_w1(1)
+        nc.sync.dma_start(out=gb[:], in_=g.rearrange("(g p t) -> p g t", g=G, p=P, t=T))
         load_x(*X_LOADS[4])
 
         ew = {}
@@ -323,11 +323,11 @@ def tile_centredequilibriumpropupdate_w4_kernel(
                 s2_pass(acc[:, m * HALF : (m + 1) * HALF], f0 + m, i, lo, lo + HALF, first, last)
 
 
-        def wide_out(f):
+        def wide_out(f, copy):
             acc = next_bank(7)
             for i in range(G):
                 s2_pass(acc[:], f, i, 0, W, i == 0, i == G - 1)
-            put_out(acc, nc.scalar.copy, f, 1, 0, W)
+            put_out(acc, copy, f, 1, 0, W)
 
         x_turn(0, 4)
         e_widen(0)
@@ -360,42 +360,42 @@ def tile_centredequilibriumpropupdate_w4_kernel(
         new_qin(2)
         r_mul(3, 0, 592)
         g_weave(0, HALF, 592)
+        e_mul(2)
         x_mul(2)
         x_mul(3)
-        e_mul(2)
         x_sort(4)
         r_weave(0, 0, HALF, nc.scalar.copy)
-        r_mul(4)
         e_neg(2)
+        r_mul(4)
         r_mul(5)
         quant(2, 0, 8)
         for j in range(4):
             f_pass(first[j][:], j // 2, j % 2, 0, W)
             tanh(first[j][:], j // 2, j % 2, 0)
+        e_turn(4, 4)
         x_turn_sorted(4, 6)
         x_turn_sorted(5, 7)
-        e_turn(4, 4)
         x_sort(6)
         nc.scalar.activation(
             out=gs[:].rearrange("p g t -> p (g t)"), in_=gb[:].rearrange("p g t -> p (g t)"), func=COPY, scale=1.0 / 32.0
         )
-        turn[0] = 3
+        turn[0] = 2
         new_qin(4)
         r_mul(3, 592, D)
-        g_weave(0, 592, 944)
+        g_weave(0, 592, 928)
+        e_mul(4)
         x_mul(4)
         x_mul(5)
-        e_mul(4)
-        r_mul(6)
         e_neg(4)
+        r_mul(6)
         r_mul(7)
         quant(4, 0, 8)
         unit(0, 1, 4)
         unit(2, 0, 4)
-        r_weave(0, 944, D, nc.scalar.copy)
-        x_turn_sorted(6, 4)
-        x_turn_sorted(7, 5)
-        e_turn(6, 6)
+        r_weave(0, 928, D, nc.scalar.copy)
+        e_turn(6, 4)
+        x_turn_sorted(6, 5)
+        x_turn_sorted(7, 6)
         gp = bank(7)
         nc.tensor.matmul(gp[:, 0 : G * T], lhsT=ident[:], rhs=gs[:].rearrange("p g t -> p (g t)"), start=True, stop=True)
         new_dif(0, 0, W, "qin0")
@@ -403,11 +403,12 @@ def tile_centredequilibriumpropupdate_w4_kernel(
         new_qin(6)
         r_weave(1, 336, 688, nc.scalar.copy)
         unit(3, 0, 4)
+        e_mul(6)
         x_mul(6)
         x_mul(7)
-        e_mul(6)
         e_neg(6)
-        quant(6, 0, 8)
+        quant(6, 0, 4)
+        quant(6, 4, 8)
         diff(0, 0, CUT, T * W)
         r_quant(0)
         unit(4, 0, 4)
@@ -416,11 +417,12 @@ def tile_centredequilibriumpropupdate_w4_kernel(
         new_dif(1, 0, W, "xw0")
         diff(1, 0, 0, CUT, nc.gpsimd)
         d_scale(0, 0, 0, W)
+        diff(1, 0, CUT, 2 * W)
         d_quant(0, 0, W)
         unit(6, 0, 7)
         unit(7, 0, 7)
         r_weave(1, 0, 336, nc.scalar.copy)
-        diff(1, 0, CUT, T * W)
+        diff(1, 0, 2 * W, T * W)
         unit(1, 1, 7)
         r_quant(1)
         new_dif(0, W, H, "xw1")
@@ -438,23 +440,26 @@ def tile_centredequilibriumpropupdate_w4_kernel(
         d_scale(0, W, W, H)
         diff(1, W, CUT, T * HALF)
         d_quant(0, W, H)
-        d_scale(1, W, W, W + HALF)
-        for f in range(6):
-            wide_out(f)
         last = W + HALF
-        for b in range(T, 2 * T):
+        for b in range(T, T + 1):
+            narrow_unit(b, last)
+        for f in range(6):
+            wide_out(f, nc.scalar.copy)
+        d_scale(1, W, W, W + HALF)
+        d_quant(1, W, W + HALF)
+        for b in range(T + 1, 2 * T):
             narrow_unit(b, last)
         new_dif(1, last, H, "qin1")
-        d_quant(1, W, W + HALF)
         diff(1, last, 0, 2 * HALF)
         diff(1, last, 2 * HALF, 3 * HALF)
-        diff(1, last, 3 * HALF, T * HALF)
+        for lo in (0, P):
+            diff(1, last, 3 * HALF + lo, 3 * HALF + lo + P)
         for lo in (last, last + P):
             d_scale(1, last, lo, lo + P)
         for lo in (last, last + P):
             d_quant(1, lo, lo + P)
         for f in range(6, 8):
-            wide_out(f)
+            wide_out(f, nc.scalar.copy)
         for j in range(4):
             acc = next_bank(7)
             for i in range(G):

@@ -24,9 +24,9 @@ G = 2
 T = 4
 W = 512
 HALF = 256
-X_LOADS = ((0, 1), (1, 1), (2, 2), (4, 2), (6, 2))
+X_LOADS = ((0, 1), (1, 1), (2, 1), (3, 1), (4, 2), (6, 2))
 E_LOADS = ((0, 2), (2, 2), (4, 4))
-CUT = 640
+CUT = 704
 
 
 def tile_centredequilibriumpropupdate_w4_kernel(
@@ -62,7 +62,7 @@ def tile_centredequilibriumpropupdate_w4_kernel(
         rs = [keep.tile([P, D], U8, name="rs%d" % i, align_bytes=64) for i in range(G)]
         dc = [keep.tile([P, H], U32, name="dc%d" % i, align_bytes=64) for i in range(G)]
         ds = [keep.tile([P, H], U8, name="ds%d" % i, align_bytes=64) for i in range(G)]
-        xm = [keep.tile([P, T, D], BF16, name="xm%d" % i, align_bytes=64) for i in range(G)]
+        xm = [keep.tile([P, T, D], BF16, name="xm%d" % i, tag="xm%d" % i, align_bytes=64) for i in range(G)]
         xw = [keep.tile([P, D, T], BF16, name="xw%d" % i, tag="xw%d" % i, align_bytes=64) for i in range(G)]
 
         xv = x.rearrange("(g p t) d -> g p t d", g=G, p=P, t=T)
@@ -81,13 +81,14 @@ def tile_centredequilibriumpropupdate_w4_kernel(
         nc.vector.memset(wsc[:].rearrange("p k n -> p (k n)").bitcast(I32), 0)
         make_identity(nc, ident[:])
         load_x(*X_LOADS[0])
-        nc.sync.dma_start(out=pt[:], in_=p.rearrange("(k q t) -> q k t", k=2, q=P, t=T))
         load_e(*E_LOADS[0])
+        nc.sync.dma_start(out=pt[:], in_=p.rearrange("(k q t) -> q k t", k=2, q=P, t=T))
         load_x(*X_LOADS[1])
-        nc.sync.dma_start(out=rb[:], in_=r.rearrange("(g p t) -> p g t", g=G, p=P, t=T))
         load_e(*E_LOADS[1])
-        nc.sync.dma_start(out=est[:], in_=e_scale.rearrange("o (q t) -> q (o t)", t=T))
+        nc.sync.dma_start(out=rb[:], in_=r.rearrange("(g p t) -> p g t", g=G, p=P, t=T))
         load_x(*X_LOADS[2])
+        nc.sync.dma_start(out=est[:], in_=e_scale.rearrange("o (q t) -> q (o t)", t=T))
+        load_x(*X_LOADS[3])
         for q in range(4):
             nc.sync.dma_start(
                 out=wsc[32 * q : 32 * q + 4, 0:2, :].bitcast(I32),
@@ -95,7 +96,7 @@ def tile_centredequilibriumpropupdate_w4_kernel(
             )
         load_w1(0)
         load_e(*E_LOADS[2])
-        load_x(*X_LOADS[3])
+        load_x(*X_LOADS[4])
         nc.sync.dma_start(out=w2t[:], in_=w2_words[0])
         for q in range(4):
             nc.sync.dma_start(
@@ -103,7 +104,7 @@ def tile_centredequilibriumpropupdate_w4_kernel(
             )
         load_w1(1)
         nc.sync.dma_start(out=gb[:], in_=g.rearrange("(g p t) -> p g t", g=G, p=P, t=T))
-        load_x(*X_LOADS[4])
+        load_x(*X_LOADS[5])
 
         ew = {}
         xbank = {}
@@ -351,6 +352,8 @@ def tile_centredequilibriumpropupdate_w4_kernel(
         quant(0, 2, 4)
         e_neg(0)
         r_mul(2)
+        r_mul(3, 0, 624)
+        g_weave(0, HALF, 624)
         quant(0, 4, 8)
         e_widen(4)
         e_widen(6)
@@ -358,8 +361,6 @@ def tile_centredequilibriumpropupdate_w4_kernel(
         for s in range(2):
             a_passes(first[2 + s][:], 1, 0, W)
         new_qin(2)
-        r_mul(3, 0, 592)
-        g_weave(0, HALF, 592)
         e_mul(2)
         x_mul(2)
         x_mul(3)
@@ -368,6 +369,8 @@ def tile_centredequilibriumpropupdate_w4_kernel(
         e_neg(2)
         r_mul(4)
         r_mul(5)
+        r_mul(3, 624, D)
+        g_weave(0, 624, 992)
         quant(2, 0, 8)
         for j in range(4):
             f_pass(first[j][:], j // 2, j % 2, 0, W)
@@ -381,8 +384,6 @@ def tile_centredequilibriumpropupdate_w4_kernel(
         )
         turn[0] = 2
         new_qin(4)
-        r_mul(3, 592, D)
-        g_weave(0, 592, 928)
         e_mul(4)
         x_mul(4)
         x_mul(5)
@@ -392,14 +393,14 @@ def tile_centredequilibriumpropupdate_w4_kernel(
         quant(4, 0, 8)
         unit(0, 1, 4)
         unit(2, 0, 4)
-        r_weave(0, 928, D, nc.scalar.copy)
+        r_weave(0, 992, D, nc.scalar.copy)
         e_turn(6, 4)
         x_turn_sorted(6, 5)
         x_turn_sorted(7, 6)
         gp = bank(7)
         nc.tensor.matmul(gp[:, 0 : G * T], lhsT=ident[:], rhs=gs[:].rearrange("p g t -> p (g t)"), start=True, stop=True)
         new_dif(0, 0, W, "qin0")
-        diff(0, 0, 0, CUT, nc.gpsimd)
+        diff(0, 0, 0, 576, nc.gpsimd)
         new_qin(6)
         r_weave(1, 336, 688, nc.scalar.copy)
         unit(3, 0, 4)
@@ -409,12 +410,12 @@ def tile_centredequilibriumpropupdate_w4_kernel(
         e_neg(6)
         quant(6, 0, 4)
         quant(6, 4, 8)
-        diff(0, 0, CUT, T * W)
+        diff(0, 0, 576, T * W)
         r_quant(0)
-        unit(4, 0, 4)
-        unit(5, 0, 4)
+        unit(4, 0, 7)
+        unit(5, 0, 7)
         r_weave(1, 688, D, nc.scalar.copy)
-        new_dif(1, 0, W, "xw0")
+        new_dif(1, 0, W, "hid0_0")
         diff(1, 0, 0, CUT, nc.gpsimd)
         d_scale(0, 0, 0, W)
         diff(1, 0, CUT, 2 * W)
@@ -426,13 +427,12 @@ def tile_centredequilibriumpropupdate_w4_kernel(
         unit(1, 1, 7)
         r_quant(1)
         new_dif(0, W, H, "xw1")
-        diff(0, W, 0, CUT, nc.gpsimd)
+        diff(0, W, 0, 640, nc.gpsimd)
         d_scale(1, 0, 0, W)
         unit(2, 1, 7)
         unit(3, 1, 7)
-        diff(0, W, CUT, 2 * W)
+        diff(0, W, 640, T * W)
         d_quant(1, 0, W)
-        diff(0, W, 2 * W, T * W)
         for b in range(T, 2 * T):
             narrow_unit(b, W)
         new_dif(1, W, W + HALF, "hid0_512")
@@ -441,16 +441,16 @@ def tile_centredequilibriumpropupdate_w4_kernel(
         diff(1, W, CUT, T * HALF)
         d_quant(0, W, H)
         last = W + HALF
-        for b in range(T, T + 1):
+        for b in range(T, T + 2):
             narrow_unit(b, last)
         for f in range(6):
             wide_out(f, nc.scalar.copy)
-        d_scale(1, W, W, W + HALF)
-        d_quant(1, W, W + HALF)
-        for b in range(T + 1, 2 * T):
-            narrow_unit(b, last)
         new_dif(1, last, H, "qin1")
+        d_scale(1, W, W, W + HALF)
         diff(1, last, 0, 2 * HALF)
+        d_quant(1, W, W + HALF)
+        for b in range(T + 2, 2 * T):
+            narrow_unit(b, last)
         diff(1, last, 2 * HALF, 3 * HALF)
         for lo in (0, P):
             diff(1, last, 3 * HALF + lo, 3 * HALF + lo + P)

@@ -23,10 +23,18 @@ FLOPS = 2 * N * D * H + 2 * N * O * H + 2 * N * D * H
 G = 2
 T = 4
 W = 512
-HALF = 256
+HALF = W // 2
+LAST = H - HALF
 X_LOADS = ((0, 1), (1, 1), (2, 1), (3, 1), (4, 2), (6, 2))
 E_LOADS = ((0, 2), (2, 2), (4, 4))
-CUT = 704
+XR_MID = (HALF + D) // 2
+XR_THIRDS = (0, 352, 704, D)
+LATE_PIECE = 640
+EARLY_PIECE = 704
+AHEAD = 2
+WIDE_FIRST = 6
+STAGE_BANKS = 4
+ALL_BANKS = 7
 
 
 def tile_centredequilibriumpropupdate_w4_kernel(
@@ -52,7 +60,7 @@ def tile_centredequilibriumpropupdate_w4_kernel(
         w2t = keep.tile([P, 2 * H], U8, name="w2t", align_bytes=64)
         wsc = keep.tile([P, 3, H], U8, name="wsc", align_bytes=64)
         rb = keep.tile([P, G, T], BF16, name="rb", align_bytes=64)
-        rf = keep.tile([P, 1], F32, name="rf", align_bytes=64)
+        r1 = keep.tile([P, 1], F32, name="r1", align_bytes=64)
         gb = keep.tile([P, G, T], BF16, name="gb", align_bytes=64)
         gs = keep.tile([P, G, T], F32, name="gs", align_bytes=64)
         ident = keep.tile([P, P], F32, name="ident", align_bytes=64)
@@ -80,6 +88,7 @@ def tile_centredequilibriumpropupdate_w4_kernel(
 
         nc.vector.memset(wsc[:].rearrange("p k n -> p (k n)").bitcast(I32), 0)
         make_identity(nc, ident[:])
+
         load_x(*X_LOADS[0])
         load_e(*E_LOADS[0])
         nc.sync.dma_start(out=pt[:], in_=p.rearrange("(k q t) -> q k t", k=2, q=P, t=T))
@@ -107,6 +116,7 @@ def tile_centredequilibriumpropupdate_w4_kernel(
         load_x(*X_LOADS[5])
 
         ew = {}
+        xsorted = {}
         xbank = {}
         ebank = {}
         qin = {}
@@ -125,19 +135,19 @@ def tile_centredequilibriumpropupdate_w4_kernel(
                     lo = P * (2 * u + k)
                     nc.tensor.transpose(xbank[b][:, lo : lo + P], words[:, 256 * k + u : 256 * (k + 1) : 2], ident[:])
 
-        sorted_x = {}
-
-        def x_sort(b0):
-            sorted_x[b0] = work.tile([P, 2, W], F32, name="xs", bufs=1, align_bytes=64)
+        def x_sort(b0, n):
+            tile = work.tile([P, n, W], F32, name="xs", bufs=2, align_bytes=64)
             nc.scalar.copy(
-                out=sorted_x[b0][:].rearrange("p j (u m) -> p j m u", u=2),
+                out=tile[:].rearrange("p j (u m) -> p j m u", u=2),
                 in_=xt[b0][:].bitcast(F32).rearrange("p j (m u) -> p j m u", u=2),
             )
+            for j in range(n):
+                xsorted[b0 + j] = tile[:, j, :]
 
         def x_turn_sorted(b, i):
             xbank[b] = bank(i)
             for lo in range(0, W, P):
-                nc.tensor.transpose(xbank[b][:, lo : lo + P], sorted_x[b - b % 2][:, b % 2, lo : lo + P], ident[:])
+                nc.tensor.transpose(xbank[b][:, lo : lo + P], xsorted[b][:, lo : lo + P], ident[:])
 
         def e_turn(b0, i):
             ebank[b0] = bank(i)
@@ -170,6 +180,11 @@ def tile_centredequilibriumpropupdate_w4_kernel(
                 op=MULT,
             )
 
+        def pair_window(b0):
+            e_mul(b0)
+            x_mul(b0)
+            x_mul(b0 + 1)
+
         def e_neg(b0):
             nc.vector.tensor_scalar(
                 out=qin[b0 // 2][:, 6:8, :], in0=qin[b0 // 2][:, 4:6, :], scalar1=-1.0, scalar2=None, op0=MULT
@@ -188,28 +203,27 @@ def tile_centredequilibriumpropupdate_w4_kernel(
                 out=xm[i][:, t, lo:hi], in0=xrow[b][:, lo:hi], scalar1=rb[:, i, t : t + 1], scalar2=None, op0=MULT
             )
 
-        def g_weave(i, lo, hi):
+        def weave_gpsimd(lo, hi):
             nc.gpsimd.tensor_scalar(
-                out=xw[i][:, lo:hi, :],
-                in0=xm[i][:, :, lo:hi].rearrange("p t n -> p n t"),
+                out=xw[0][:, lo:hi, :],
+                in0=xm[0][:, :, lo:hi].rearrange("p t n -> p n t"),
                 scalar1=1.0,
                 scalar2=0.0,
                 op0=MULT,
                 op1=ADD,
             )
 
-        def weave(copy, dst, src):
-            copy(out=dst.rearrange("p (n j) t -> p n t j", j=4), in_=src.rearrange("p t (n j) -> p n t j", j=4))
-
-        def r_weave(i, lo, hi, copy):
-            weave(copy, xw[i][:, lo:hi, :], xm[i][:, :, lo:hi])
+        def weave_scalar(i, lo, hi):
+            nc.scalar.copy(
+                out=xw[i][:, lo:hi, :].rearrange("p (n j) t -> p n t j", j=4),
+                in_=xm[i][:, :, lo:hi].rearrange("p t (n j) -> p n t j", j=4),
+            )
 
         def r_quant(i):
             nc.vector.quantize_mx(
                 out=rc[i][:].bitcast(FP8X4), scales=rs[i][:], in_=xw[i][:].rearrange("p n t -> p (n t)")
             )
 
-        ub = {}
         hid = {}
         turn = [0]
 
@@ -243,7 +257,8 @@ def tile_centredequilibriumpropupdate_w4_kernel(
 
         def hid_tile(i, lo, hi):
             if (i, lo) not in hid:
-                hid[i, lo] = keep.tile([P, 2, T, hi - lo], F32, name="hid%d_%d" % (i, lo), tag="hid%d_%d" % (i, lo), align_bytes=64)
+                name = "hid%d_%d" % (i, lo)
+                hid[i, lo] = keep.tile([P, 2, T, hi - lo], F32, name=name, tag=name, align_bytes=64)
             return hid[i, lo]
 
         def tanh(src, b, s, lo):
@@ -257,7 +272,7 @@ def tile_centredequilibriumpropupdate_w4_kernel(
                 tanh(acc[:], b, s, c * W)
 
         def narrow_unit(b, lo):
-            acc = next_bank(7)
+            acc = next_bank(ALL_BANKS)
             for s in range(2):
                 a_passes(acc[:, s * HALF : (s + 1) * HALF], b, lo, lo + HALF)
                 f_pass(acc[:, s * HALF : (s + 1) * HALF], b, s, lo, lo + HALF)
@@ -267,9 +282,8 @@ def tile_centredequilibriumpropupdate_w4_kernel(
                 func=TANH,
             )
 
-        dg = {}
-
         dif = {}
+        dg = {}
 
         def new_dif(i, lo, hi, tag):
             dif[i, lo] = keep.tile([P, T, hi - lo], F32, name="dif%d_%d" % (i, lo), tag=tag, align_bytes=64)
@@ -318,17 +332,17 @@ def tile_centredequilibriumpropupdate_w4_kernel(
                 in_=res[:].rearrange("p (j n) -> p j n", j=nf),
             )
 
-        def bank_passes(acc, f0, i, lo):
+        def wide_out(f):
+            acc = next_bank(ALL_BANKS)
+            for i in range(G):
+                s2_pass(acc[:], f, i, 0, W, i == 0, i == G - 1)
+            put_out(acc, nc.scalar.copy, f, 1, 0, W)
+
+        def pair_passes(acc, f0, i, lo):
             for m in range(2):
                 first, last = (i, m) == (0, 0), (i, m) == (G - 1, 1)
                 s2_pass(acc[:, m * HALF : (m + 1) * HALF], f0 + m, i, lo, lo + HALF, first, last)
 
-
-        def wide_out(f, copy):
-            acc = next_bank(7)
-            for i in range(G):
-                s2_pass(acc[:], f, i, 0, W, i == 0, i == G - 1)
-            put_out(acc, copy, f, 1, 0, W)
 
         x_turn(0, 4)
         e_widen(0)
@@ -338,12 +352,13 @@ def tile_centredequilibriumpropupdate_w4_kernel(
         r_mul(0)
         quant(0, 0, 2)
         e_turn(0, 6)
-        nc.scalar.copy(out=rf[:], in_=rb[:, 0, 1:2])
+        nc.scalar.copy(out=r1[:], in_=rb[:, 0, 1:2])
         e_widen(2)
-        nc.scalar.activation(out=xm[0][:, 1, :], in_=xrow[1], func=COPY, scale=rf[:])
+        x_sort(3, 1)
         x_turn(2, 7)
-        x_turn(3, 3)
         e_turn(2, 4)
+        x_turn_sorted(3, 3)
+        nc.scalar.activation(out=xm[0][:, 1, :], in_=xrow[1], func=COPY, scale=r1[:])
         first = [bank(j) for j in range(2)]
         for s in range(2):
             a_passes(first[s][:], 0, 0, W)
@@ -352,123 +367,124 @@ def tile_centredequilibriumpropupdate_w4_kernel(
         quant(0, 2, 4)
         e_neg(0)
         r_mul(2)
-        r_mul(3, 0, 624)
-        g_weave(0, HALF, 624)
+        r_mul(3, 0, XR_MID)
+        weave_gpsimd(HALF, XR_MID)
         quant(0, 4, 8)
         e_widen(4)
         e_widen(6)
         first.extend([bank(2), bank(5)])
         for s in range(2):
             a_passes(first[2 + s][:], 1, 0, W)
+
         new_qin(2)
-        e_mul(2)
-        x_mul(2)
-        x_mul(3)
-        x_sort(4)
-        r_weave(0, 0, HALF, nc.scalar.copy)
+        pair_window(2)
+        x_sort(4, 2)
+        weave_scalar(0, 0, HALF)
         e_neg(2)
         r_mul(4)
         r_mul(5)
-        r_mul(3, 624, D)
-        g_weave(0, 624, 992)
+        r_mul(3, XR_MID, D)
+        weave_gpsimd(XR_MID, D)
         quant(2, 0, 8)
         for j in range(4):
             f_pass(first[j][:], j // 2, j % 2, 0, W)
             tanh(first[j][:], j // 2, j % 2, 0)
+
         e_turn(4, 4)
         x_turn_sorted(4, 6)
         x_turn_sorted(5, 7)
-        x_sort(6)
+        x_sort(6, 2)
         nc.scalar.activation(
             out=gs[:].rearrange("p g t -> p (g t)"), in_=gb[:].rearrange("p g t -> p (g t)"), func=COPY, scale=1.0 / 32.0
         )
         turn[0] = 2
         new_qin(4)
-        e_mul(4)
-        x_mul(4)
-        x_mul(5)
+        pair_window(4)
         e_neg(4)
         r_mul(6)
         r_mul(7)
         quant(4, 0, 8)
-        unit(0, 1, 4)
-        unit(2, 0, 4)
-        r_weave(0, 992, D, nc.scalar.copy)
+        unit(0, 1, STAGE_BANKS)
+        unit(2, 0, STAGE_BANKS)
+
         e_turn(6, 4)
         x_turn_sorted(6, 5)
         x_turn_sorted(7, 6)
-        gp = bank(7)
+        gp = bank(ALL_BANKS)
         nc.tensor.matmul(gp[:, 0 : G * T], lhsT=ident[:], rhs=gs[:].rearrange("p g t -> p (g t)"), start=True, stop=True)
         new_dif(0, 0, W, "qin0")
-        diff(0, 0, 0, 576, nc.gpsimd)
+        diff(0, 0, 0, LATE_PIECE, nc.gpsimd)
         new_qin(6)
-        r_weave(1, 336, 688, nc.scalar.copy)
-        unit(3, 0, 4)
-        e_mul(6)
-        x_mul(6)
-        x_mul(7)
+        weave_scalar(1, *XR_THIRDS[0:2])
+        unit(3, 0, STAGE_BANKS)
+        pair_window(6)
         e_neg(6)
         quant(6, 0, 4)
         quant(6, 4, 8)
-        diff(0, 0, 576, T * W)
+
+        diff(0, 0, LATE_PIECE, T * W)
         r_quant(0)
-        unit(4, 0, 7)
-        unit(5, 0, 7)
-        r_weave(1, 688, D, nc.scalar.copy)
+        unit(4, 0, ALL_BANKS)
+        unit(5, 0, ALL_BANKS)
+        weave_scalar(1, *XR_THIRDS[1:3])
         new_dif(1, 0, W, "hid0_0")
-        diff(1, 0, 0, CUT, nc.gpsimd)
+        diff(1, 0, 0, EARLY_PIECE, nc.gpsimd)
         d_scale(0, 0, 0, W)
-        diff(1, 0, CUT, 2 * W)
+        diff(1, 0, EARLY_PIECE, 2 * W)
         d_quant(0, 0, W)
-        unit(6, 0, 7)
-        unit(7, 0, 7)
-        r_weave(1, 0, 336, nc.scalar.copy)
+        unit(6, 0, ALL_BANKS)
+        unit(7, 0, ALL_BANKS)
+        weave_scalar(1, *XR_THIRDS[2:4])
         diff(1, 0, 2 * W, T * W)
-        unit(1, 1, 7)
+        unit(1, 1, ALL_BANKS)
         r_quant(1)
         new_dif(0, W, H, "xw1")
-        diff(0, W, 0, 640, nc.gpsimd)
+        diff(0, W, 0, LATE_PIECE, nc.gpsimd)
         d_scale(1, 0, 0, W)
-        unit(2, 1, 7)
-        unit(3, 1, 7)
-        diff(0, W, 640, T * W)
+
+        unit(2, 1, ALL_BANKS)
+        unit(3, 1, ALL_BANKS)
+        diff(0, W, LATE_PIECE, T * W)
         d_quant(1, 0, W)
         for b in range(T, 2 * T):
             narrow_unit(b, W)
-        new_dif(1, W, W + HALF, "hid0_512")
-        diff(1, W, 0, CUT, nc.gpsimd)
+        new_dif(1, W, LAST, "hid0_%d" % W)
+        diff(1, W, 0, EARLY_PIECE, nc.gpsimd)
         d_scale(0, W, W, H)
-        diff(1, W, CUT, T * HALF)
+        diff(1, W, EARLY_PIECE, T * HALF)
         d_quant(0, W, H)
-        last = W + HALF
-        for b in range(T, T + 2):
-            narrow_unit(b, last)
-        for f in range(6):
-            wide_out(f, nc.scalar.copy)
-        new_dif(1, last, H, "qin1")
-        d_scale(1, W, W, W + HALF)
-        diff(1, last, 0, 2 * HALF)
-        d_quant(1, W, W + HALF)
-        for b in range(T + 2, 2 * T):
-            narrow_unit(b, last)
-        diff(1, last, 2 * HALF, 3 * HALF)
-        for lo in (0, P):
-            diff(1, last, 3 * HALF + lo, 3 * HALF + lo + P)
-        for lo in (last, last + P):
-            d_scale(1, last, lo, lo + P)
-        for lo in (last, last + P):
+        new_dif(1, LAST, H, "qin1")
+        for b in range(T, T + AHEAD):
+            narrow_unit(b, LAST)
+        for f in range(WIDE_FIRST):
+            wide_out(f)
+        d_scale(1, W, W, LAST)
+        diff(1, LAST, 0, AHEAD * HALF)
+        d_quant(1, W, LAST)
+        for b in range(T + AHEAD, 2 * T):
+            narrow_unit(b, LAST)
+
+        diff(1, LAST, AHEAD * HALF, (T - 1) * HALF)
+        halves = (LAST, LAST + P)
+        for lo in halves:
+            diff(1, LAST, (T - 1) * HALF + lo - LAST, (T - 1) * HALF + lo - LAST + P)
+        for lo in halves:
+            d_scale(1, LAST, lo, lo + P)
+        for lo in halves:
             d_quant(1, lo, lo + P)
-        for f in range(6, 8):
-            wide_out(f, nc.scalar.copy)
-        for j in range(4):
-            acc = next_bank(7)
+
+        for f in range(WIDE_FIRST, D // P):
+            wide_out(f)
+        for f0 in range(0, D // P, 2):
+            acc = next_bank(ALL_BANKS)
             for i in range(G):
-                bank_passes(acc, 2 * j, i, W)
-            put_out(acc, nc.scalar.copy, 2 * j, 2, W, last)
-        accs = [next_bank(7) for j in range(4)]
-        for j in range(4):
-            if j % 2 == 0:
-                bank_passes(accs[j], 2 * j, 0, last)
-                bank_passes(accs[j + 1], 2 * j + 2, 0, last)
-            bank_passes(accs[j], 2 * j, 1, last)
-            put_out(accs[j], (nc.scalar.copy, nc.vector.tensor_copy)[j % 2], 2 * j, 2, last, H)
+                pair_passes(acc, f0, i, W)
+            put_out(acc, nc.scalar.copy, f0, 2, W, LAST)
+        for f0 in range(0, D // P, 4):
+            accs = []
+            for j in range(2):
+                accs.append(next_bank(ALL_BANKS))
+                pair_passes(accs[j], f0 + 2 * j, 0, LAST)
+            for j, copy in enumerate((nc.scalar.copy, nc.vector.tensor_copy)):
+                pair_passes(accs[j], f0 + 2 * j, 1, LAST)
+                put_out(accs[j], copy, f0 + 2 * j, 2, LAST, H)

@@ -33,6 +33,7 @@ LATE_PIECE = 640
 EARLY_PIECE = 704
 AHEAD = 2
 WIDE_FIRST = 6
+LINE = 256
 STAGE_BANKS = 4
 ALL_BANKS = 7
 
@@ -50,28 +51,28 @@ def tile_centredequilibriumpropupdate_w4_kernel(
         def bank(i):
             return psum.tile([P, W], F32, name="bank%d" % i)
 
-        xt = {b0: keep.tile([P, n, D], BF16, name="xt%d" % b0, align_bytes=64) for b0, n in X_LOADS}
+        xt = {b0: keep.tile([P, n, D], BF16, name="xt%d" % b0, align_bytes=LINE) for b0, n in X_LOADS}
         xrow = {b0 + j: xt[b0][:, j, :] for b0, n in X_LOADS for j in range(n)}
-        eb = {b0: keep.tile([P, n * O], U8, name="eb%d" % b0, align_bytes=64) for b0, n in E_LOADS}
+        eb = {b0: keep.tile([P, n * O], U8, name="eb%d" % b0, align_bytes=LINE) for b0, n in E_LOADS}
         epair = {b0 + j: eb[b0][:, j * O : (j + 2) * O] for b0, n in E_LOADS for j in range(0, n, 2)}
         est = keep.tile([P, T], F32, name="est", align_bytes=64)
         pt = keep.tile([P, 2, T], BF16, name="pt", align_bytes=64)
-        w1t = [keep.tile([P, 2, 2 * W], U8, name="w1t%d" % c, align_bytes=64) for c in range(2)]
-        w2t = keep.tile([P, 2 * H], U8, name="w2t", align_bytes=64)
-        wsc = keep.tile([P, 3, H], U8, name="wsc", align_bytes=64)
+        w1t = [keep.tile([P, 2, 2 * W], U8, name="w1t%d" % c, align_bytes=LINE) for c in range(2)]
+        w2t = keep.tile([P, 2 * H], U8, name="w2t", align_bytes=LINE)
+        wsc = keep.tile([P, 3, H], U8, name="wsc", align_bytes=LINE)
         rb = keep.tile([P, G, T], BF16, name="rb", align_bytes=64)
         r1 = keep.tile([P, 1], F32, name="r1", align_bytes=64)
         gb = keep.tile([P, G, T], BF16, name="gb", align_bytes=64)
         gs = keep.tile([P, G, T], F32, name="gs", align_bytes=64)
-        ident = keep.tile([P, P], F32, name="ident", align_bytes=64)
-        qc = keep.tile([P, G * T // 2, 8, P], U32, name="qc", align_bytes=64)
-        qs = keep.tile([P, G * T // 2, 8, P], U8, name="qs", align_bytes=64)
-        rc = [keep.tile([P, D], U32, name="rc%d" % i, align_bytes=64) for i in range(G)]
-        rs = [keep.tile([P, D], U8, name="rs%d" % i, align_bytes=64) for i in range(G)]
-        dc = [keep.tile([P, H], U32, name="dc%d" % i, align_bytes=64) for i in range(G)]
-        ds = [keep.tile([P, H], U8, name="ds%d" % i, align_bytes=64) for i in range(G)]
-        xm = [keep.tile([P, T, D], BF16, name="xm%d" % i, tag="xm%d" % i, align_bytes=64) for i in range(G)]
-        xw = [keep.tile([P, D, T], BF16, name="xw%d" % i, tag="xw%d" % i, align_bytes=64) for i in range(G)]
+        ident = keep.tile([P, P], F32, name="ident", align_bytes=LINE)
+        qc = keep.tile([P, G * T // 2, 8, P], U32, name="qc", align_bytes=LINE)
+        qs = keep.tile([P, G * T // 2, 8, P], U8, name="qs", align_bytes=LINE)
+        rc = [keep.tile([P, D], U32, name="rc%d" % i, align_bytes=LINE) for i in range(G)]
+        rs = [keep.tile([P, D], U8, name="rs%d" % i, align_bytes=LINE) for i in range(G)]
+        dc = [keep.tile([P, H], U32, name="dc%d" % i, align_bytes=LINE) for i in range(G)]
+        ds = [keep.tile([P, H], U8, name="ds%d" % i, align_bytes=LINE) for i in range(G)]
+        xm = [keep.tile([P, T, D], BF16, name="xm%d" % i, tag="xm%d" % i, align_bytes=LINE) for i in range(G)]
+        xw = [keep.tile([P, D, T], BF16, name="xw%d" % i, tag="xw%d" % i, align_bytes=LINE) for i in range(G)]
 
         xv = x.rearrange("(g p t) d -> g p t d", g=G, p=P, t=T)
         ev = e_bytes.rearrange("(g p t) o -> g p (t o)", g=G, p=P, t=T)
@@ -122,7 +123,7 @@ def tile_centredequilibriumpropupdate_w4_kernel(
         qin = {}
 
         def e_widen(b0):
-            ew[b0] = work.tile([P, 2, O], BF16, name="ew", bufs=4, align_bytes=64)
+            ew[b0] = work.tile([P, 2, O], BF16, name="ew", bufs=4, align_bytes=LINE)
             nc.scalar.activation(
                 out=ew[b0][:].rearrange("p j o -> p (j o)"), in_=epair[b0].bitcast(E4M3), func=COPY, scale=0.5
             )
@@ -136,7 +137,7 @@ def tile_centredequilibriumpropupdate_w4_kernel(
                     nc.tensor.transpose(xbank[b][:, lo : lo + P], words[:, 256 * k + u : 256 * (k + 1) : 2], ident[:])
 
         def x_sort(b0, n):
-            tile = work.tile([P, n, W], F32, name="xs", bufs=2, align_bytes=64)
+            tile = work.tile([P, n, W], F32, name="xs", bufs=2, align_bytes=LINE)
             nc.scalar.copy(
                 out=tile[:].rearrange("p j (u m) -> p j m u", u=2),
                 in_=xt[b0][:].bitcast(F32).rearrange("p j (m u) -> p j m u", u=2),
@@ -161,7 +162,7 @@ def tile_centredequilibriumpropupdate_w4_kernel(
             return 2 * (b % 2) + k if k < 2 else 2 * k + b % 2
 
         def new_qin(b0):
-            qin[b0 // 2] = keep.tile([P, 8, P * T], BF16, name="qin%d" % b0, tag="qin%d" % (b0 // 2 % 2), align_bytes=64)
+            qin[b0 // 2] = keep.tile([P, 8, P * T], BF16, name="qin%d" % b0, tag="qin%d" % (b0 // 2 % 2), align_bytes=LINE)
 
         def x_mul(b):
             lo = slot(b, 0)
@@ -258,7 +259,7 @@ def tile_centredequilibriumpropupdate_w4_kernel(
         def hid_tile(i, lo, hi):
             if (i, lo) not in hid:
                 name = "hid%d_%d" % (i, lo)
-                hid[i, lo] = keep.tile([P, 2, T, hi - lo], F32, name=name, tag=name, align_bytes=64)
+                hid[i, lo] = keep.tile([P, 2, T, hi - lo], F32, name=name, tag=name, align_bytes=LINE)
             return hid[i, lo]
 
         def tanh(src, b, s, lo):
@@ -286,7 +287,7 @@ def tile_centredequilibriumpropupdate_w4_kernel(
         dg = {}
 
         def new_dif(i, lo, hi, tag):
-            dif[i, lo] = keep.tile([P, T, hi - lo], F32, name="dif%d_%d" % (i, lo), tag=tag, align_bytes=64)
+            dif[i, lo] = keep.tile([P, T, hi - lo], F32, name="dif%d_%d" % (i, lo), tag=tag, align_bytes=LINE)
 
         def diff(i, lo, m0, m1, engine=nc.vector):
             both = hid[i, lo][:].rearrange("p s t n -> p s (t n)")
@@ -298,7 +299,7 @@ def tile_centredequilibriumpropupdate_w4_kernel(
             )
 
         def d_scale(i, base, lo, hi):
-            dg[i, lo] = work.tile([P, hi - lo, T], BF16, name="dg", bufs=3, align_bytes=64)
+            dg[i, lo] = work.tile([P, hi - lo, T], BF16, name="dg", bufs=3, align_bytes=LINE)
             nc.vector.tensor_tensor(
                 out=dg[i, lo][:].rearrange("p (n j) t -> p n t j", j=4),
                 in0=dif[i, base][:, :, lo - base : hi - base].rearrange("p t (n j) -> p n t j", j=4),
@@ -325,7 +326,7 @@ def tile_centredequilibriumpropupdate_w4_kernel(
             )
 
         def put_out(acc, copy, f0, nf, lo, hi):
-            res = work.tile([P, W], F32, name="res", bufs=8, align_bytes=64)
+            res = work.tile([P, W], F32, name="res", bufs=8, align_bytes=LINE)
             copy(out=res[:], in_=acc[:])
             nc.sync.dma_start(
                 out=out[f0 * P : (f0 + nf) * P, lo:hi].rearrange("(j p) n -> p j n", p=P),

@@ -61,7 +61,8 @@ def tile_centredequilibriumpropupdate_w4_kernel(
         w2t = keep.tile([P, 2 * H], U8, name="w2t", align_bytes=LINE)
         wsc = keep.tile([P, 3, H], U8, name="wsc", align_bytes=LINE)
         rb = keep.tile([P, G, T], BF16, name="rb", align_bytes=64)
-        r1 = keep.tile([P, 1], F32, name="r1", align_bytes=64)
+        r32 = keep.tile([P, G * T], F32, name="r32", align_bytes=64)
+        half = keep.tile([P, 1], F32, name="half", align_bytes=64)
         gb = keep.tile([P, G, T], BF16, name="gb", align_bytes=64)
         gs = keep.tile([P, G, T], F32, name="gs", align_bytes=64)
         ident = keep.tile([P, P], F32, name="ident", align_bytes=LINE)
@@ -88,14 +89,15 @@ def tile_centredequilibriumpropupdate_w4_kernel(
             nc.sync.dma_start(out=w1t[c][:], in_=w1v[:, :, 2 * W * c : 2 * W * (c + 1)])
 
         nc.vector.memset(wsc[:].rearrange("p k n -> p (k n)").bitcast(I32), 0)
+        nc.vector.memset(half[:], 0.5)
         make_identity(nc, ident[:])
 
         load_x(*X_LOADS[0])
+        nc.sync.dma_start(out=rb[:], in_=r.rearrange("(g p t) -> p g t", g=G, p=P, t=T))
         load_e(*E_LOADS[0])
         nc.sync.dma_start(out=pt[:], in_=p.rearrange("(k q t) -> q k t", k=2, q=P, t=T))
         load_x(*X_LOADS[1])
         load_e(*E_LOADS[1])
-        nc.sync.dma_start(out=rb[:], in_=r.rearrange("(g p t) -> p g t", g=G, p=P, t=T))
         load_x(*X_LOADS[2])
         nc.sync.dma_start(out=est[:], in_=e_scale.rearrange("o (q t) -> q (o t)", t=T))
         load_x(*X_LOADS[3])
@@ -128,6 +130,16 @@ def tile_centredequilibriumpropupdate_w4_kernel(
                 out=ew[b0][:].rearrange("p j o -> p (j o)"), in_=epair[b0].bitcast(E4M3), func=COPY, scale=0.5
             )
 
+        def e_widen_sorted(b0):
+            ew[b0] = work.tile([P, 2, O], BF16, name="ew", bufs=4, align_bytes=LINE)
+            nc.vector.tensor_scalar(
+                out=ew[b0][:].rearrange("p u (m e) -> p m u e", e=2),
+                in0=epair[b0].bitcast(E4M3).rearrange("p (m u e) -> p m u e", u=2, e=2),
+                scalar1=half[:],
+                scalar2=None,
+                op0=MULT,
+            )
+
         def x_turn(b, i):
             xbank[b] = bank(i)
             words = xrow[b].bitcast(F32)
@@ -149,6 +161,12 @@ def tile_centredequilibriumpropupdate_w4_kernel(
             xbank[b] = bank(i)
             for lo in range(0, W, P):
                 nc.tensor.transpose(xbank[b][:, lo : lo + P], xsorted[b][:, lo : lo + P], ident[:])
+
+        def e_turn_sorted(b0, i):
+            ebank[b0] = bank(i)
+            words = ew[b0][:].rearrange("p u m -> p (u m)").bitcast(F32)
+            for lo in range(0, W, P):
+                nc.tensor.transpose(ebank[b0][:, lo : lo + P], words[:, lo : lo + P], ident[:])
 
         def e_turn(b0, i):
             ebank[b0] = bank(i)
@@ -203,6 +221,9 @@ def tile_centredequilibriumpropupdate_w4_kernel(
             nc.vector.tensor_scalar(
                 out=xm[i][:, t, lo:hi], in0=xrow[b][:, lo:hi], scalar1=rb[:, i, t : t + 1], scalar2=None, op0=MULT
             )
+
+        def r_mul_scalar(b):
+            nc.scalar.activation(out=xm[b // T][:, b % T, :], in_=xrow[b], func=COPY, scale=r32[:, b : b + 1])
 
         def weave_gpsimd(lo, hi):
             nc.gpsimd.tensor_scalar(
@@ -346,20 +367,21 @@ def tile_centredequilibriumpropupdate_w4_kernel(
 
 
         x_turn(0, 4)
-        e_widen(0)
+        e_widen_sorted(0)
+        nc.scalar.copy(out=r32[:], in_=rb[:].rearrange("p g t -> p (g t)"))
+        r_mul_scalar(0)
         x_turn(1, 5)
         new_qin(0)
         x_mul(0)
-        r_mul(0)
+        r_mul(1)
         quant(0, 0, 2)
-        e_turn(0, 6)
-        nc.scalar.copy(out=r1[:], in_=rb[:, 0, 1:2])
+        e_turn_sorted(0, 6)
         e_widen(2)
         x_sort(3, 1)
         x_turn(2, 7)
         e_turn(2, 4)
         x_turn_sorted(3, 3)
-        nc.scalar.activation(out=xm[0][:, 1, :], in_=xrow[1], func=COPY, scale=r1[:])
+        r_mul_scalar(2)
         first = [bank(j) for j in range(2)]
         for s in range(2):
             a_passes(first[s][:], 0, 0, W)
@@ -367,7 +389,6 @@ def tile_centredequilibriumpropupdate_w4_kernel(
         e_mul(0)
         quant(0, 2, 4)
         e_neg(0)
-        r_mul(2)
         r_mul(3, 0, XR_MID)
         weave_gpsimd(HALF, XR_MID)
         quant(0, 4, 8)

from contextlib import ExitStack

import concourse.mybir as mybir
from concourse.masks import make_identity

F32 = mybir.dt.float32
BF16 = mybir.dt.bfloat16
U32 = mybir.dt.uint32
I32 = mybir.dt.int32
U8 = mybir.dt.uint8
E4M3 = mybir.dt.float8_e4m3fn
FP8X4 = mybir.dt.float8_e4m3fn_x4
FP4X4 = mybir.dt.float4_e2m1fn_x4
MULT = mybir.AluOpType.mult
ADD = mybir.AluOpType.add
SUB = mybir.AluOpType.subtract
TANH = mybir.ActivationFunctionType.Tanh
COPY = mybir.ActivationFunctionType.Copy

P = 128
N, D, H, O = 1024, 1024, 1024, 512
FLOPS = 2 * N * D * H + 2 * N * O * H + 2 * N * D * H
G = 2
T = 4
W = 512
HALF = W // 2
LAST = H - HALF
X_LOADS = ((0, 1), (1, 1), (2, 1), (3, 1), (4, 2), (6, 2))
E_LOADS = ((0, 2), (2, 2), (4, 4))
XR_MID = (HALF + D) // 2
XR_THIRDS = (0, 352, 704, D)
LATE_PIECE = 640
EARLY_PIECE = 704
AHEAD = 2
WIDE_FIRST = 6
LINE = 256
STAGE_BANKS = 4
ALL_BANKS = 7


def tile_centredequilibriumpropupdate_w4_kernel(
    tc, x, p, w1_words, w1_scales, e_bytes, e_scale, w2_words, w2_scales, r, g, out
):
    nc = tc.nc
    with ExitStack() as ctx:
        keep = ctx.enter_context(tc.tile_pool(name="keep", bufs=1))
        work = ctx.enter_context(tc.tile_pool(name="work", bufs=3))
        psum = ctx.enter_context(tc.psum_pool(name="psum", bufs=1))
        ctx.enter_context(tc.manual_schedule())

        def bank(i):
            return psum.tile([P, W], F32, name="bank%d" % i)

        xt = {b0: keep.tile([P, n, D], BF16, name="xt%d" % b0, align_bytes=LINE) for b0, n in X_LOADS}
        xrow = {b0 + j: xt[b0][:, j, :] for b0, n in X_LOADS for j in range(n)}
        eb = {b0: keep.tile([P, n * O], U8, name="eb%d" % b0, align_bytes=LINE) for b0, n in E_LOADS}
        epair = {b0 + j: eb[b0][:, j * O : (j + 2) * O] for b0, n in E_LOADS for j in range(0, n, 2)}
        est = keep.tile([P, T], F32, name="est", align_bytes=64)
        pt = keep.tile([P, 2, T], BF16, name="pt", align_bytes=64)
        w1t = [keep.tile([P, 2, 2 * W], U8, name="w1t%d" % c, align_bytes=LINE) for c in range(2)]
        w2t = keep.tile([P, 2 * H], U8, name="w2t", align_bytes=LINE)
        wsc = keep.tile([P, 3, H], U8, name="wsc", align_bytes=LINE)
        rb = keep.tile([P, G, T], BF16, name="rb", align_bytes=64)
        r32 = keep.tile([P, G * T], F32, name="r32", align_bytes=64)
        half = keep.tile([P, 1], F32, name="half", align_bytes=64)
        gb = keep.tile([P, G, T], BF16, name="gb", align_bytes=64)
        gs = keep.tile([P, G, T], F32, name="gs", align_bytes=64)
        ident = keep.tile([P, P], F32, name="ident", align_bytes=LINE)
        qc = keep.tile([P, G * T // 2, 8, P], U32, name="qc", align_bytes=LINE)
        qs = keep.tile([P, G * T // 2, 8, P], U8, name="qs", align_bytes=LINE)
        rc = [keep.tile([P, D], U32, name="rc%d" % i, align_bytes=LINE) for i in range(G)]
        rs = [keep.tile([P, D], U8, name="rs%d" % i, align_bytes=LINE) for i in range(G)]
        dc = [keep.tile([P, H], U32, name="dc%d" % i, align_bytes=LINE) for i in range(G)]
        ds = [keep.tile([P, H], U8, name="ds%d" % i, align_bytes=LINE) for i in range(G)]
        xm = [keep.tile([P, T, D], BF16, name="xm%d" % i, tag="xm%d" % i, align_bytes=LINE) for i in range(G)]
        xw = [keep.tile([P, D, T], BF16, name="xw%d" % i, tag="xw%d" % i, align_bytes=LINE) for i in range(G)]

        xv = x.rearrange("(g p t) d -> g p t d", g=G, p=P, t=T)
        ev = e_bytes.rearrange("(g p t) o -> g p (t o)", g=G, p=P, t=T)
        w1v = w1_words.rearrange("g p w -> p g w")

        def load_x(b0, n):
            nc.sync.dma_start(out=xt[b0][:], in_=xv[b0 // T, :, b0 % T : b0 % T + n, :])

        def load_e(b0, n):
            nc.sync.dma_start(out=eb[b0][:], in_=ev[b0 // T, :, b0 % T * O : (b0 % T + n) * O])

        def load_w1(c):
            nc.sync.dma_start(out=w1t[c][:], in_=w1v[:, :, 2 * W * c : 2 * W * (c + 1)])

        nc.vector.memset(wsc[:].rearrange("p k n -> p (k n)").bitcast(I32), 0)
        nc.vector.memset(half[:], 0.5)
        make_identity(nc, ident[:])

        load_x(*X_LOADS[0])
        nc.sync.dma_start(out=rb[:], in_=r.rearrange("(g p t) -> p g t", g=G, p=P, t=T))
        load_e(*E_LOADS[0])
        nc.sync.dma_start(out=pt[:], in_=p.rearrange("(k q t) -> q k t", k=2, q=P, t=T))
        load_x(*X_LOADS[1])
        load_e(*E_LOADS[1])
        load_x(*X_LOADS[2])
        nc.sync.dma_start(out=est[:], in_=e_scale.rearrange("o (q t) -> q (o t)", t=T))
        load_x(*X_LOADS[3])
        for q in range(4):
            nc.sync.dma_start(
                out=wsc[32 * q : 32 * q + 4, 0:2, :].bitcast(I32),
                in_=w1_scales[:, 4 * q : 4 * q + 4, :].rearrange("g q n -> q g n").bitcast(I32),
            )
        load_w1(0)
        load_e(*E_LOADS[2])
        load_x(*X_LOADS[4])
        nc.sync.dma_start(out=w2t[:], in_=w2_words[0])
        for q in range(4):
            nc.sync.dma_start(
                out=wsc[32 * q : 32 * q + 4, 2, :].bitcast(I32), in_=w2_scales[0, 4 * q : 4 * q + 4, :].bitcast(I32)
            )
        load_w1(1)
        nc.sync.dma_start(out=gb[:], in_=g.rearrange("(g p t) -> p g t", g=G, p=P, t=T))
        load_x(*X_LOADS[5])

        ew = {}
        xsorted = {}
        xbank = {}
        ebank = {}
        qin = {}

        def e_widen(b0):
            ew[b0] = work.tile([P, 2, O], BF16, name="ew", bufs=4, align_bytes=LINE)
            nc.scalar.activation(
                out=ew[b0][:].rearrange("p j o -> p (j o)"), in_=epair[b0].bitcast(E4M3), func=COPY, scale=0.5
            )

        def e_widen_sorted(b0):
            ew[b0] = work.tile([P, 2, O], BF16, name="ew", bufs=4, align_bytes=LINE)
            nc.vector.tensor_scalar(
                out=ew[b0][:].rearrange("p u (m e) -> p m u e", e=2),
                in0=epair[b0].bitcast(E4M3).rearrange("p (m u e) -> p m u e", u=2, e=2),
                scalar1=half[:],
                scalar2=None,
                op0=MULT,
            )

        def x_turn(b, i):
            xbank[b] = bank(i)
            words = xrow[b].bitcast(F32)
            for k in range(2):
                for u in range(2):
                    lo = P * (2 * u + k)
                    nc.tensor.transpose(xbank[b][:, lo : lo + P], words[:, 256 * k + u : 256 * (k + 1) : 2], ident[:])

        def x_sort(b0, n):
            tile = work.tile([P, n, W], F32, name="xs", bufs=2, align_bytes=LINE)
            nc.scalar.copy(
                out=tile[:].rearrange("p j (u m) -> p j m u", u=2),
                in_=xt[b0][:].bitcast(F32).rearrange("p j (m u) -> p j m u", u=2),
            )
            for j in range(n):
                xsorted[b0 + j] = tile[:, j, :]

        def x_turn_sorted(b, i):
            xbank[b] = bank(i)
            for lo in range(0, W, P):
                nc.tensor.transpose(xbank[b][:, lo : lo + P], xsorted[b][:, lo : lo + P], ident[:])

        def e_turn_sorted(b0, i):
            ebank[b0] = bank(i)
            words = ew[b0][:].rearrange("p u m -> p (u m)").bitcast(F32)
            for lo in range(0, W, P):
                nc.tensor.transpose(ebank[b0][:, lo : lo + P], words[:, lo : lo + P], ident[:])

        def e_turn(b0, i):
            ebank[b0] = bank(i)
            for j in range(2):
                words = ew[b0][:, j, :].bitcast(F32)
                for u in range(2):
                    lo = P * (2 * u + j)
                    nc.tensor.transpose(ebank[b0][:, lo : lo + P], words[:, u:256:2], ident[:])

        def slot(b, k):
            return 2 * (b % 2) + k if k < 2 else 2 * k + b % 2

        def new_qin(b0):
            qin[b0 // 2] = keep.tile([P, 8, P * T], BF16, name="qin%d" % b0, tag="qin%d" % (b0 // 2 % 2), align_bytes=LINE)

        def x_mul(b):
            lo = slot(b, 0)
            nc.vector.tensor_tensor(
                out=qin[b // 2][:, lo : lo + 2, :].rearrange("p k (n u e) -> p k n u e", u=2, e=2),
                in0=xbank[b][:].bitcast(BF16).rearrange("p (u k n e) -> p k n u e", u=2, k=2, e=2),
                in1=pt[:].rearrange("p k (u e) -> p k u e", u=2).unsqueeze(2).to_broadcast([P, 2, P, 2, 2]),
                op=MULT,
            )

        def e_mul(b0):
            nc.vector.tensor_tensor(
                out=qin[b0 // 2][:, 4:6, :].rearrange("p j (n u e) -> p (j n) u e", u=2, e=2),
                in0=ebank[b0][:].bitcast(BF16).rearrange("p (u m e) -> p m u e", u=2, e=2),
                in1=est[:].rearrange("p (u e) -> p u e", u=2).unsqueeze(1).to_broadcast([P, 2 * P, 2, 2]),
                op=MULT,
            )

        def pair_window(b0):
            e_mul(b0)
            x_mul(b0)
            x_mul(b0 + 1)

        def e_neg(b0):
            nc.vector.tensor_scalar(
                out=qin[b0 // 2][:, 6:8, :], in0=qin[b0 // 2][:, 4:6, :], scalar1=-1.0, scalar2=None, op0=MULT
            )

        def quant(b0, lo, hi):
            nc.vector.quantize_mx(
                out=qc[:, b0 // 2, lo:hi, :].rearrange("p k n -> p (k n)").bitcast(FP8X4),
                scales=qs[:, b0 // 2, lo:hi, :].rearrange("p k n -> p (k n)"),
                in_=qin[b0 // 2][:, lo:hi, :].rearrange("p k m -> p (k m)"),
            )

        def r_mul(b, lo=0, hi=D):
            i, t = divmod(b, T)
            nc.vector.tensor_scalar(
                out=xm[i][:, t, lo:hi], in0=xrow[b][:, lo:hi], scalar1=rb[:, i, t : t + 1], scalar2=None, op0=MULT
            )

        def r_mul_scalar(b):
            nc.scalar.activation(out=xm[b // T][:, b % T, :], in_=xrow[b], func=COPY, scale=r32[:, b : b + 1])

        def weave_gpsimd(lo, hi):
            nc.gpsimd.tensor_scalar(
                out=xw[0][:, lo:hi, :],
                in0=xm[0][:, :, lo:hi].rearrange("p t n -> p n t"),
                scalar1=1.0,
                scalar2=0.0,
                op0=MULT,
                op1=ADD,
            )

        def weave_scalar(i, lo, hi):
            nc.scalar.copy(
                out=xw[i][:, lo:hi, :].rearrange("p (n j) t -> p n t j", j=4),
                in_=xm[i][:, :, lo:hi].rearrange("p t (n j) -> p n t j", j=4),
            )

        def r_quant(i):
            nc.vector.quantize_mx(
                out=rc[i][:].bitcast(FP8X4), scales=rs[i][:], in_=xw[i][:].rearrange("p n t -> p (n t)")
            )

        hid = {}
        turn = [0]

        def next_bank(count):
            turn[0] = (turn[0] + 1) % count
            return bank(turn[0])

        def a_passes(dst, b, lo, hi):
            c = lo // W
            for k in range(2):
                nc.tensor.matmul_mx(
                    out=dst,
                    lhsT=qc[:, b // 2, slot(b, k), :].bitcast(FP8X4),
                    lhsT_scale=qs[:, b // 2, slot(b, k), :],
                    rhs=w1t[c][:, k, 2 * (lo - c * W) : 2 * (hi - c * W)].bitcast(FP4X4),
                    rhs_scale=wsc[:, k, lo:hi],
                    start=(k == 0),
                    stop=False,
                )

        def f_pass(dst, b, s, lo, hi):
            nc.tensor.matmul_mx(
                out=dst,
                lhsT=qc[:, b // 2, slot(b, 2 + s), :].bitcast(FP8X4),
                lhsT_scale=qs[:, b // 2, slot(b, 2 + s), :],
                rhs=w2t[:, 2 * lo : 2 * hi].bitcast(FP4X4),
                rhs_scale=wsc[:, 2, lo:hi],
                start=False,
                stop=True,
            )

        def hid_tile(i, lo, hi):
            if (i, lo) not in hid:
                name = "hid%d_%d" % (i, lo)
                hid[i, lo] = keep.tile([P, 2, T, hi - lo], F32, name=name, tag=name, align_bytes=LINE)
            return hid[i, lo]

        def tanh(src, b, s, lo):
            nc.scalar.activation(out=hid_tile(b // T, lo, lo + W)[:, s, b % T, :], in_=src, func=TANH)

        def unit(b, c, count):
            for s in range(2):
                acc = next_bank(count)
                a_passes(acc[:], b, c * W, (c + 1) * W)
                f_pass(acc[:], b, s, c * W, (c + 1) * W)
                tanh(acc[:], b, s, c * W)

        def narrow_unit(b, lo):
            acc = next_bank(ALL_BANKS)
            for s in range(2):
                a_passes(acc[:, s * HALF : (s + 1) * HALF], b, lo, lo + HALF)
                f_pass(acc[:, s * HALF : (s + 1) * HALF], b, s, lo, lo + HALF)
            nc.scalar.activation(
                out=hid_tile(b // T, lo, lo + HALF)[:, :, b % T, :],
                in_=acc[:].rearrange("p (s n) -> p s n", s=2),
                func=TANH,
            )

        dif = {}
        dg = {}

        def new_dif(i, lo, hi, tag):
            dif[i, lo] = keep.tile([P, T, hi - lo], F32, name="dif%d_%d" % (i, lo), tag=tag, align_bytes=LINE)

        def diff(i, lo, m0, m1, engine=nc.vector):
            both = hid[i, lo][:].rearrange("p s t n -> p s (t n)")
            engine.tensor_tensor(
                out=dif[i, lo][:].rearrange("p t n -> p (t n)")[:, m0:m1],
                in0=both[:, 0, m0:m1],
                in1=both[:, 1, m0:m1],
                op=SUB,
            )

        def d_scale(i, base, lo, hi):
            dg[i, lo] = work.tile([P, hi - lo, T], BF16, name="dg", bufs=3, align_bytes=LINE)
            nc.vector.tensor_tensor(
                out=dg[i, lo][:].rearrange("p (n j) t -> p n t j", j=4),
                in0=dif[i, base][:, :, lo - base : hi - base].rearrange("p t (n j) -> p n t j", j=4),
                in1=gp[:, i * T : (i + 1) * T].unsqueeze(1).unsqueeze(3).to_broadcast([P, (hi - lo) // 4, T, 4]),
                op=MULT,
            )

        def d_quant(i, lo, hi):
            nc.vector.quantize_mx(
                out=dc[i][:, lo:hi].bitcast(FP8X4),
                scales=ds[i][:, lo:hi],
                in_=dg[i, lo][:].rearrange("p n t -> p (n t)"),
            )

        def s2_pass(dst, f, i, lo, hi, start, stop):
            nc.tensor.matmul_mx(
                out=dst,
                lhsT=rc[i][:, f * P : (f + 1) * P].bitcast(FP8X4),
                lhsT_scale=rs[i][:, f * P : (f + 1) * P],
                rhs=dc[i][:, lo:hi].bitcast(FP8X4),
                rhs_scale=ds[i][:, lo:hi],
                start=start,
                stop=stop,
            )

        def put_out(acc, copy, f0, nf, lo, hi):
            res = work.tile([P, W], F32, name="res", bufs=8, align_bytes=LINE)
            copy(out=res[:], in_=acc[:])
            nc.sync.dma_start(
                out=out[f0 * P : (f0 + nf) * P, lo:hi].rearrange("(j p) n -> p j n", p=P),
                in_=res[:].rearrange("p (j n) -> p j n", j=nf),
            )

        def wide_out(f):
            acc = next_bank(ALL_BANKS)
            for i in range(G):
                s2_pass(acc[:], f, i, 0, W, i == 0, i == G - 1)
            put_out(acc, nc.scalar.copy, f, 1, 0, W)

        def pair_passes(acc, f0, i, lo):
            for m in range(2):
                first, last = (i, m) == (0, 0), (i, m) == (G - 1, 1)
                s2_pass(acc[:, m * HALF : (m + 1) * HALF], f0 + m, i, lo, lo + HALF, first, last)


        x_turn(0, 4)
        e_widen_sorted(0)
        nc.scalar.copy(out=r32[:], in_=rb[:].rearrange("p g t -> p (g t)"))
        r_mul_scalar(0)
        x_turn(1, 5)
        new_qin(0)
        x_mul(0)
        r_mul(1)
        quant(0, 0, 2)
        e_turn_sorted(0, 6)
        e_widen(2)
        x_sort(3, 1)
        x_turn(2, 7)
        e_turn(2, 4)
        x_turn_sorted(3, 3)
        r_mul_scalar(2)
        first = [bank(j) for j in range(2)]
        for s in range(2):
            a_passes(first[s][:], 0, 0, W)
        x_mul(1)
        e_mul(0)
        quant(0, 2, 4)
        e_neg(0)
        r_mul(3, 0, XR_MID)
        weave_gpsimd(HALF, XR_MID)
        quant(0, 4, 8)
        e_widen(4)
        e_widen(6)
        first.extend([bank(2), bank(5)])
        for s in range(2):
            a_passes(first[2 + s][:], 1, 0, W)

        new_qin(2)
        pair_window(2)
        x_sort(4, 2)
        weave_scalar(0, 0, HALF)
        e_neg(2)
        r_mul(4)
        r_mul(5)
        r_mul(3, XR_MID, D)
        weave_gpsimd(XR_MID, D)
        quant(2, 0, 8)
        for j in range(4):
            f_pass(first[j][:], j // 2, j % 2, 0, W)
            tanh(first[j][:], j // 2, j % 2, 0)

        e_turn(4, 4)
        x_turn_sorted(4, 6)
        x_turn_sorted(5, 7)
        x_sort(6, 2)
        nc.scalar.activation(
            out=gs[:].rearrange("p g t -> p (g t)"), in_=gb[:].rearrange("p g t -> p (g t)"), func=COPY, scale=1.0 / 32.0
        )
        turn[0] = 2
        new_qin(4)
        pair_window(4)
        e_neg(4)
        r_mul(6)
        r_mul(7)
        quant(4, 0, 8)
        unit(0, 1, STAGE_BANKS)
        unit(2, 0, STAGE_BANKS)

        e_turn(6, 4)
        x_turn_sorted(6, 5)
        x_turn_sorted(7, 6)
        gp = bank(ALL_BANKS)
        nc.tensor.matmul(gp[:, 0 : G * T], lhsT=ident[:], rhs=gs[:].rearrange("p g t -> p (g t)"), start=True, stop=True)
        new_dif(0, 0, W, "qin0")
        diff(0, 0, 0, LATE_PIECE, nc.gpsimd)
        new_qin(6)
        weave_scalar(1, *XR_THIRDS[0:2])
        unit(3, 0, STAGE_BANKS)
        pair_window(6)
        e_neg(6)
        quant(6, 0, 4)
        quant(6, 4, 8)

        diff(0, 0, LATE_PIECE, T * W)
        r_quant(0)
        unit(4, 0, ALL_BANKS)
        unit(5, 0, ALL_BANKS)
        weave_scalar(1, *XR_THIRDS[1:3])
        new_dif(1, 0, W, "hid0_0")
        diff(1, 0, 0, EARLY_PIECE, nc.gpsimd)
        d_scale(0, 0, 0, W)
        diff(1, 0, EARLY_PIECE, 2 * W)
        d_quant(0, 0, W)
        unit(6, 0, ALL_BANKS)
        unit(7, 0, ALL_BANKS)
        weave_scalar(1, *XR_THIRDS[2:4])
        diff(1, 0, 2 * W, T * W)
        unit(1, 1, ALL_BANKS)
        r_quant(1)
        new_dif(0, W, H, "xw1")
        diff(0, W, 0, LATE_PIECE, nc.gpsimd)
        d_scale(1, 0, 0, W)

        unit(2, 1, ALL_BANKS)
        unit(3, 1, ALL_BANKS)
        diff(0, W, LATE_PIECE, T * W)
        d_quant(1, 0, W)
        for b in range(T, 2 * T):
            narrow_unit(b, W)
        new_dif(1, W, LAST, "hid0_%d" % W)
        diff(1, W, 0, EARLY_PIECE, nc.gpsimd)
        d_scale(0, W, W, H)
        diff(1, W, EARLY_PIECE, T * HALF)
        d_quant(0, W, H)
        new_dif(1, LAST, H, "qin1")
        for b in range(T, T + AHEAD):
            narrow_unit(b, LAST)
        for f in range(WIDE_FIRST):
            wide_out(f)
        d_scale(1, W, W, LAST)
        diff(1, LAST, 0, AHEAD * HALF)
        d_quant(1, W, LAST)
        for b in range(T + AHEAD, 2 * T):
            narrow_unit(b, LAST)

        diff(1, LAST, AHEAD * HALF, (T - 1) * HALF)
        halves = (LAST, LAST + P)
        for lo in halves:
            diff(1, LAST, (T - 1) * HALF + lo - LAST, (T - 1) * HALF + lo - LAST + P)
        for lo in halves:
            d_scale(1, LAST, lo, lo + P)
        for lo in halves:
            d_quant(1, lo, lo + P)

        for f in range(WIDE_FIRST, D // P):
            wide_out(f)
        for f0 in range(0, D // P, 2):
            acc = next_bank(ALL_BANKS)
            for i in range(G):
                pair_passes(acc, f0, i, W)
            put_out(acc, nc.scalar.copy, f0, 2, W, LAST)
        for f0 in range(0, D // P, 4):
            accs = []
            for j in range(2):
                accs.append(next_bank(ALL_BANKS))
                pair_passes(accs[j], f0 + 2 * j, 0, LAST)
            for j, copy in enumerate((nc.scalar.copy, nc.vector.tensor_copy)):
                pair_passes(accs[j], f0 + 2 * j, 1, LAST)
                put_out(accs[j], copy, f0 + 2 * j, 2, LAST, H)
